import numpy as np
import ml_dtypes


def mxq(x, axis, fmt="e4m3"):
    dtype, down = {"e4m3": (ml_dtypes.float8_e4m3fn, 7), "e5m2": (ml_dtypes.float8_e5m2, 14)}[fmt]
    v = np.moveaxis(np.asarray(x, np.float32).astype(ml_dtypes.bfloat16).astype(np.float64), axis, -1)
    blocks = v.reshape(v.shape[:-1] + (-1, 32))
    amax = np.abs(blocks).max(-1, keepdims=True)
    byte = np.maximum(np.where(amax > 0, np.frexp(amax)[1] - 1 + 127, 0) - down, 1)
    scale = np.exp2(byte - 127.0)
    codes = (blocks / scale).astype(np.float32).astype(dtype).astype(np.float64)
    return np.moveaxis((codes * scale).reshape(v.shape), -1, axis)


WIDE = False


def mx_kscale(k):
    if not WIDE:
        return np.ones(k)
    levels = np.array([10, -10, 5, -5, 0])
    if k % 512:
        return np.exp2(np.random.permutation(np.resize(levels, k // 32))).repeat(32)
    a = np.empty((k // 512, 16))
    for p in range(k // 512):
        a[p, :8] = np.random.permutation(np.resize(levels, 8))
        for g in range(8):
            far = levels[np.abs(levels - a[p, g]) >= 10]
            a[p, g + 8] = far[np.random.randint(len(far))]
    return np.exp2(a.ravel()).repeat(32)


def f64(x):
    return np.asarray(x).astype(np.float64)


def striped(idx):
    return np.tile(idx.reshape(-1, 16).T, (8, 1)).astype(np.uint16)


def unstriped(offs):
    return offs[:16].T.reshape(-1).astype(np.int64)


E2M1 = np.array([0.0, 0.5, 1.0, 1.5, 2.0, 3.0, 4.0, 6.0, -0.0, -0.5, -1.0, -1.5, -2.0, -3.0, -4.0, -6.0])


def pack_weight(w, fmt):
    k, n = w.shape
    w = f64(np.asarray(w, np.float32).astype(ml_dtypes.bfloat16)).reshape(k // 32, 32, n)
    amax = np.abs(w).max(1)
    if fmt == "e4m3":
        byte = np.frexp(amax)[1] - 1 + 127 - 7
    else:
        mant, ex = np.frexp(amax / 6.0)
        byte = np.where(mant > 0.5, ex, ex - 1) + 127
    byte = np.clip(np.where(amax > 0, byte, 1), 1, 254)
    scaled = (w * np.exp2(127.0 - byte)[:, None, :]).reshape(k, n).astype(np.float32)
    by_word = np.ascontiguousarray(scaled.reshape(k // 512, 128, 4, n).transpose(0, 1, 3, 2))
    if fmt == "e4m3":
        words = by_word.astype(ml_dtypes.float8_e4m3fn).view(np.uint8)
    else:
        c = by_word.astype(ml_dtypes.float4_e2m1fn).view(np.uint8) & 0xF
        words = (c[..., 0::2] | (c[..., 1::2] << 4)).reshape(k // 512, 128, 2 * n)
    return np.ascontiguousarray(words), np.ascontiguousarray(byte.astype(np.uint8).reshape(k // 512, 16, n))


def unpack_weight(words, scales, fmt):
    g, _, n = scales.shape
    words = np.ascontiguousarray(words).reshape(g, 128, n, -1)
    if fmt == "e4m3":
        vals = words.view(ml_dtypes.float8_e4m3fn).astype(np.float64)
    else:
        nib = np.empty((g, 128, n, 4), np.uint8)
        nib[..., 0::2] = words & 0xF
        nib[..., 1::2] = words >> 4
        vals = E2M1[nib]
    vals = vals * np.repeat(np.exp2(scales.astype(np.float64) - 127.0), 8, axis=1)[..., None]
    return vals.transpose(0, 1, 3, 2).reshape(g * 512, n)


K, T, E, C, N = 2560, 640, 2, 256, 512
M = 256


def by_expert(wq, xq):
    return np.concatenate([wq[e].T @ xq[:, e * C:(e + 1) * C] for e in range(E)], axis=1)


def setup_inputs():
    n = np.random.standard_normal
    s = mx_kscale(K)[:, None]
    v = mx_kscale(N)
    w = [pack_weight(m, "e2m1") for m in n((E, K, N)) / np.sqrt(K) / s[None] * v[None, None, :]]
    return {
        "xT": (n((K, T)) * s).astype(np.float32),
        "w_words": np.stack([m[0] for m in w]),
        "w_scales": np.stack([m[1] for m in w]),
        "b": (0.3 * n((N, E)) * v[:, None]).astype(np.float32),
        "wp": (n((N, M)) / np.sqrt(N) / v[:, None]).astype(np.float32),
        "gate": np.tile(np.random.uniform(0.2, 1.0, E * C), (N, 1)).astype(np.float32),
        "offs": striped(np.random.permutation(T)[:E * C]),
    }


def reference(xT, w_words, w_scales, b, wp, gate, offs):
    idx = unstriped(offs)
    w = np.stack([unpack_weight(w_words[e], w_scales[e], "e2m1") for e in range(E)])
    xq = mxq(f64(xT)[:, idx], 0, "e4m3")
    y = by_expert(w, xq)
    y = y + np.repeat(f64(b), C, axis=1)
    c = np.zeros((N, T))
    c[:, idx] = f64(gate) * y
    return mxq(f64(wp), 0, "e4m3").T @ mxq(c, 0, "e4m3")

@@ -1,0 +1,301 @@
+from contextlib import ExitStack
+
+import concourse.mybir as mybir
+from concourse.masks import make_identity
+
+K, T, E, C, N, M = 2560, 640, 2, 256, 512, 256
+P = 128
+PACK = 4
+PASSES = K // (P * PACK)
+S = E * C
+TILES = S // P
+FT = M // P
+LIST = 16
+
+WORD_COLUMNS = 688
+BYTE_COLUMNS = 704
+
+SHARED_ROW = 4
+
+LOADS = (((0, 256), (256, 384)), ((0, 640),), ((0, 640),), ((0, 640),), ((0, 512), (512, 128)))
+CASTS = (
+    (("vector", 0, 256), ("vector", 256, 384)),
+    (("scalar", 256, 256), ("vector", 0, 256), ("vector", 512, 128)),
+    (("scalar", 0, 512), ("vector", 512, 128)),
+    (("scalar", 0, 512), ("scalar", 512, 128)),
+    (("scalar", 0, 256), ("scalar", 256, 256), ("scalar", 512, 128)),
+)
+QUANTISED = (
+    ((0, 256), (256, 256), (512, 128)),
+    ((0, 256), (512, 128), (256, 256)),
+    ((512, 128), (0, 512)),
+    ((0, 512), (512, 128)),
+    ((0, 256), (256, 256), (512, 128)),
+)
+WHOLE_PASSES = (0, 1, 2)
+SPLIT_PASSES = (3, 4)
+ORDER = (1, 2, 3, 0, 4)
+
+FLOPS = 2 * K * N * S + 2 * N * M * T
+BYTES = 4 * (K * T + N * E + N * M + S + M * T) + E * PASSES * (2 * P * N + 16 * N) + 2 * P * S // LIST
+
+F32 = mybir.dt.float32
+BF16 = mybir.dt.bfloat16
+I32 = mybir.dt.int32
+U32 = mybir.dt.uint32
+U16 = mybir.dt.uint16
+U8 = mybir.dt.uint8
+FP8X4 = mybir.dt.float8_e4m3fn_x4
+FP4X4 = mybir.dt.float4_e2m1fn_x4
+COPY = mybir.ActivationFunctionType.Copy
+MULT = mybir.AluOpType.mult
+ADD = mybir.AluOpType.add
+
+
+def tile_moe_nxt_lin_bias_kernel(tc, xT, w_words, w_scales, b, wp, gate, offs, out):
+    nc = tc.nc
+
+    def round_and_interleave(engine, dst, src):
+        dst = dst.rearrange("p (c i) j -> p c j i", i=4)
+        src = src.rearrange("p j (c i) -> p c j i", i=4)
+        if engine == "scalar":
+            nc.scalar.activation(out=dst, in_=src, func=COPY)
+        else:
+            nc.vector.tensor_copy(dst, src)
+
+    with ExitStack() as ctx:
+        keep = ctx.enter_context(tc.tile_pool(name="keep", bufs=1))
+        psum = ctx.enter_context(tc.psum_pool(name="psum", bufs=1))
+
+        early = keep.tile([P, 1], F32, name="early")
+        nc.gpsimd.memset(early[:], 0.0)
+        early_copy = keep.tile([P, 1], F32, name="early_copy")
+        nc.scalar.activation(out=early_copy[:], in_=early[:], func=COPY)
+
+        offsets = keep.tile([P, S // LIST], U16, name="offsets")
+        bias_rows = keep.tile([P, PACK * E], F32, name="bias_rows")
+        gate_column = keep.tile([P, TILES], F32, name="gate_column")
+        w_bytes = keep.tile([P, E * PASSES, N], U8, name="w_bytes", align_bytes=64)
+        w_codes = [keep.tile([P, PASSES, 2 * N], U8, name=f"w_codes_{e}", align_bytes=64) for e in range(E)]
+        wp_raw = keep.tile([P, PACK, M], F32, name="wp_raw")
+        x_raw = {}
+
+        nc.vector.memset(w_bytes[:].rearrange("p g n -> p (g n)").bitcast(I32), 0)
+
+        for a in range(PASSES):
+            rows = xT[P * PACK * a : P * PACK * (a + 1), :].rearrange("(p j) t -> p j t", j=PACK)
+            for t0, n in LOADS[a]:
+                piece = keep.tile([P, PACK, n], F32, name=f"x_raw_{a}_{t0}")
+                nc.sync.dma_start(out=piece[:], in_=rows[:, :, t0 : t0 + n])
+                x_raw[(a, t0)] = piece
+                if (a, t0) == (0, 0):
+                    nc.sync.dma_start(offsets[:], offs)
+            if a == 1:
+                nc.sync.dma_start(out=bias_rows[:], in_=b.rearrange("(p j) e -> p (j e)", j=PACK))
+                diagonal = gate.rearrange("n s -> (n s)")[0 : P * (S + 1)].rearrange("(p r) -> p r", r=S + 1)
+                with nc.allow_non_contiguous_dma(reason="one gate a partition"):
+                    nc.sync.dma_start(out=gate_column[:], in_=diagonal[:, 0:S:P])
+
+        byte_rows = w_scales.rearrange("e a (q r) n -> r q (e a) n", r=4)
+        for r in range(4):
+            nc.sync.dma_start(out=w_bytes[r:P:32, :, :].bitcast(I32), in_=byte_rows[r].bitcast(I32))
+
+        def load_expert(e):
+            nc.sync.dma_start(out=w_codes[e][:].bitcast(I32), in_=w_words[e].rearrange("a p c -> p a c").bitcast(I32))
+
+        load_expert(0)
+        nc.sync.dma_start(out=wp_raw[:], in_=wp.rearrange("(p j) f -> p j f", j=PACK))
+        load_expert(1)
+
+        identity = keep.tile([P, P], F32, name="identity")
+        make_identity(nc, identity[:])
+
+        words = [keep.tile([P, WORD_COLUMNS], I32, name=f"words_{a}", align_bytes=64) for a in range(PASSES)]
+        for a in range(PASSES):
+            nc.vector.memset(words[a][:, T:WORD_COLUMNS], 0)
+        scales = {}
+        for a in range(1, PASSES):
+            scales[a] = keep.tile([P, BYTE_COLUMNS], U8, name=f"scales_{a}", align_bytes=64)
+            nc.gpsimd.memset(scales[a][:, T:BYTE_COLUMNS], 0)
+        scales[0] = scales[1]
+
+        slot_words, slot_scales = {}, {}
+        for a in WHOLE_PASSES:
+            words_tile = keep.tile([P, S], U32, name=f"slot_words_{a}", align_bytes=64)
+            bytes_tile = keep.tile([P, S], U8, name=f"slot_scales_{a}", align_bytes=64)
+            slot_words[(a, "all")], slot_scales[(a, "all")] = words_tile[:], bytes_tile[:]
+            for e in range(E):
+                slot_words[(a, e)] = words_tile[:, e * C : (e + 1) * C]
+                slot_scales[(a, e)] = bytes_tile[:, e * C : (e + 1) * C]
+        for a in SPLIT_PASSES:
+            for e in range(E):
+                words_tile = keep.tile([P, C], U32, name=f"slot_words_{a}_{e}", align_bytes=64)
+                bytes_tile = keep.tile([P, C], U8, name=f"slot_scales_{a}_{e}", align_bytes=64)
+                slot_words[(a, e)], slot_scales[(a, e)] = words_tile[:], bytes_tile[:]
+        nc.gpsimd.memset(slot_scales[(0, "all")].bitcast(I32), 0)
+
+        out_tile = [keep.tile([P, T], F32, name=f"out_tile_{f}") for f in range(FT)]
+        for f in range(FT):
+            nc.gpsimd.memset(out_tile[f][:], 0.0)
+
+        x_rounded = [keep.tile([P, T, PACK], BF16, name=f"x_rounded_{a}", align_bytes=64) for a in range(PASSES)]
+
+        def round_tokens(a):
+            for engine, t0, n in CASTS[a]:
+                start = max(u for u, count in LOADS[a] if u <= t0)
+                round_and_interleave(
+                    engine, x_rounded[a][:, t0 : t0 + n, :], x_raw[(a, start)][:, :, t0 - start : t0 - start + n]
+                )
+
+        def quantise_tokens(a):
+            row = SHARED_ROW if a == 0 else 0
+            for t0, n in QUANTISED[a]:
+                nc.vector.quantize_mx(
+                    out=words[a][:, t0 : t0 + n].bitcast(FP8X4),
+                    scales=scales[a][row:P, t0 : t0 + n],
+                    in_=x_rounded[a][:, t0 : t0 + n, :].rearrange("p t j -> p (t j)"),
+                )
+
+        def slot_list(e):
+            return offsets[:] if e == "all" else offsets[:, e * C // LIST : (e + 1) * C // LIST]
+
+        def gather_words(a, e):
+            nc.vector.tensor_copy(slot_words[(a, e)], words[a][:].bitcast(U32).indirect(slot_list(e)))
+
+        def gather_scales(a, e):
+            nc.vector.tensor_copy(slot_scales[(a, e)], scales[a][:].indirect(slot_list(e)))
+
+        y = [psum.tile([P, N], F32, name=f"y_{s}") for s in range(TILES)]
+
+        def multiply(e):
+            for a in ORDER:
+                for h in range(2):
+                    slots = slice(h * P, (h + 1) * P)
+                    nc.tensor.matmul_mx(
+                        out=y[2 * e + h][:],
+                        lhsT=slot_words[(a, e)][:, slots].bitcast(FP8X4),
+                        lhsT_scale=slot_scales[(a, e)][:, slots],
+                        rhs=w_codes[e][:, a, :].bitcast(FP4X4),
+                        rhs_scale=w_bytes[:, e * PASSES + a, :],
+                        start=(a == ORDER[0]),
+                        stop=(a == ORDER[-1]),
+                    )
+
+        gated_bias = [keep.tile([P, N], F32, name=f"gated_bias_{s}") for s in range(TILES)]
+
+        def spread_bias():
+            for e in range(E):
+                spread = psum.tile([P, PACK, P], F32, name=f"spread_{e}", tag=f"turn_{e}")
+                for j in range(PACK):
+                    column = bias_rows[:, E * j + e : E * j + e + 1]
+                    nc.tensor.transpose(spread[:, j, :], column.to_broadcast([P, P]), identity[:])
+                for s in (2 * e, 2 * e + 1):
+                    nc.scalar.activation(
+                        out=gated_bias[s][:].rearrange("s (q j) -> s q j", j=PACK),
+                        in_=spread[:].rearrange("s j q -> s q j"),
+                        func=COPY,
+                        scale=gate_column[:, s : s + 1],
+                    )
+
+        wp_rounded = keep.tile([P, M, PACK], BF16, name="wp_rounded", align_bytes=64)
+        wp_words = keep.tile([P, M], U32, name="wp_words", align_bytes=64)
+        wp_scales = keep.tile([P, M], U8, name="wp_scales", align_bytes=64)
+
+        def quantise_wp():
+            round_and_interleave("scalar", wp_rounded[:], wp_raw[:])
+            nc.vector.quantize_mx(
+                out=wp_words[:].bitcast(FP8X4), scales=wp_scales[:], in_=wp_rounded[:].rearrange("p f j -> p (f j)")
+            )
+
+        c = [keep.tile([P, N], BF16, name=f"c_{s}", align_bytes=64) for s in range(TILES)]
+        c_turned = [keep.tile([P, P, PACK], BF16, name=f"c_turned_{s}", align_bytes=64) for s in range(TILES)]
+        c_words = keep.tile([P, S], U32, name="c_words", align_bytes=64)
+        c_scales = keep.tile([P, S], U8, name="c_scales", align_bytes=64)
+        z_copy = [keep.tile([P, FT, P], F32, name=f"z_copy_{s}") for s in range(TILES)]
+        turn_bank, z_bank = {}, {}
+
+        def finish_tile(s):
+            nc.vector.scalar_tensor_tensor(
+                out=c[s][:], in0=y[s][:], scalar=gate_column[:, s : s + 1], in1=gated_bias[s][:], op0=MULT, op1=ADD
+            )
+
+        def turn_tile(s):
+            e, h = divmod(s, 2)
+            if h == 0:
+                turn_bank[e] = psum.tile([P, 2, 2, P], F32, name=f"turned_{e}", tag=f"turn_{e}")
+            pairs = c[s][:].bitcast(F32)
+            for u in range(2):
+                nc.tensor.transpose(turn_bank[e][:, h, u, :], pairs[:, u : N // 2 : 2], identity[:])
+            nc.scalar.copy(
+                out=c_turned[s][:].rearrange("p r j -> p (r j)").bitcast(F32).rearrange("p (r u) -> p r u", u=2),
+                in_=turn_bank[e][:, h, :, :].rearrange("p u r -> p r u"),
+            )
+
+        def project_tile(s):
+            e, h = divmod(s, 2)
+            slots = slice(s * P, (s + 1) * P)
+            nc.vector.quantize_mx(
+                out=c_words[:, slots].bitcast(FP8X4),
+                scales=c_scales[:, slots],
+                in_=c_turned[s][:].rearrange("p r j -> p (r j)"),
+            )
+            if h == 0:
+                z_bank[e] = psum.tile([P, 2, FT, P], F32, name=f"z_{e}")
+            for f in range(FT):
+                outputs = slice(f * P, (f + 1) * P)
+                nc.tensor.matmul_mx(
+                    out=z_bank[e][:, h, f, :],
+                    lhsT=wp_words[:, outputs].bitcast(FP8X4),
+                    lhsT_scale=wp_scales[:, outputs],
+                    rhs=c_words[:, slots].bitcast(FP8X4),
+                    rhs_scale=c_scales[:, slots],
+                    start=True,
+                    stop=True,
+                )
+            nc.scalar.activation(out=z_copy[s][:], in_=z_bank[e][:, h, :, :], func=COPY)
+
+        def scatter_tile(s):
+            places = offsets[:, s * P // LIST : (s + 1) * P // LIST]
+            for f in range(FT):
+                nc.vector.tensor_copy(out_tile[f][:].indirect(places), z_copy[s][:, f, :])
+
+        round_tokens(0)
+        quantise_tokens(0)
+        round_tokens(1)
+        gather_words(0, "all")
+        quantise_tokens(1)
+        gather_scales(1, "all")
+        nc.sync.dma_start(
+            out=slot_scales[(0, "all")][0 : P - SHARED_ROW, :].bitcast(I32),
+            in_=slot_scales[(1, "all")][SHARED_ROW:P, :].bitcast(I32),
+        )
+        gather_words(1, "all")
+        round_tokens(2)
+        quantise_tokens(2)
+        round_tokens(3)
+        gather_words(2, "all")
+        gather_scales(2, "all")
+        quantise_tokens(3)
+        round_tokens(4)
+        spread_bias()
+        gather_words(3, 0)
+        gather_scales(3, 0)
+        quantise_tokens(4)
+        gather_words(4, 0)
+        gather_scales(4, 0)
+        for a in SPLIT_PASSES:
+            gather_words(a, 1)
+            gather_scales(a, 1)
+        multiply(0)
+        quantise_wp()
+        multiply(1)
+
+        for s in range(TILES):
+            finish_tile(s)
+            turn_tile(s)
+        for s in range(TILES):
+            project_tile(s)
+        for s in range(TILES):
+            scatter_tile(s)
+        for f in range(FT):
+            nc.sync.dma_start(out=out[f * P : (f + 1) * P, :], in_=out_tile[f][:])

@@ -15,26 +15,26 @@ LIST = 16
 WORD_COLUMNS = 688
 BYTE_COLUMNS = 704
 
-SHARED_ROW = 4
-
-LOADS = (((0, 256), (256, 384)), ((0, 640),), ((0, 640),), ((0, 640),), ((0, 512), (512, 128)))
+LOADS = (((0, 640),), ((0, 640),), ((0, 640),), ((0, 640),), ((0, 384), (384, 256)))
 CASTS = (
-    (("vector", 0, 256), ("vector", 256, 384)),
+    (("vector", 0, 256), ("scalar", 256, 256), ("vector", 512, 128)),
     (("scalar", 256, 256), ("vector", 0, 256), ("vector", 512, 128)),
     (("scalar", 0, 512), ("vector", 512, 128)),
     (("scalar", 0, 512), ("scalar", 512, 128)),
-    (("scalar", 0, 256), ("scalar", 256, 256), ("scalar", 512, 128)),
+    (("scalar", 0, 256), ("scalar", 256, 128), ("scalar", 384, 128), ("vector", 512, 128)),
 )
 QUANTISED = (
-    ((0, 256), (256, 256), (512, 128)),
+    ((0, 256), (512, 128), (256, 256)),
     ((0, 256), (512, 128), (256, 256)),
     ((512, 128), (0, 512)),
     ((0, 512), (512, 128)),
-    ((0, 256), (256, 256), (512, 128)),
+    ((0, 256), (512, 128), (256, 256)),
 )
-WHOLE_PASSES = (0, 1, 2)
-SPLIT_PASSES = (3, 4)
+LAST = PASSES - 1
+SHARED_ROW = 4
 ORDER = (1, 2, 3, 0, 4)
+EARLY = 3
+VECTOR_TILES = (0, 1)
 
 FLOPS = 2 * K * N * S + 2 * N * M * T
 BYTES = 4 * (K * T + N * E + N * M + S + M * T) + E * PASSES * (2 * P * N + 16 * N) + 2 * P * S // LIST
@@ -67,45 +67,55 @@ def tile_moe_nxt_lin_bias_kernel(tc, xT, w_words, w_scales, b, wp, gate, offs, o
         keep = ctx.enter_context(tc.tile_pool(name="keep", bufs=1))
         psum = ctx.enter_context(tc.psum_pool(name="psum", bufs=1))
 
-        early = keep.tile([P, 1], F32, name="early")
-        nc.gpsimd.memset(early[:], 0.0)
-        early_copy = keep.tile([P, 1], F32, name="early_copy")
-        nc.scalar.activation(out=early_copy[:], in_=early[:], func=COPY)
+        out_tile = [keep.tile([P, T], F32, name=f"out_tile_{f}") for f in range(FT)]
+        gate_rows = keep.tile([P, P], F32, name="gate_rows")
+        nc.gpsimd.memset(gate_rows[:], 0.0)
+        nc.gpsimd.memset(out_tile[0][:], 0.0)
+        nc.scalar.activation(out=out_tile[1][:], in_=out_tile[0][:], func=COPY)
 
         offsets = keep.tile([P, S // LIST], U16, name="offsets")
         bias_rows = keep.tile([P, PACK * E], F32, name="bias_rows")
         gate_column = keep.tile([P, TILES], F32, name="gate_column")
         w_bytes = keep.tile([P, E * PASSES, N], U8, name="w_bytes", align_bytes=64)
-        w_codes = [keep.tile([P, PASSES, 2 * N], U8, name=f"w_codes_{e}", align_bytes=64) for e in range(E)]
+        w_codes = {}
         wp_raw = keep.tile([P, PACK, M], F32, name="wp_raw")
         x_raw = {}
 
         nc.vector.memset(w_bytes[:].rearrange("p g n -> p (g n)").bitcast(I32), 0)
 
-        for a in range(PASSES):
+        def load_tokens(a, pieces):
             rows = xT[P * PACK * a : P * PACK * (a + 1), :].rearrange("(p j) t -> p j t", j=PACK)
-            for t0, n in LOADS[a]:
+            for t0, n in pieces:
                 piece = keep.tile([P, PACK, n], F32, name=f"x_raw_{a}_{t0}")
                 nc.sync.dma_start(out=piece[:], in_=rows[:, :, t0 : t0 + n])
                 x_raw[(a, t0)] = piece
-                if (a, t0) == (0, 0):
-                    nc.sync.dma_start(offsets[:], offs)
-            if a == 1:
-                nc.sync.dma_start(out=bias_rows[:], in_=b.rearrange("(p j) e -> p (j e)", j=PACK))
-                diagonal = gate.rearrange("n s -> (n s)")[0 : P * (S + 1)].rearrange("(p r) -> p r", r=S + 1)
-                with nc.allow_non_contiguous_dma(reason="one gate a partition"):
-                    nc.sync.dma_start(out=gate_column[:], in_=diagonal[:, 0:S:P])
 
-        byte_rows = w_scales.rearrange("e a (q r) n -> r q (e a) n", r=4)
-        for r in range(4):
-            nc.sync.dma_start(out=w_bytes[r:P:32, :, :].bitcast(I32), in_=byte_rows[r].bitcast(I32))
+        def load_scales(e):
+            byte_rows = w_scales[e].rearrange("a (q r) n -> r q a n", r=4)
+            for r in range(4):
+                nc.sync.dma_start(
+                    out=w_bytes[r:P:32, e * PASSES : (e + 1) * PASSES, :].bitcast(I32), in_=byte_rows[r].bitcast(I32)
+                )
 
-        def load_expert(e):
-            nc.sync.dma_start(out=w_codes[e][:].bitcast(I32), in_=w_words[e].rearrange("a p c -> p a c").bitcast(I32))
+        def load_codes(e, first, count):
+            piece = keep.tile([P, count, 2 * N], U8, name=f"w_codes_{e}_{first}", align_bytes=64)
+            rows = w_words[e, first : first + count].rearrange("a p c -> p a c")
+            nc.sync.dma_start(out=piece[:].bitcast(I32), in_=rows.bitcast(I32))
+            for a in range(count):
+                w_codes[(e, first + a)] = piece[:, a, :]
 
-        load_expert(0)
+        load_tokens(0, LOADS[0])
+        nc.sync.dma_start(offsets[:], offs)
+        nc.sync.dma_start(out=bias_rows[:], in_=b.rearrange("(p j) e -> p (j e)", j=PACK))
+        nc.sync.dma_start(out=gate_rows[0:TILES, :], in_=gate[0:1, :].rearrange("o (s u) -> (o s) u", u=P))
+        for a in range(1, LAST):
+            load_tokens(a, LOADS[a])
+        load_scales(0)
+        load_codes(0, 0, PASSES)
+        load_tokens(LAST, LOADS[LAST])
+        load_scales(1)
+        load_codes(1, 0, PASSES)
         nc.sync.dma_start(out=wp_raw[:], in_=wp.rearrange("(p j) f -> p j f", j=PACK))
-        load_expert(1)
 
         identity = keep.tile([P, P], F32, name="identity")
         make_identity(nc, identity[:])
@@ -120,23 +130,14 @@ def tile_moe_nxt_lin_bias_kernel(tc, xT, w_words, w_scales, b, wp, gate, offs, o
         scales[0] = scales[1]
 
         slot_words, slot_scales = {}, {}
-        for a in WHOLE_PASSES:
+        for a in range(LAST):
             words_tile = keep.tile([P, S], U32, name=f"slot_words_{a}", align_bytes=64)
             bytes_tile = keep.tile([P, S], U8, name=f"slot_scales_{a}", align_bytes=64)
             slot_words[(a, "all")], slot_scales[(a, "all")] = words_tile[:], bytes_tile[:]
             for e in range(E):
                 slot_words[(a, e)] = words_tile[:, e * C : (e + 1) * C]
                 slot_scales[(a, e)] = bytes_tile[:, e * C : (e + 1) * C]
-        for a in SPLIT_PASSES:
-            for e in range(E):
-                words_tile = keep.tile([P, C], U32, name=f"slot_words_{a}_{e}", align_bytes=64)
-                bytes_tile = keep.tile([P, C], U8, name=f"slot_scales_{a}_{e}", align_bytes=64)
-                slot_words[(a, e)], slot_scales[(a, e)] = words_tile[:], bytes_tile[:]
         nc.gpsimd.memset(slot_scales[(0, "all")].bitcast(I32), 0)
-
-        out_tile = [keep.tile([P, T], F32, name=f"out_tile_{f}") for f in range(FT)]
-        for f in range(FT):
-            nc.gpsimd.memset(out_tile[f][:], 0.0)
 
         x_rounded = [keep.tile([P, T, PACK], BF16, name=f"x_rounded_{a}", align_bytes=64) for a in range(PASSES)]
 
@@ -165,37 +166,70 @@ def tile_moe_nxt_lin_bias_kernel(tc, xT, w_words, w_scales, b, wp, gate, offs, o
         def gather_scales(a, e):
             nc.vector.tensor_copy(slot_scales[(a, e)], scales[a][:].indirect(slot_list(e)))
 
-        y = [psum.tile([P, N], F32, name=f"y_{s}") for s in range(TILES)]
+        def gather_last(first, count, words_tag, bytes_tag):
+            words_tile = keep.tile([P, count * P], U32, name=f"last_words_{first}", tag=words_tag, align_bytes=64)
+            bytes_tile = keep.tile([P, count * P], U8, name=f"last_scales_{first}", tag=bytes_tag, align_bytes=64)
+            places = offsets[:, first * P // LIST : (first + count) * P // LIST]
+            nc.vector.tensor_copy(words_tile[:], words[LAST][:].bitcast(U32).indirect(places))
+            nc.vector.tensor_copy(bytes_tile[:], scales[LAST][:].indirect(places))
+            for h in range(count):
+                last[first + h] = (words_tile[:, h * P : (h + 1) * P], bytes_tile[:, h * P : (h + 1) * P])
 
-        def multiply(e):
-            for a in ORDER:
-                for h in range(2):
-                    slots = slice(h * P, (h + 1) * P)
-                    nc.tensor.matmul_mx(
-                        out=y[2 * e + h][:],
-                        lhsT=slot_words[(a, e)][:, slots].bitcast(FP8X4),
-                        lhsT_scale=slot_scales[(a, e)][:, slots],
-                        rhs=w_codes[e][:, a, :].bitcast(FP4X4),
-                        rhs_scale=w_bytes[:, e * PASSES + a, :],
-                        start=(a == ORDER[0]),
-                        stop=(a == ORDER[-1]),
-                    )
+        last = {}
 
-        gated_bias = [keep.tile([P, N], F32, name=f"gated_bias_{s}") for s in range(TILES)]
+        y = [psum.tile([P, N], F32, name=f"y_{s}", tag=f"y_{s}") for s in range(TILES)]
+
+        def multiply(s, passes):
+            e, h = divmod(s, 2)
+            slots = slice(h * P, (h + 1) * P)
+            for a in passes:
+                codes, planes = last[s] if a == LAST else (slot_words[(a, e)][:, slots], slot_scales[(a, e)][:, slots])
+                nc.tensor.matmul_mx(
+                    out=y[s][:],
+                    lhsT=codes.bitcast(FP8X4),
+                    lhsT_scale=planes,
+                    rhs=w_codes[(e, a)].bitcast(FP4X4),
+                    rhs_scale=w_bytes[:, e * PASSES + a, :],
+                    start=(a == ORDER[0]),
+                    stop=(a == LAST),
+                )
+
+        gated_bias = [keep.tile([P, N], F32, name=f"gated_bias_{s}", tag=f"gated_bias_{s}", align_bytes=64) for s in range(TILES)]
+
+        turn_bank = {}
 
         def spread_bias():
+            gate_turned = psum.tile([P, P], F32, name="gate_turned", tag="sum_2")
+            nc.tensor.transpose(gate_turned[:], gate_rows[:], identity[:])
+            nc.scalar.activation(out=gate_column[:], in_=gate_turned[:, 0:TILES], func=COPY)
             for e in range(E):
-                spread = psum.tile([P, PACK, P], F32, name=f"spread_{e}", tag=f"turn_{e}")
+                spread = psum.tile([P, PACK, P], F32, name=f"spread_{e}", tag=f"spread_{e}")
                 for j in range(PACK):
                     column = bias_rows[:, E * j + e : E * j + e + 1]
                     nc.tensor.transpose(spread[:, j, :], column.to_broadcast([P, P]), identity[:])
                 for s in (2 * e, 2 * e + 1):
-                    nc.scalar.activation(
-                        out=gated_bias[s][:].rearrange("s (q j) -> s q j", j=PACK),
-                        in_=spread[:].rearrange("s j q -> s q j"),
-                        func=COPY,
-                        scale=gate_column[:, s : s + 1],
-                    )
+                    if s in VECTOR_TILES:
+                        dst = gated_bias[s][:].rearrange("s (q j) -> s q j", j=PACK)
+                        src = spread[:].rearrange("s j q -> s q j")
+                    else:
+                        dst = gated_bias[s][:].rearrange("s (j q) -> s j q", j=PACK)
+                        src = spread[:]
+                    nc.scalar.activation(out=dst, in_=src, func=COPY, scale=gate_column[:, s : s + 1])
+
+        def turn_and_add(s, src, first):
+            for j in range(PACK):
+                nc.tensor.matmul(
+                    turn_bank[s][:, j, :],
+                    lhsT=src[:, j * P : (j + 1) * P],
+                    rhs=identity[:],
+                    is_transpose=True,
+                    start=(first and j == 0),
+                    stop=(not first and j == PACK - 1),
+                )
+
+        def open_tile(s):
+            turn_bank[s] = psum.tile([P, PACK, P], F32, name=f"sum_{s}", tag=f"sum_{s}")
+            turn_and_add(s, gated_bias[s], True)
 
         wp_rounded = keep.tile([P, M, PACK], BF16, name="wp_rounded", align_bytes=64)
         wp_words = keep.tile([P, M], U32, name="wp_words", align_bytes=64)
@@ -207,12 +241,12 @@ def tile_moe_nxt_lin_bias_kernel(tc, xT, w_words, w_scales, b, wp, gate, offs, o
                 out=wp_words[:].bitcast(FP8X4), scales=wp_scales[:], in_=wp_rounded[:].rearrange("p f j -> p (f j)")
             )
 
-        c = [keep.tile([P, N], BF16, name=f"c_{s}", align_bytes=64) for s in range(TILES)]
-        c_turned = [keep.tile([P, P, PACK], BF16, name=f"c_turned_{s}", align_bytes=64) for s in range(TILES)]
+        c = {s: keep.tile([P, N], BF16, name=f"c_{s}", align_bytes=64) for s in VECTOR_TILES}
+        gated_y = {s: keep.tile([P, N], F32, name=f"gated_y_{s}", tag=f"gated_y_{s}") for s in range(TILES) if s not in VECTOR_TILES}
+        c_turned = [keep.tile([P, P, PACK], BF16, name=f"c_turned_{s}", tag=f"c_turned_{s}", align_bytes=64) for s in range(TILES)]
         c_words = keep.tile([P, S], U32, name="c_words", align_bytes=64)
         c_scales = keep.tile([P, S], U8, name="c_scales", align_bytes=64)
-        z_copy = [keep.tile([P, FT, P], F32, name=f"z_copy_{s}") for s in range(TILES)]
-        turn_bank, z_bank = {}, {}
+        z_bank, z_copy = {}, {}
 
         def finish_tile(s):
             nc.vector.scalar_tensor_tensor(
@@ -220,31 +254,37 @@ def tile_moe_nxt_lin_bias_kernel(tc, xT, w_words, w_scales, b, wp, gate, offs, o
             )
 
         def turn_tile(s):
-            e, h = divmod(s, 2)
-            if h == 0:
-                turn_bank[e] = psum.tile([P, 2, 2, P], F32, name=f"turned_{e}", tag=f"turn_{e}")
+            bank = psum.tile([P, 2, P], F32, name=f"turned_{s}", tag=f"spread_{s % 2}")
             pairs = c[s][:].bitcast(F32)
             for u in range(2):
-                nc.tensor.transpose(turn_bank[e][:, h, u, :], pairs[:, u : N // 2 : 2], identity[:])
+                nc.tensor.transpose(bank[:, u, :], pairs[:, u : N // 2 : 2], identity[:])
             nc.scalar.copy(
                 out=c_turned[s][:].rearrange("p r j -> p (r j)").bitcast(F32).rearrange("p (r u) -> p r u", u=2),
-                in_=turn_bank[e][:, h, :, :].rearrange("p u r -> p r u"),
+                in_=bank[:].rearrange("p u r -> p r u"),
             )
 
+        def finish_and_turn_tile(s):
+            nc.scalar.activation(
+                out=gated_y[s][:].rearrange("s (j q) -> s j q", j=PACK),
+                in_=y[s][:].rearrange("s (q j) -> s j q", j=PACK),
+                func=COPY,
+                scale=gate_column[:, s : s + 1],
+            )
+            turn_and_add(s, gated_y[s], False)
+            nc.scalar.activation(out=c_turned[s][:], in_=turn_bank[s][:].rearrange("p j r -> p r j"), func=COPY)
+
         def project_tile(s):
-            e, h = divmod(s, 2)
             slots = slice(s * P, (s + 1) * P)
             nc.vector.quantize_mx(
                 out=c_words[:, slots].bitcast(FP8X4),
                 scales=c_scales[:, slots],
                 in_=c_turned[s][:].rearrange("p r j -> p (r j)"),
             )
-            if h == 0:
-                z_bank[e] = psum.tile([P, 2, FT, P], F32, name=f"z_{e}")
+            z = psum.tile([P, FT, P], F32, name=f"z_{s}", tag=f"y_{s}")
             for f in range(FT):
                 outputs = slice(f * P, (f + 1) * P)
                 nc.tensor.matmul_mx(
-                    out=z_bank[e][:, h, f, :],
+                    out=z[:, f, :],
                     lhsT=wp_words[:, outputs].bitcast(FP8X4),
                     lhsT_scale=wp_scales[:, outputs],
                     rhs=c_words[:, slots].bitcast(FP8X4),
@@ -252,50 +292,67 @@ def tile_moe_nxt_lin_bias_kernel(tc, xT, w_words, w_scales, b, wp, gate, offs, o
                     start=True,
                     stop=True,
                 )
-            nc.scalar.activation(out=z_copy[s][:], in_=z_bank[e][:, h, :, :], func=COPY)
+            z_bank[s] = z
 
-        def scatter_tile(s):
+        def copy_result(s, first, count, tag):
+            piece = keep.tile([P, count, P], F32, name=f"z_copy_{s}_{first}", tag=tag)
+            nc.scalar.activation(out=piece[:], in_=z_bank[s][:, first : first + count, :], func=COPY)
+            for f in range(count):
+                z_copy[(s, first + f)] = piece[:, f, :]
+
+        def scatter(s, f):
             places = offsets[:, s * P // LIST : (s + 1) * P // LIST]
-            for f in range(FT):
-                nc.vector.tensor_copy(out_tile[f][:].indirect(places), z_copy[s][:, f, :])
+            nc.vector.tensor_copy(out_tile[f][:].indirect(places), z_copy[(s, f)])
 
         round_tokens(0)
-        quantise_tokens(0)
-        round_tokens(1)
-        gather_words(0, "all")
-        quantise_tokens(1)
-        gather_scales(1, "all")
-        nc.sync.dma_start(
-            out=slot_scales[(0, "all")][0 : P - SHARED_ROW, :].bitcast(I32),
-            in_=slot_scales[(1, "all")][SHARED_ROW:P, :].bitcast(I32),
-        )
-        gather_words(1, "all")
-        round_tokens(2)
-        quantise_tokens(2)
-        round_tokens(3)
-        gather_words(2, "all")
-        gather_scales(2, "all")
-        quantise_tokens(3)
-        round_tokens(4)
-        spread_bias()
-        gather_words(3, 0)
-        gather_scales(3, 0)
-        quantise_tokens(4)
-        gather_words(4, 0)
-        gather_scales(4, 0)
-        for a in SPLIT_PASSES:
-            gather_words(a, 1)
-            gather_scales(a, 1)
-        multiply(0)
+        for a in range(LAST):
+            quantise_tokens(a)
+            round_tokens(a + 1)
+            if a == 0:
+                spread_bias()
+                for s in range(TILES):
+                    if s not in VECTOR_TILES:
+                        open_tile(s)
+            gather_words(a, "all")
+            if a > 0:
+                gather_scales(a, "all")
+            if a == 1:
+                nc.gpsimd.dma_start(
+                    out=slot_scales[(0, "all")][0 : P - SHARED_ROW, :].bitcast(I32),
+                    in_=slot_scales[(1, "all")][SHARED_ROW:P, :].bitcast(I32),
+                )
+        quantise_tokens(LAST)
+        for a in ORDER[:-1]:
+            for s in (0, 1):
+                multiply(s, (a,))
+        for s in (0, 1):
+            gather_last(s, 1, f"last_words_{s}", f"last_scales_{s}")
+            multiply(s, (LAST,))
         quantise_wp()
-        multiply(1)
-
-        for s in range(TILES):
+        for s in (0, 1):
             finish_tile(s)
             turn_tile(s)
-        for s in range(TILES):
-            project_tile(s)
-        for s in range(TILES):
-            scatter_tile(s)
+        project_tile(0)
+        copy_result(0, 0, 2, "z_copy_0")
+        gather_last(2, 2, "gated_bias_0", "c_turned_0")
+        project_tile(1)
+        copy_result(1, 0, 1, "z_copy_1")
+        for s in (2, 3):
+            multiply(s, ORDER)
+        scatter(0, 0)
+        scatter(0, 1)
+        finish_and_turn_tile(2)
+        project_tile(2)
+        copy_result(1, 1, 1, "gated_y_2")
+        copy_result(2, 0, 1, "z_copy_2")
+        scatter(1, 0)
+        scatter(1, 1)
+        finish_and_turn_tile(3)
+        project_tile(3)
+        copy_result(2, 1, 1, "gated_y_3")
+        copy_result(3, 0, 2, "z_copy_3")
+        for s in (2, 3):
+            scatter(s, 0)
+            scatter(s, 1)
         for f in range(FT):
             nc.sync.dma_start(out=out[f * P : (f + 1) * P, :], in_=out_tile[f][:])

@@ -15,26 +15,27 @@ LIST = 16
 WORD_COLUMNS = 688
 BYTE_COLUMNS = 704
 
-LOADS = (((0, 640),), ((0, 640),), ((0, 640),), ((0, 640),), ((0, 384), (384, 256)))
+LOADS = (((0, 640),), ((0, 640),), ((0, 640),), ((0, 640),), ((0, 640),))
 CASTS = (
     (("vector", 0, 256), ("scalar", 256, 256), ("vector", 512, 128)),
     (("scalar", 256, 256), ("vector", 0, 256), ("vector", 512, 128)),
-    (("scalar", 0, 512), ("vector", 512, 128)),
-    (("scalar", 0, 512), ("scalar", 512, 128)),
-    (("scalar", 0, 256), ("scalar", 256, 128), ("scalar", 384, 128), ("vector", 512, 128)),
+    (("scalar", 256, 256), ("vector", 0, 256), ("scalar", 512, 128)),
+    (("scalar", 0, 256), ("scalar", 256, 256), ("scalar", 512, 128)),
+    (("scalar", 0, 256), ("scalar", 256, 256), ("scalar", 512, 128)),
 )
 QUANTISED = (
     ((0, 256), (512, 128), (256, 256)),
     ((0, 256), (512, 128), (256, 256)),
-    ((512, 128), (0, 512)),
+    ((0, 256), (256, 256), (512, 128)),
     ((0, 512), (512, 128)),
-    ((0, 256), (512, 128), (256, 256)),
+    ((0, 512), (512, 128)),
 )
 LAST = PASSES - 1
-SHARED_ROW = 4
-ORDER = (1, 2, 3, 0, 4)
+SHARED_ROW = (4, 8, 0, 0, 0)
+SHARED = 2
+ORDER = (2, 3, 0, 1, 4)
 EARLY = 3
-VECTOR_TILES = (0, 1)
+VECTOR_TILES = (0,)
 
 FLOPS = 2 * K * N * S + 2 * N * M * T
 BYTES = 4 * (K * T + N * E + N * M + S + M * T) + E * PASSES * (2 * P * N + 16 * N) + 2 * P * S // LIST
@@ -78,7 +79,6 @@ def tile_moe_nxt_lin_bias_kernel(tc, xT, w_words, w_scales, b, wp, gate, offs, o
         gate_column = keep.tile([P, TILES], F32, name="gate_column")
         w_bytes = keep.tile([P, E * PASSES, N], U8, name="w_bytes", align_bytes=64)
         w_codes = {}
-        wp_raw = keep.tile([P, PACK, M], F32, name="wp_raw")
         x_raw = {}
 
         nc.vector.memset(w_bytes[:].rearrange("p g n -> p (g n)").bitcast(I32), 0)
@@ -86,19 +86,17 @@ def tile_moe_nxt_lin_bias_kernel(tc, xT, w_words, w_scales, b, wp, gate, offs, o
         def load_tokens(a, pieces):
             rows = xT[P * PACK * a : P * PACK * (a + 1), :].rearrange("(p j) t -> p j t", j=PACK)
             for t0, n in pieces:
-                piece = keep.tile([P, PACK, n], F32, name=f"x_raw_{a}_{t0}")
+                piece = keep.tile([P, PACK, n], F32, name=f"x_raw_{a}_{t0}", tag=f"x_raw_{a}", align_bytes=64)
                 nc.sync.dma_start(out=piece[:], in_=rows[:, :, t0 : t0 + n])
                 x_raw[(a, t0)] = piece
 
-        def load_scales(e):
-            byte_rows = w_scales[e].rearrange("a (q r) n -> r q a n", r=4)
+        def load_scales():
+            byte_rows = w_scales.rearrange("e a (q r) n -> r q (e a) n", r=4)
             for r in range(4):
-                nc.sync.dma_start(
-                    out=w_bytes[r:P:32, e * PASSES : (e + 1) * PASSES, :].bitcast(I32), in_=byte_rows[r].bitcast(I32)
-                )
+                nc.sync.dma_start(out=w_bytes[r:P:32, :, :].bitcast(I32), in_=byte_rows[r].bitcast(I32))
 
-        def load_codes(e, first, count):
-            piece = keep.tile([P, count, 2 * N], U8, name=f"w_codes_{e}_{first}", align_bytes=64)
+        def load_codes(e, first, count, tag):
+            piece = keep.tile([P, count, 2 * N], U8, name=f"w_codes_{e}_{first}", tag=tag, align_bytes=64)
             rows = w_words[e, first : first + count].rearrange("a p c -> p a c")
             nc.sync.dma_start(out=piece[:].bitcast(I32), in_=rows.bitcast(I32))
             for a in range(count):
@@ -108,26 +106,24 @@ def tile_moe_nxt_lin_bias_kernel(tc, xT, w_words, w_scales, b, wp, gate, offs, o
         nc.sync.dma_start(offsets[:], offs)
         nc.sync.dma_start(out=bias_rows[:], in_=b.rearrange("(p j) e -> p (j e)", j=PACK))
         nc.sync.dma_start(out=gate_rows[0:TILES, :], in_=gate[0:1, :].rearrange("o (s u) -> (o s) u", u=P))
-        for a in range(1, LAST):
+        for a in range(1, PASSES):
             load_tokens(a, LOADS[a])
-        load_scales(0)
-        load_codes(0, 0, PASSES)
-        load_tokens(LAST, LOADS[LAST])
-        load_scales(1)
-        load_codes(1, 0, PASSES)
-        nc.sync.dma_start(out=wp_raw[:], in_=wp.rearrange("(p j) f -> p j f", j=PACK))
+        load_scales()
+        load_codes(0, 2, 3, "w_codes_late")
+        load_codes(0, 0, 2, "w_codes_early")
 
         identity = keep.tile([P, P], F32, name="identity")
         make_identity(nc, identity[:])
 
-        words = [keep.tile([P, WORD_COLUMNS], I32, name=f"words_{a}", align_bytes=64) for a in range(PASSES)]
+        words = [keep.tile([P, WORD_COLUMNS], I32, name=f"words_{a}", tag=f"words_{a}", align_bytes=64) for a in range(PASSES)]
         for a in range(PASSES):
             nc.vector.memset(words[a][:, T:WORD_COLUMNS], 0)
         scales = {}
-        for a in range(1, PASSES):
-            scales[a] = keep.tile([P, BYTE_COLUMNS], U8, name=f"scales_{a}", align_bytes=64)
+        for a in range(SHARED, PASSES):
+            scales[a] = keep.tile([P, BYTE_COLUMNS], U8, name=f"scales_{a}", tag=f"scales_{a}", align_bytes=64)
             nc.gpsimd.memset(scales[a][:, T:BYTE_COLUMNS], 0)
-        scales[0] = scales[1]
+        for a in range(SHARED):
+            scales[a] = scales[SHARED]
 
         slot_words, slot_scales = {}, {}
         for a in range(LAST):
@@ -137,7 +133,8 @@ def tile_moe_nxt_lin_bias_kernel(tc, xT, w_words, w_scales, b, wp, gate, offs, o
             for e in range(E):
                 slot_words[(a, e)] = words_tile[:, e * C : (e + 1) * C]
                 slot_scales[(a, e)] = bytes_tile[:, e * C : (e + 1) * C]
-        nc.gpsimd.memset(slot_scales[(0, "all")].bitcast(I32), 0)
+        for a in range(SHARED):
+            nc.gpsimd.memset(slot_scales[(a, "all")].bitcast(I32), 0)
 
         x_rounded = [keep.tile([P, T, PACK], BF16, name=f"x_rounded_{a}", align_bytes=64) for a in range(PASSES)]
 
@@ -149,7 +146,7 @@ def tile_moe_nxt_lin_bias_kernel(tc, xT, w_words, w_scales, b, wp, gate, offs, o
                 )
 
         def quantise_tokens(a):
-            row = SHARED_ROW if a == 0 else 0
+            row = SHARED_ROW[a]
             for t0, n in QUANTISED[a]:
                 nc.vector.quantize_mx(
                     out=words[a][:, t0 : t0 + n].bitcast(FP8X4),
@@ -177,12 +174,14 @@ def tile_moe_nxt_lin_bias_kernel(tc, xT, w_words, w_scales, b, wp, gate, offs, o
 
         last = {}
 
-        y = [psum.tile([P, N], F32, name=f"y_{s}", tag=f"y_{s}") for s in range(TILES)]
+        y = {}
 
         def multiply(s, passes):
             e, h = divmod(s, 2)
             slots = slice(h * P, (h + 1) * P)
             for a in passes:
+                if a == ORDER[0]:
+                    y[s] = psum.tile([P, N], F32, name=f"y_{s}", tag=f"y_{s}")
                 codes, planes = last[s] if a == LAST else (slot_words[(a, e)][:, slots], slot_scales[(a, e)][:, slots])
                 nc.tensor.matmul_mx(
                     out=y[s][:],
@@ -199,11 +198,11 @@ def tile_moe_nxt_lin_bias_kernel(tc, xT, w_words, w_scales, b, wp, gate, offs, o
         turn_bank = {}
 
         def spread_bias():
-            gate_turned = psum.tile([P, P], F32, name="gate_turned", tag="sum_2")
+            gate_turned = psum.tile([P, P], F32, name="gate_turned", tag="y_2")
             nc.tensor.transpose(gate_turned[:], gate_rows[:], identity[:])
             nc.scalar.activation(out=gate_column[:], in_=gate_turned[:, 0:TILES], func=COPY)
             for e in range(E):
-                spread = psum.tile([P, PACK, P], F32, name=f"spread_{e}", tag=f"spread_{e}")
+                spread = psum.tile([P, PACK, P], F32, name=f"spread_{e}", tag=("turned", "y_3")[e])
                 for j in range(PACK):
                     column = bias_rows[:, E * j + e : E * j + e + 1]
                     nc.tensor.transpose(spread[:, j, :], column.to_broadcast([P, P]), identity[:])
@@ -235,7 +234,7 @@ def tile_moe_nxt_lin_bias_kernel(tc, xT, w_words, w_scales, b, wp, gate, offs, o
         wp_words = keep.tile([P, M], U32, name="wp_words", align_bytes=64)
         wp_scales = keep.tile([P, M], U8, name="wp_scales", align_bytes=64)
 
-        def quantise_wp():
+        def quantise_wp(wp_raw):
             round_and_interleave("scalar", wp_rounded[:], wp_raw[:])
             nc.vector.quantize_mx(
                 out=wp_words[:].bitcast(FP8X4), scales=wp_scales[:], in_=wp_rounded[:].rearrange("p f j -> p (f j)")
@@ -243,7 +242,7 @@ def tile_moe_nxt_lin_bias_kernel(tc, xT, w_words, w_scales, b, wp, gate, offs, o
 
         c = {s: keep.tile([P, N], BF16, name=f"c_{s}", align_bytes=64) for s in VECTOR_TILES}
         gated_y = {s: keep.tile([P, N], F32, name=f"gated_y_{s}", tag=f"gated_y_{s}") for s in range(TILES) if s not in VECTOR_TILES}
-        c_turned = [keep.tile([P, P, PACK], BF16, name=f"c_turned_{s}", tag=f"c_turned_{s}", align_bytes=64) for s in range(TILES)]
+        c_turned = {}
         c_words = keep.tile([P, S], U32, name="c_words", align_bytes=64)
         c_scales = keep.tile([P, S], U8, name="c_scales", align_bytes=64)
         z_bank, z_copy = {}, {}
@@ -254,7 +253,8 @@ def tile_moe_nxt_lin_bias_kernel(tc, xT, w_words, w_scales, b, wp, gate, offs, o
             )
 
         def turn_tile(s):
-            bank = psum.tile([P, 2, P], F32, name=f"turned_{s}", tag=f"spread_{s % 2}")
+            c_turned[s] = keep.tile([P, P, PACK], BF16, name=f"c_turned_{s}", tag="words_2", align_bytes=64)
+            bank = psum.tile([P, 2, P], F32, name=f"turned_{s}", tag="turned")
             pairs = c[s][:].bitcast(F32)
             for u in range(2):
                 nc.tensor.transpose(bank[:, u, :], pairs[:, u : N // 2 : 2], identity[:])
@@ -271,6 +271,7 @@ def tile_moe_nxt_lin_bias_kernel(tc, xT, w_words, w_scales, b, wp, gate, offs, o
                 scale=gate_column[:, s : s + 1],
             )
             turn_and_add(s, gated_y[s], False)
+            c_turned[s] = keep.tile([P, P, PACK], BF16, name=f"c_turned_{s}", align_bytes=64)
             nc.scalar.activation(out=c_turned[s][:], in_=turn_bank[s][:].rearrange("p j r -> p r j"), func=COPY)
 
         def project_tile(s):
@@ -313,32 +314,40 @@ def tile_moe_nxt_lin_bias_kernel(tc, xT, w_words, w_scales, b, wp, gate, offs, o
                 for s in range(TILES):
                     if s not in VECTOR_TILES:
                         open_tile(s)
-            gather_words(a, "all")
-            if a > 0:
+            if a >= SHARED:
                 gather_scales(a, "all")
-            if a == 1:
-                nc.gpsimd.dma_start(
-                    out=slot_scales[(0, "all")][0 : P - SHARED_ROW, :].bitcast(I32),
-                    in_=slot_scales[(1, "all")][SHARED_ROW:P, :].bitcast(I32),
-                )
+            if a == SHARED:
+                for u, queue in ((0, nc.sync), (1, nc.sync)):
+                    queue.dma_start(
+                        out=slot_scales[(u, "all")][0 : P - SHARED_ROW[u], :].bitcast(I32),
+                        in_=slot_scales[(SHARED, "all")][SHARED_ROW[u] : P, :].bitcast(I32),
+                    )
+            gather_words(a, "all")
+        load_codes(1, 2, 2, "scales_2")
+        wp_raw = keep.tile([P, PACK, M], F32, name="wp_raw", tag="words_2", align_bytes=64)
+        nc.sync.dma_start(out=wp_raw[:], in_=wp.rearrange("(p j) f -> p j f", j=PACK))
+        load_codes(1, 0, 2, "x_raw_3")
+        load_codes(1, 4, 1, "x_raw_4")
         quantise_tokens(LAST)
         for a in ORDER[:-1]:
             for s in (0, 1):
                 multiply(s, (a,))
+        for s in (2, 3):
+            multiply(s, ORDER[:2])
         for s in (0, 1):
             gather_last(s, 1, f"last_words_{s}", f"last_scales_{s}")
             multiply(s, (LAST,))
-        quantise_wp()
-        for s in (0, 1):
-            finish_tile(s)
-            turn_tile(s)
+        quantise_wp(wp_raw)
+        finish_tile(0)
+        turn_tile(0)
+        finish_and_turn_tile(1)
         project_tile(0)
         copy_result(0, 0, 2, "z_copy_0")
-        gather_last(2, 2, "gated_bias_0", "c_turned_0")
+        gather_last(2, 2, "gated_bias_0", "words_2")
         project_tile(1)
         copy_result(1, 0, 1, "z_copy_1")
         for s in (2, 3):
-            multiply(s, ORDER)
+            multiply(s, ORDER[2:])
         scatter(0, 0)
         scatter(0, 1)
         finish_and_turn_tile(2)

@@ -31,11 +31,11 @@ QUANTISED = (
     ((0, 512), (512, 128)),
 )
 LAST = PASSES - 1
-SHARED_ROW = (4, 8, 0, 0, 0)
+SHARED_ROW = (0, 4, 8, 0, 0)
 SHARED = 2
-ORDER = (2, 3, 0, 1, 4)
+ORDER = (0, 1, 2, 3, 4)
 EARLY = 3
-VECTOR_TILES = (0,)
+VECTOR_TILES = (0, 1)
 
 FLOPS = 2 * K * N * S + 2 * N * M * T
 BYTES = 4 * (K * T + N * E + N * M + S + M * T) + E * PASSES * (2 * P * N + 16 * N) + 2 * P * S // LIST
@@ -109,8 +109,9 @@ def tile_moe_nxt_lin_bias_kernel(tc, xT, w_words, w_scales, b, wp, gate, offs, o
         for a in range(1, PASSES):
             load_tokens(a, LOADS[a])
         load_scales()
-        load_codes(0, 2, 3, "w_codes_late")
-        load_codes(0, 0, 2, "w_codes_early")
+        load_codes(0, 0, 3, "w_codes_early")
+        load_codes(1, 0, 1, "w_codes_first")
+        load_codes(0, 3, 2, "w_codes_late")
 
         identity = keep.tile([P, P], F32, name="identity")
         make_identity(nc, identity[:])
@@ -133,7 +134,7 @@ def tile_moe_nxt_lin_bias_kernel(tc, xT, w_words, w_scales, b, wp, gate, offs, o
             for e in range(E):
                 slot_words[(a, e)] = words_tile[:, e * C : (e + 1) * C]
                 slot_scales[(a, e)] = bytes_tile[:, e * C : (e + 1) * C]
-        for a in range(SHARED):
+        for a in range(1, SHARED + 1):
             nc.gpsimd.memset(slot_scales[(a, "all")].bitcast(I32), 0)
 
         x_rounded = [keep.tile([P, T, PACK], BF16, name=f"x_rounded_{a}", align_bytes=64) for a in range(PASSES)]
@@ -202,7 +203,7 @@ def tile_moe_nxt_lin_bias_kernel(tc, xT, w_words, w_scales, b, wp, gate, offs, o
             nc.tensor.transpose(gate_turned[:], gate_rows[:], identity[:])
             nc.scalar.activation(out=gate_column[:], in_=gate_turned[:, 0:TILES], func=COPY)
             for e in range(E):
-                spread = psum.tile([P, PACK, P], F32, name=f"spread_{e}", tag=("turned", "y_3")[e])
+                spread = psum.tile([P, PACK, P], F32, name=f"spread_{e}", tag=f"turned_{e}")
                 for j in range(PACK):
                     column = bias_rows[:, E * j + e : E * j + e + 1]
                     nc.tensor.transpose(spread[:, j, :], column.to_broadcast([P, P]), identity[:])
@@ -253,8 +254,8 @@ def tile_moe_nxt_lin_bias_kernel(tc, xT, w_words, w_scales, b, wp, gate, offs, o
             )
 
         def turn_tile(s):
-            c_turned[s] = keep.tile([P, P, PACK], BF16, name=f"c_turned_{s}", tag="words_2", align_bytes=64)
-            bank = psum.tile([P, 2, P], F32, name=f"turned_{s}", tag="turned")
+            c_turned[s] = keep.tile([P, P, PACK], BF16, name=f"c_turned_{s}", tag=("words_2", "c_turned_1")[s], align_bytes=64)
+            bank = psum.tile([P, 2, P], F32, name=f"turned_{s}", tag=f"turned_{s}")
             pairs = c[s][:].bitcast(F32)
             for u in range(2):
                 nc.tensor.transpose(bank[:, u, :], pairs[:, u : N // 2 : 2], identity[:])
@@ -314,40 +315,41 @@ def tile_moe_nxt_lin_bias_kernel(tc, xT, w_words, w_scales, b, wp, gate, offs, o
                 for s in range(TILES):
                     if s not in VECTOR_TILES:
                         open_tile(s)
-            if a >= SHARED:
+            if a > SHARED:
                 gather_scales(a, "all")
             if a == SHARED:
-                for u, queue in ((0, nc.sync), (1, nc.sync)):
-                    queue.dma_start(
+                gather_scales(0, "all")
+                for u in range(1, SHARED + 1):
+                    nc.sync.dma_start(
                         out=slot_scales[(u, "all")][0 : P - SHARED_ROW[u], :].bitcast(I32),
-                        in_=slot_scales[(SHARED, "all")][SHARED_ROW[u] : P, :].bitcast(I32),
+                        in_=slot_scales[(0, "all")][SHARED_ROW[u] : P, :].bitcast(I32),
                     )
             gather_words(a, "all")
-        load_codes(1, 2, 2, "scales_2")
+        load_codes(1, 1, 2, "scales_2")
         wp_raw = keep.tile([P, PACK, M], F32, name="wp_raw", tag="words_2", align_bytes=64)
         nc.sync.dma_start(out=wp_raw[:], in_=wp.rearrange("(p j) f -> p j f", j=PACK))
-        load_codes(1, 0, 2, "x_raw_3")
-        load_codes(1, 4, 1, "x_raw_4")
+        load_codes(1, 3, 2, "x_raw_3")
         quantise_tokens(LAST)
-        for a in ORDER[:-1]:
+        for s in range(TILES):
+            multiply(s, ORDER[:1])
+        for a in ORDER[1:-1]:
             for s in (0, 1):
                 multiply(s, (a,))
-        for s in (2, 3):
-            multiply(s, ORDER[:2])
         for s in (0, 1):
             gather_last(s, 1, f"last_words_{s}", f"last_scales_{s}")
             multiply(s, (LAST,))
         quantise_wp(wp_raw)
-        finish_tile(0)
-        turn_tile(0)
-        finish_and_turn_tile(1)
+        for s in (0, 1):
+            finish_tile(s)
+            turn_tile(s)
+        gather_last(2, 1, "gated_bias_0", "slot_last_2")
+        multiply(2, ORDER[1:])
         project_tile(0)
         copy_result(0, 0, 2, "z_copy_0")
-        gather_last(2, 2, "gated_bias_0", "words_2")
+        gather_last(3, 1, "words_2", "last_scales_0")
         project_tile(1)
         copy_result(1, 0, 1, "z_copy_1")
-        for s in (2, 3):
-            multiply(s, ORDER[2:])
+        multiply(3, ORDER[1:])
         scatter(0, 0)
         scatter(0, 1)
         finish_and_turn_tile(2)

@@ -36,6 +36,7 @@ SHARED = 2
 ORDER = (0, 1, 2, 3, 4)
 EARLY = 3
 VECTOR_TILES = (0, 1)
+GATED_TAG = (None, None, "c_words_0", "gated_y_3")
 
 FLOPS = 2 * K * N * S + 2 * N * M * T
 BYTES = 4 * (K * T + N * E + N * M + S + M * T) + E * PASSES * (2 * P * N + 16 * N) + 2 * P * S // LIST
@@ -242,9 +243,9 @@ def tile_moe_nxt_lin_bias_kernel(tc, xT, w_words, w_scales, b, wp, gate, offs, o
             )
 
         c = {s: keep.tile([P, N], BF16, name=f"c_{s}", align_bytes=64) for s in VECTOR_TILES}
-        gated_y = {s: keep.tile([P, N], F32, name=f"gated_y_{s}", tag=f"gated_y_{s}") for s in range(TILES) if s not in VECTOR_TILES}
+        gated_y = {}
         c_turned = {}
-        c_words = keep.tile([P, S], U32, name="c_words", align_bytes=64)
+        c_words = {}
         c_scales = keep.tile([P, S], U8, name="c_scales", align_bytes=64)
         z_bank, z_copy = {}, {}
 
@@ -265,6 +266,7 @@ def tile_moe_nxt_lin_bias_kernel(tc, xT, w_words, w_scales, b, wp, gate, offs, o
             )
 
         def finish_and_turn_tile(s):
+            gated_y[s] = keep.tile([P, N], F32, name=f"gated_y_{s}", tag=GATED_TAG[s], align_bytes=64)
             nc.scalar.activation(
                 out=gated_y[s][:].rearrange("s (j q) -> s j q", j=PACK),
                 in_=y[s][:].rearrange("s (q j) -> s j q", j=PACK),
@@ -277,8 +279,9 @@ def tile_moe_nxt_lin_bias_kernel(tc, xT, w_words, w_scales, b, wp, gate, offs, o
 
         def project_tile(s):
             slots = slice(s * P, (s + 1) * P)
+            c_words[s] = keep.tile([P, P], U32, name=f"c_words_{s}", tag=f"c_words_{s}", align_bytes=64)
             nc.vector.quantize_mx(
-                out=c_words[:, slots].bitcast(FP8X4),
+                out=c_words[s][:].bitcast(FP8X4),
                 scales=c_scales[:, slots],
                 in_=c_turned[s][:].rearrange("p r j -> p (r j)"),
             )
@@ -289,7 +292,7 @@ def tile_moe_nxt_lin_bias_kernel(tc, xT, w_words, w_scales, b, wp, gate, offs, o
                     out=z[:, f, :],
                     lhsT=wp_words[:, outputs].bitcast(FP8X4),
                     lhsT_scale=wp_scales[:, outputs],
-                    rhs=c_words[:, slots].bitcast(FP8X4),
+                    rhs=c_words[s][:].bitcast(FP8X4),
                     rhs_scale=c_scales[:, slots],
                     start=True,
                     stop=True,
@@ -297,7 +300,7 @@ def tile_moe_nxt_lin_bias_kernel(tc, xT, w_words, w_scales, b, wp, gate, offs, o
             z_bank[s] = z
 
         def copy_result(s, first, count, tag):
-            piece = keep.tile([P, count, P], F32, name=f"z_copy_{s}_{first}", tag=tag)
+            piece = keep.tile([P, count, P], F32, name=f"z_copy_{s}_{first}", tag=tag, align_bytes=64)
             nc.scalar.activation(out=piece[:], in_=z_bank[s][:, first : first + count, :], func=COPY)
             for f in range(count):
                 z_copy[(s, first + f)] = piece[:, f, :]
@@ -325,6 +328,17 @@ def tile_moe_nxt_lin_bias_kernel(tc, xT, w_words, w_scales, b, wp, gate, offs, o
                         in_=slot_scales[(0, "all")][SHARED_ROW[u] : P, :].bitcast(I32),
                     )
             gather_words(a, "all")
+        idle = psum.tile([P, N], F32, name="idle", tag="turned_0")
+        for u in range(4):
+            nc.tensor.matmul_mx(
+                out=idle[:],
+                lhsT=slot_words[(0, "all")][:, 0:P].bitcast(FP8X4),
+                lhsT_scale=slot_scales[(0, "all")][:, 0:P],
+                rhs=slot_words[(0, "all")].bitcast(FP8X4),
+                rhs_scale=slot_scales[(0, "all")],
+                start=True,
+                stop=True,
+            )
         load_codes(1, 1, 2, "scales_2")
         wp_raw = keep.tile([P, PACK, M], F32, name="wp_raw", tag="words_2", align_bytes=64)
         nc.sync.dma_start(out=wp_raw[:], in_=wp.rearrange("(p j) f -> p j f", j=PACK))
@@ -354,13 +368,13 @@ def tile_moe_nxt_lin_bias_kernel(tc, xT, w_words, w_scales, b, wp, gate, offs, o
         scatter(0, 1)
         finish_and_turn_tile(2)
         project_tile(2)
-        copy_result(1, 1, 1, "gated_y_2")
+        copy_result(1, 1, 1, GATED_TAG[2])
         copy_result(2, 0, 1, "z_copy_2")
         scatter(1, 0)
         scatter(1, 1)
         finish_and_turn_tile(3)
         project_tile(3)
-        copy_result(2, 1, 1, "gated_y_3")
+        copy_result(2, 1, 1, GATED_TAG[3])
         copy_result(3, 0, 2, "z_copy_3")
         for s in (2, 3):
             scatter(s, 0)

@@ -15,7 +15,7 @@ LIST = 16
 WORD_COLUMNS = 688
 BYTE_COLUMNS = 704
 
-LOADS = (((0, 640),), ((0, 640),), ((0, 640),), ((0, 640),), ((0, 640),))
+LOADS = (((0, 640),), ((0, 640),), ((0, 640),), ((0, 256), (256, 256), (512, 128)), ((0, 256), (256, 256), (512, 128)))
 CASTS = (
     (("vector", 0, 256), ("scalar", 256, 256), ("vector", 512, 128)),
     (("scalar", 256, 256), ("vector", 0, 256), ("vector", 512, 128)),
@@ -33,9 +33,11 @@ QUANTISED = (
 LAST = PASSES - 1
 SHARED_ROW = (0, 4, 8, 0, 0)
 SHARED = 2
+MOVED_ROWS = 112
 ORDER = (0, 1, 2, 3, 4)
 EARLY = 3
 VECTOR_TILES = (0, 1)
+Y_BANK = ("y_0", "y_1", "y_2", "y_3")
 GATED_TAG = (None, None, "c_words_0", "gated_y_3")
 
 FLOPS = 2 * K * N * S + 2 * N * M * T
@@ -78,26 +80,33 @@ def tile_moe_nxt_lin_bias_kernel(tc, xT, w_words, w_scales, b, wp, gate, offs, o
         offsets = keep.tile([P, S // LIST], U16, name="offsets")
         bias_rows = keep.tile([P, PACK * E], F32, name="bias_rows")
         gate_column = keep.tile([P, TILES], F32, name="gate_column")
-        w_bytes = keep.tile([P, E * PASSES, N], U8, name="w_bytes", align_bytes=64)
+        late = ctx.enter_context(tc.tile_pool(name="late", bufs=1))
+        w_bytes = {0: keep.tile([P, PASSES, N], U8, name="w_bytes_0", align_bytes=64)}
         w_codes = {}
         x_raw = {}
 
-        nc.vector.memset(w_bytes[:].rearrange("p g n -> p (g n)").bitcast(I32), 0)
+        nc.vector.memset(w_bytes[0][:].rearrange("p g n -> p (g n)").bitcast(I32), 0)
 
         def load_tokens(a, pieces):
             rows = xT[P * PACK * a : P * PACK * (a + 1), :].rearrange("(p j) t -> p j t", j=PACK)
             for t0, n in pieces:
-                piece = keep.tile([P, PACK, n], F32, name=f"x_raw_{a}_{t0}", tag=f"x_raw_{a}", align_bytes=64)
+                if (a, t0) == (3, 512):
+                    piece = late.tile([P, PACK, n], F32, name="x_raw_3_512", offset=16384, align_bytes=64)
+                else:
+                    piece = keep.tile([P, PACK, n], F32, name=f"x_raw_{a}_{t0}", tag=f"x_raw_{a}_{t0}", align_bytes=64)
                 nc.sync.dma_start(out=piece[:], in_=rows[:, :, t0 : t0 + n])
                 x_raw[(a, t0)] = piece
 
-        def load_scales():
-            byte_rows = w_scales.rearrange("e a (q r) n -> r q (e a) n", r=4)
+        def load_scales(e):
+            byte_rows = w_scales[e].rearrange("a (q r) n -> r q a n", r=4)
             for r in range(4):
-                nc.sync.dma_start(out=w_bytes[r:P:32, :, :].bitcast(I32), in_=byte_rows[r].bitcast(I32))
+                nc.sync.dma_start(out=w_bytes[e][r:P:32, :, :].bitcast(I32), in_=byte_rows[r].bitcast(I32))
 
-        def load_codes(e, first, count, tag):
-            piece = keep.tile([P, count, 2 * N], U8, name=f"w_codes_{e}_{first}", tag=tag, align_bytes=64)
+        def load_codes(e, first, count, tag, offset=None):
+            if offset is None:
+                piece = keep.tile([P, count, 2 * N], U8, name=f"w_codes_{e}_{first}", tag=tag, align_bytes=64)
+            else:
+                piece = late.tile([P, count, 2 * N], U8, name=f"w_codes_{e}_{first}", offset=offset, align_bytes=64)
             rows = w_words[e, first : first + count].rearrange("a p c -> p a c")
             nc.sync.dma_start(out=piece[:].bitcast(I32), in_=rows.bitcast(I32))
             for a in range(count):
@@ -107,22 +116,26 @@ def tile_moe_nxt_lin_bias_kernel(tc, xT, w_words, w_scales, b, wp, gate, offs, o
         nc.sync.dma_start(offsets[:], offs)
         nc.sync.dma_start(out=bias_rows[:], in_=b.rearrange("(p j) e -> p (j e)", j=PACK))
         nc.sync.dma_start(out=gate_rows[0:TILES, :], in_=gate[0:1, :].rearrange("o (s u) -> (o s) u", u=P))
-        for a in range(1, PASSES):
+        for a in range(1, LAST):
             load_tokens(a, LOADS[a])
-        load_scales()
+        load_scales(0)
         load_codes(0, 0, 3, "w_codes_early")
-        load_codes(1, 0, 1, "w_codes_first")
-        load_codes(0, 3, 2, "w_codes_late")
+        load_tokens(LAST, LOADS[LAST])
 
         identity = keep.tile([P, P], F32, name="identity")
         make_identity(nc, identity[:])
 
-        words = [keep.tile([P, WORD_COLUMNS], I32, name=f"words_{a}", tag=f"words_{a}", align_bytes=64) for a in range(PASSES)]
+        words = [keep.tile([P, WORD_COLUMNS], I32, name=f"words_{a}", tag=f"words_{a}", align_bytes=64) for a in (0, 1)]
+        words.append(late.tile([P, WORD_COLUMNS], I32, name="words_2", offset=8192 + 1024, align_bytes=64))
+        words.extend(keep.tile([P, WORD_COLUMNS], I32, name=f"words_{a}", align_bytes=64) for a in (3, 4))
         for a in range(PASSES):
             nc.vector.memset(words[a][:, T:WORD_COLUMNS], 0)
         scales = {}
         for a in range(SHARED, PASSES):
-            scales[a] = keep.tile([P, BYTE_COLUMNS], U8, name=f"scales_{a}", tag=f"scales_{a}", align_bytes=64)
+            if a == 2:
+                scales[a] = late.tile([P, BYTE_COLUMNS], U8, name="scales_2", offset=2048 - 256, align_bytes=64)
+            else:
+                scales[a] = keep.tile([P, BYTE_COLUMNS], U8, name=f"scales_{a}", tag=f"scales_{a}", align_bytes=64)
             nc.gpsimd.memset(scales[a][:, T:BYTE_COLUMNS], 0)
         for a in range(SHARED):
             scales[a] = scales[SHARED]
@@ -165,8 +178,11 @@ def tile_moe_nxt_lin_bias_kernel(tc, xT, w_words, w_scales, b, wp, gate, offs, o
         def gather_scales(a, e):
             nc.vector.tensor_copy(slot_scales[(a, e)], scales[a][:].indirect(slot_list(e)))
 
-        def gather_last(first, count, words_tag, bytes_tag):
-            words_tile = keep.tile([P, count * P], U32, name=f"last_words_{first}", tag=words_tag, align_bytes=64)
+        def gather_last(first, count, words_tag, bytes_tag, offset=None):
+            if offset is None:
+                words_tile = keep.tile([P, count * P], U32, name=f"last_words_{first}", tag=words_tag, align_bytes=64)
+            else:
+                words_tile = late.tile([P, count * P], U32, name=f"last_words_{first}", offset=offset, align_bytes=64)
             bytes_tile = keep.tile([P, count * P], U8, name=f"last_scales_{first}", tag=bytes_tag, align_bytes=64)
             places = offsets[:, first * P // LIST : (first + count) * P // LIST]
             nc.vector.tensor_copy(words_tile[:], words[LAST][:].bitcast(U32).indirect(places))
@@ -183,14 +199,14 @@ def tile_moe_nxt_lin_bias_kernel(tc, xT, w_words, w_scales, b, wp, gate, offs, o
             slots = slice(h * P, (h + 1) * P)
             for a in passes:
                 if a == ORDER[0]:
-                    y[s] = psum.tile([P, N], F32, name=f"y_{s}", tag=f"y_{s}")
+                    y[s] = psum.tile([P, N], F32, name=f"y_{s}", tag=Y_BANK[s])
                 codes, planes = last[s] if a == LAST else (slot_words[(a, e)][:, slots], slot_scales[(a, e)][:, slots])
                 nc.tensor.matmul_mx(
                     out=y[s][:],
                     lhsT=codes.bitcast(FP8X4),
                     lhsT_scale=planes,
                     rhs=w_codes[(e, a)].bitcast(FP4X4),
-                    rhs_scale=w_bytes[:, e * PASSES + a, :],
+                    rhs_scale=w_bytes[e][:, a, :],
                     start=(a == ORDER[0]),
                     stop=(a == LAST),
                 )
@@ -237,7 +253,6 @@ def tile_moe_nxt_lin_bias_kernel(tc, xT, w_words, w_scales, b, wp, gate, offs, o
         wp_scales = keep.tile([P, M], U8, name="wp_scales", align_bytes=64)
 
         def quantise_wp(wp_raw):
-            round_and_interleave("scalar", wp_rounded[:], wp_raw[:])
             nc.vector.quantize_mx(
                 out=wp_words[:].bitcast(FP8X4), scales=wp_scales[:], in_=wp_rounded[:].rearrange("p f j -> p (f j)")
             )
@@ -255,7 +270,7 @@ def tile_moe_nxt_lin_bias_kernel(tc, xT, w_words, w_scales, b, wp, gate, offs, o
             )
 
         def turn_tile(s):
-            c_turned[s] = keep.tile([P, P, PACK], BF16, name=f"c_turned_{s}", tag=("words_2", "c_turned_1")[s], align_bytes=64)
+            c_turned[s] = late.tile([P, P, PACK], BF16, name=f"c_turned_{s}", offset=12288 + 1024 * s, align_bytes=64)
             bank = psum.tile([P, 2, P], F32, name=f"turned_{s}", tag=f"turned_{s}")
             pairs = c[s][:].bitcast(F32)
             for u in range(2):
@@ -285,7 +300,7 @@ def tile_moe_nxt_lin_bias_kernel(tc, xT, w_words, w_scales, b, wp, gate, offs, o
                 scales=c_scales[:, slots],
                 in_=c_turned[s][:].rearrange("p r j -> p (r j)"),
             )
-            z = psum.tile([P, FT, P], F32, name=f"z_{s}", tag=f"y_{s}")
+            z = psum.tile([P, FT, P], F32, name=f"z_{s}", tag=Y_BANK[s])
             for f in range(FT):
                 outputs = slice(f * P, (f + 1) * P)
                 nc.tensor.matmul_mx(
@@ -324,43 +339,50 @@ def tile_moe_nxt_lin_bias_kernel(tc, xT, w_words, w_scales, b, wp, gate, offs, o
                 gather_scales(0, "all")
                 for u in range(1, SHARED + 1):
                     nc.sync.dma_start(
-                        out=slot_scales[(u, "all")][0 : P - SHARED_ROW[u], :].bitcast(I32),
-                        in_=slot_scales[(0, "all")][SHARED_ROW[u] : P, :].bitcast(I32),
+                        out=slot_scales[(u, "all")][0:MOVED_ROWS, :].bitcast(I32),
+                        in_=slot_scales[(0, "all")][SHARED_ROW[u] : SHARED_ROW[u] + MOVED_ROWS, :].bitcast(I32),
                     )
             gather_words(a, "all")
         idle = psum.tile([P, N], F32, name="idle", tag="turned_0")
         for u in range(4):
             nc.tensor.matmul_mx(
                 out=idle[:],
-                lhsT=slot_words[(0, "all")][:, 0:P].bitcast(FP8X4),
+                lhsT=slot_words[(2, "all")][:, 0:P].bitcast(FP8X4),
                 lhsT_scale=slot_scales[(0, "all")][:, 0:P],
-                rhs=slot_words[(0, "all")].bitcast(FP8X4),
+                rhs=slot_words[(2, "all")].bitcast(FP8X4),
                 rhs_scale=slot_scales[(0, "all")],
                 start=True,
                 stop=True,
             )
-        load_codes(1, 1, 2, "scales_2")
-        wp_raw = keep.tile([P, PACK, M], F32, name="wp_raw", tag="words_2", align_bytes=64)
+        w_bytes[1] = late.tile([P, PASSES, N], U8, name="w_bytes_1", offset=2048, align_bytes=64)
+        load_scales(1)
+        load_codes(1, 0, 1, None, 1024)
+        load_codes(0, 3, 2, None, 8192)
+        wp_raw = late.tile([P, PACK, M], F32, name="wp_raw", offset=8192 + 2048, align_bytes=64)
         nc.sync.dma_start(out=wp_raw[:], in_=wp.rearrange("(p j) f -> p j f", j=PACK))
-        load_codes(1, 3, 2, "x_raw_3")
+        load_codes(1, 1, 2, None, 16384)
+        load_codes(1, 3, 2, "x_raw_4_0")
         quantise_tokens(LAST)
-        for s in range(TILES):
-            multiply(s, ORDER[:1])
-        for a in ORDER[1:-1]:
+        for a in ORDER[:3]:
             for s in (0, 1):
                 multiply(s, (a,))
+        for s in (2, 3):
+            multiply(s, ORDER[:1])
+        for s in (0, 1):
+            multiply(s, ORDER[3:4])
         for s in (0, 1):
             gather_last(s, 1, f"last_words_{s}", f"last_scales_{s}")
             multiply(s, (LAST,))
-        quantise_wp(wp_raw)
+        round_and_interleave("scalar", wp_rounded[:], wp_raw[:])
         for s in (0, 1):
             finish_tile(s)
             turn_tile(s)
+        quantise_wp(wp_raw)
         gather_last(2, 1, "gated_bias_0", "slot_last_2")
-        multiply(2, ORDER[1:])
         project_tile(0)
+        multiply(2, ORDER[1:])
         copy_result(0, 0, 2, "z_copy_0")
-        gather_last(3, 1, "words_2", "last_scales_0")
+        gather_last(3, 1, None, "last_scales_0", 12288)
         project_tile(1)
         copy_result(1, 0, 1, "z_copy_1")
         multiply(3, ORDER[1:])

@@ -15,7 +15,7 @@ LIST = 16
 WORD_COLUMNS = 688
 BYTE_COLUMNS = 704
 
-LOADS = (((0, 640),), ((0, 640),), ((0, 640),), ((0, 256), (256, 256), (512, 128)), ((0, 256), (256, 256), (512, 128)))
+LOADS = (((0, 640),), ((0, 640),), ((0, 640),), ((0, 640),), ((0, 640),))
 CASTS = (
     (("vector", 0, 256), ("scalar", 256, 256), ("vector", 512, 128)),
     (("scalar", 256, 256), ("vector", 0, 256), ("vector", 512, 128)),
@@ -90,8 +90,8 @@ def tile_moe_nxt_lin_bias_kernel(tc, xT, w_words, w_scales, b, wp, gate, offs, o
         def load_tokens(a, pieces):
             rows = xT[P * PACK * a : P * PACK * (a + 1), :].rearrange("(p j) t -> p j t", j=PACK)
             for t0, n in pieces:
-                if (a, t0) == (3, 512):
-                    piece = late.tile([P, PACK, n], F32, name="x_raw_3_512", offset=16384, align_bytes=64)
+                if a == 3:
+                    piece = late.tile([P, PACK, n], F32, name="x_raw_3", offset=16384, align_bytes=64)
                 else:
                     piece = keep.tile([P, PACK, n], F32, name=f"x_raw_{a}_{t0}", tag=f"x_raw_{a}_{t0}", align_bytes=64)
                 nc.sync.dma_start(out=piece[:], in_=rows[:, :, t0 : t0 + n])
@@ -118,9 +118,9 @@ def tile_moe_nxt_lin_bias_kernel(tc, xT, w_words, w_scales, b, wp, gate, offs, o
         nc.sync.dma_start(out=gate_rows[0:TILES, :], in_=gate[0:1, :].rearrange("o (s u) -> (o s) u", u=P))
         for a in range(1, LAST):
             load_tokens(a, LOADS[a])
+        load_tokens(LAST, LOADS[LAST])
         load_scales(0)
         load_codes(0, 0, 3, "w_codes_early")
-        load_tokens(LAST, LOADS[LAST])
 
         identity = keep.tile([P, P], F32, name="identity")
         make_identity(nc, identity[:])
@@ -361,7 +361,7 @@ def tile_moe_nxt_lin_bias_kernel(tc, xT, w_words, w_scales, b, wp, gate, offs, o
         wp_raw = late.tile([P, PACK, M], F32, name="wp_raw", offset=8192 + 2048, align_bytes=64)
         nc.sync.dma_start(out=wp_raw[:], in_=wp.rearrange("(p j) f -> p j f", j=PACK))
         load_codes(1, 1, 2, None, 16384)
-        load_codes(1, 3, 2, "x_raw_4_0")
+        load_codes(1, 3, 2, None, 16384 + 2048)
         quantise_tokens(LAST)
         for a in ORDER[:3]:
             for s in (0, 1):

@@ -15,7 +15,6 @@ LIST = 16
 WORD_COLUMNS = 688
 BYTE_COLUMNS = 704
 
-LOADS = (((0, 640),), ((0, 640),), ((0, 640),), ((0, 640),), ((0, 640),))
 CASTS = (
     (("vector", 0, 256), ("scalar", 256, 256), ("vector", 512, 128)),
     (("scalar", 256, 256), ("vector", 0, 256), ("vector", 512, 128)),
@@ -31,14 +30,20 @@ QUANTISED = (
     ((0, 512), (512, 128)),
 )
 LAST = PASSES - 1
-SHARED_ROW = (0, 4, 8, 0, 0)
 SHARED = 2
+SHARED_ROW = (0, 4, 8, 0, 0)
 MOVED_ROWS = 112
-ORDER = (0, 1, 2, 3, 4)
-EARLY = 3
+WARM_UP = 4
 VECTOR_TILES = (0, 1)
-Y_BANK = ("y_0", "y_1", "y_2", "y_3")
-GATED_TAG = (None, None, "c_words_0", "gated_y_3")
+
+AT_SHARED_SCALES = 1792
+AT_W_BYTES_1 = 2048
+AT_SHARED_WORDS = 9216
+AT_MIDDLE_CODES = 7168
+AT_WP_RAW = 10240
+AT_TURNED = 12288
+HELD = 3
+AT_HELD_RAW = 16384
 
 FLOPS = 2 * K * N * S + 2 * N * M * T
 BYTES = 4 * (K * T + N * E + N * M + S + M * T) + E * PASSES * (2 * P * N + 16 * N) + 2 * P * S // LIST
@@ -80,85 +85,78 @@ def tile_moe_nxt_lin_bias_kernel(tc, xT, w_words, w_scales, b, wp, gate, offs, o
         offsets = keep.tile([P, S // LIST], U16, name="offsets")
         bias_rows = keep.tile([P, PACK * E], F32, name="bias_rows")
         gate_column = keep.tile([P, TILES], F32, name="gate_column")
-        late = ctx.enter_context(tc.tile_pool(name="late", bufs=1))
+        reused = ctx.enter_context(tc.tile_pool(name="reused", bufs=1))
         w_bytes = {0: keep.tile([P, PASSES, N], U8, name="w_bytes_0", align_bytes=64)}
         w_codes = {}
         x_raw = {}
 
         nc.vector.memset(w_bytes[0][:].rearrange("p g n -> p (g n)").bitcast(I32), 0)
 
-        def load_tokens(a, pieces):
+        def load_tokens(a):
             rows = xT[P * PACK * a : P * PACK * (a + 1), :].rearrange("(p j) t -> p j t", j=PACK)
-            for t0, n in pieces:
-                if a == 3:
-                    piece = late.tile([P, PACK, n], F32, name="x_raw_3", offset=16384, align_bytes=64)
-                else:
-                    piece = keep.tile([P, PACK, n], F32, name=f"x_raw_{a}_{t0}", tag=f"x_raw_{a}_{t0}", align_bytes=64)
-                nc.sync.dma_start(out=piece[:], in_=rows[:, :, t0 : t0 + n])
-                x_raw[(a, t0)] = piece
+            if a == HELD:
+                x_raw[a] = reused.tile([P, PACK, T], F32, name=f"x_raw_{a}", offset=AT_HELD_RAW, align_bytes=64)
+            else:
+                x_raw[a] = keep.tile([P, PACK, T], F32, name=f"x_raw_{a}", align_bytes=64)
+            nc.sync.dma_start(out=x_raw[a][:], in_=rows)
 
         def load_scales(e):
             byte_rows = w_scales[e].rearrange("a (q r) n -> r q a n", r=4)
             for r in range(4):
                 nc.sync.dma_start(out=w_bytes[e][r:P:32, :, :].bitcast(I32), in_=byte_rows[r].bitcast(I32))
 
-        def load_codes(e, first, count, tag, offset=None):
+        def load_codes(first, count, offset=None):
             if offset is None:
-                piece = keep.tile([P, count, 2 * N], U8, name=f"w_codes_{e}_{first}", tag=tag, align_bytes=64)
+                piece = keep.tile([P, count, 2 * N], U8, name=f"w_codes_{first}", align_bytes=64)
             else:
-                piece = late.tile([P, count, 2 * N], U8, name=f"w_codes_{e}_{first}", offset=offset, align_bytes=64)
-            rows = w_words[e, first : first + count].rearrange("a p c -> p a c")
+                piece = reused.tile([P, count, 2 * N], U8, name=f"w_codes_{first}", offset=offset, align_bytes=64)
+            rows = w_words.rearrange("e a p c -> p (e a) c")[:, first : first + count, :]
             nc.sync.dma_start(out=piece[:].bitcast(I32), in_=rows.bitcast(I32))
-            for a in range(count):
-                w_codes[(e, first + a)] = piece[:, a, :]
+            for u in range(count):
+                w_codes[divmod(first + u, PASSES)] = piece[:, u, :]
 
-        load_tokens(0, LOADS[0])
+        load_tokens(0)
         nc.sync.dma_start(offsets[:], offs)
         nc.sync.dma_start(out=bias_rows[:], in_=b.rearrange("(p j) e -> p (j e)", j=PACK))
         nc.sync.dma_start(out=gate_rows[0:TILES, :], in_=gate[0:1, :].rearrange("o (s u) -> (o s) u", u=P))
-        for a in range(1, LAST):
-            load_tokens(a, LOADS[a])
-        load_tokens(LAST, LOADS[LAST])
+        for a in range(1, PASSES):
+            load_tokens(a)
         load_scales(0)
-        load_codes(0, 0, 3, "w_codes_early")
+        load_codes(0, SHARED + 1)
 
         identity = keep.tile([P, P], F32, name="identity")
         make_identity(nc, identity[:])
 
-        words = [keep.tile([P, WORD_COLUMNS], I32, name=f"words_{a}", tag=f"words_{a}", align_bytes=64) for a in (0, 1)]
-        words.append(late.tile([P, WORD_COLUMNS], I32, name="words_2", offset=8192 + 1024, align_bytes=64))
-        words.extend(keep.tile([P, WORD_COLUMNS], I32, name=f"words_{a}", align_bytes=64) for a in (3, 4))
+        words = {}
+        for a in range(PASSES):
+            if a == SHARED:
+                words[a] = reused.tile([P, WORD_COLUMNS], I32, name=f"words_{a}", offset=AT_SHARED_WORDS, align_bytes=64)
+            else:
+                words[a] = keep.tile([P, WORD_COLUMNS], I32, name=f"words_{a}", align_bytes=64)
         for a in range(PASSES):
             nc.vector.memset(words[a][:, T:WORD_COLUMNS], 0)
         scales = {}
         for a in range(SHARED, PASSES):
-            if a == 2:
-                scales[a] = late.tile([P, BYTE_COLUMNS], U8, name="scales_2", offset=2048 - 256, align_bytes=64)
+            if a == SHARED:
+                scales[a] = reused.tile([P, BYTE_COLUMNS], U8, name=f"scales_{a}", offset=AT_SHARED_SCALES, align_bytes=64)
             else:
-                scales[a] = keep.tile([P, BYTE_COLUMNS], U8, name=f"scales_{a}", tag=f"scales_{a}", align_bytes=64)
+                scales[a] = keep.tile([P, BYTE_COLUMNS], U8, name=f"scales_{a}", align_bytes=64)
             nc.gpsimd.memset(scales[a][:, T:BYTE_COLUMNS], 0)
         for a in range(SHARED):
             scales[a] = scales[SHARED]
 
         slot_words, slot_scales = {}, {}
         for a in range(LAST):
-            words_tile = keep.tile([P, S], U32, name=f"slot_words_{a}", align_bytes=64)
-            bytes_tile = keep.tile([P, S], U8, name=f"slot_scales_{a}", align_bytes=64)
-            slot_words[(a, "all")], slot_scales[(a, "all")] = words_tile[:], bytes_tile[:]
-            for e in range(E):
-                slot_words[(a, e)] = words_tile[:, e * C : (e + 1) * C]
-                slot_scales[(a, e)] = bytes_tile[:, e * C : (e + 1) * C]
+            slot_words[a] = keep.tile([P, S], U32, name=f"slot_words_{a}", align_bytes=64)
+            slot_scales[a] = keep.tile([P, S], U8, name=f"slot_scales_{a}", align_bytes=64)
         for a in range(1, SHARED + 1):
-            nc.gpsimd.memset(slot_scales[(a, "all")].bitcast(I32), 0)
+            nc.gpsimd.memset(slot_scales[a][:].bitcast(I32), 0)
 
         x_rounded = [keep.tile([P, T, PACK], BF16, name=f"x_rounded_{a}", align_bytes=64) for a in range(PASSES)]
 
         def round_tokens(a):
             for engine, t0, n in CASTS[a]:
-                start = max(u for u, count in LOADS[a] if u <= t0)
-                round_and_interleave(
-                    engine, x_rounded[a][:, t0 : t0 + n, :], x_raw[(a, start)][:, :, t0 - start : t0 - start + n]
-                )
+                round_and_interleave(engine, x_rounded[a][:, t0 : t0 + n, :], x_raw[a][:, :, t0 : t0 + n])
 
         def quantise_tokens(a):
             row = SHARED_ROW[a]
@@ -169,45 +167,39 @@ def tile_moe_nxt_lin_bias_kernel(tc, xT, w_words, w_scales, b, wp, gate, offs, o
                     in_=x_rounded[a][:, t0 : t0 + n, :].rearrange("p t j -> p (t j)"),
                 )
 
-        def slot_list(e):
-            return offsets[:] if e == "all" else offsets[:, e * C // LIST : (e + 1) * C // LIST]
+        def gather_words(a):
+            nc.vector.tensor_copy(slot_words[a][:], words[a][:].bitcast(U32).indirect(offsets[:]))
 
-        def gather_words(a, e):
-            nc.vector.tensor_copy(slot_words[(a, e)], words[a][:].bitcast(U32).indirect(slot_list(e)))
+        def gather_scales(a):
+            nc.vector.tensor_copy(slot_scales[a][:], scales[a][:].indirect(offsets[:]))
 
-        def gather_scales(a, e):
-            nc.vector.tensor_copy(slot_scales[(a, e)], scales[a][:].indirect(slot_list(e)))
-
-        def gather_last(first, count, words_tag, bytes_tag, offset=None):
-            if offset is None:
-                words_tile = keep.tile([P, count * P], U32, name=f"last_words_{first}", tag=words_tag, align_bytes=64)
-            else:
-                words_tile = late.tile([P, count * P], U32, name=f"last_words_{first}", offset=offset, align_bytes=64)
-            bytes_tile = keep.tile([P, count * P], U8, name=f"last_scales_{first}", tag=bytes_tag, align_bytes=64)
-            places = offsets[:, first * P // LIST : (first + count) * P // LIST]
-            nc.vector.tensor_copy(words_tile[:], words[LAST][:].bitcast(U32).indirect(places))
-            nc.vector.tensor_copy(bytes_tile[:], scales[LAST][:].indirect(places))
-            for h in range(count):
-                last[first + h] = (words_tile[:, h * P : (h + 1) * P], bytes_tile[:, h * P : (h + 1) * P])
+        def places(s):
+            return offsets[:, s * P // LIST : (s + 1) * P // LIST]
 
         last = {}
+
+        def gather_last(s, words_tile, bytes_tag):
+            bytes_tile = keep.tile([P, P], U8, name=f"last_scales_{s}", tag=bytes_tag, align_bytes=64)
+            nc.vector.tensor_copy(words_tile[:], words[LAST][:].bitcast(U32).indirect(places(s)))
+            nc.vector.tensor_copy(bytes_tile[:], scales[LAST][:].indirect(places(s)))
+            last[s] = (words_tile[:], bytes_tile[:])
 
         y = {}
 
         def multiply(s, passes):
-            e, h = divmod(s, 2)
-            slots = slice(h * P, (h + 1) * P)
+            e = s // 2
+            slots = slice(s * P, (s + 1) * P)
             for a in passes:
-                if a == ORDER[0]:
-                    y[s] = psum.tile([P, N], F32, name=f"y_{s}", tag=Y_BANK[s])
-                codes, planes = last[s] if a == LAST else (slot_words[(a, e)][:, slots], slot_scales[(a, e)][:, slots])
+                if a == 0:
+                    y[s] = psum.tile([P, N], F32, name=f"y_{s}", tag=f"y_{s}")
+                codes, code_scales = last[s] if a == LAST else (slot_words[a][:, slots], slot_scales[a][:, slots])
                 nc.tensor.matmul_mx(
                     out=y[s][:],
                     lhsT=codes.bitcast(FP8X4),
-                    lhsT_scale=planes,
+                    lhsT_scale=code_scales,
                     rhs=w_codes[(e, a)].bitcast(FP4X4),
                     rhs_scale=w_bytes[e][:, a, :],
-                    start=(a == ORDER[0]),
+                    start=(a == 0),
                     stop=(a == LAST),
                 )
 
@@ -252,11 +244,6 @@ def tile_moe_nxt_lin_bias_kernel(tc, xT, w_words, w_scales, b, wp, gate, offs, o
         wp_words = keep.tile([P, M], U32, name="wp_words", align_bytes=64)
         wp_scales = keep.tile([P, M], U8, name="wp_scales", align_bytes=64)
 
-        def quantise_wp(wp_raw):
-            nc.vector.quantize_mx(
-                out=wp_words[:].bitcast(FP8X4), scales=wp_scales[:], in_=wp_rounded[:].rearrange("p f j -> p (f j)")
-            )
-
         c = {s: keep.tile([P, N], BF16, name=f"c_{s}", align_bytes=64) for s in VECTOR_TILES}
         gated_y = {}
         c_turned = {}
@@ -270,7 +257,8 @@ def tile_moe_nxt_lin_bias_kernel(tc, xT, w_words, w_scales, b, wp, gate, offs, o
             )
 
         def turn_tile(s):
-            c_turned[s] = late.tile([P, P, PACK], BF16, name=f"c_turned_{s}", offset=12288 + 1024 * s, align_bytes=64)
+            offset = AT_TURNED + 2 * P * PACK * s
+            c_turned[s] = reused.tile([P, P, PACK], BF16, name=f"c_turned_{s}", offset=offset, align_bytes=64)
             bank = psum.tile([P, 2, P], F32, name=f"turned_{s}", tag=f"turned_{s}")
             pairs = c[s][:].bitcast(F32)
             for u in range(2):
@@ -280,8 +268,8 @@ def tile_moe_nxt_lin_bias_kernel(tc, xT, w_words, w_scales, b, wp, gate, offs, o
                 in_=bank[:].rearrange("p u r -> p r u"),
             )
 
-        def finish_and_turn_tile(s):
-            gated_y[s] = keep.tile([P, N], F32, name=f"gated_y_{s}", tag=GATED_TAG[s], align_bytes=64)
+        def finish_and_turn_tile(s, tag):
+            gated_y[s] = keep.tile([P, N], F32, name=f"gated_y_{s}", tag=tag, align_bytes=64)
             nc.scalar.activation(
                 out=gated_y[s][:].rearrange("s (j q) -> s j q", j=PACK),
                 in_=y[s][:].rearrange("s (q j) -> s j q", j=PACK),
@@ -300,7 +288,7 @@ def tile_moe_nxt_lin_bias_kernel(tc, xT, w_words, w_scales, b, wp, gate, offs, o
                 scales=c_scales[:, slots],
                 in_=c_turned[s][:].rearrange("p r j -> p (r j)"),
             )
-            z = psum.tile([P, FT, P], F32, name=f"z_{s}", tag=Y_BANK[s])
+            z = psum.tile([P, FT, P], F32, name=f"z_{s}", tag=f"y_{s}")
             for f in range(FT):
                 outputs = slice(f * P, (f + 1) * P)
                 nc.tensor.matmul_mx(
@@ -321,8 +309,7 @@ def tile_moe_nxt_lin_bias_kernel(tc, xT, w_words, w_scales, b, wp, gate, offs, o
                 z_copy[(s, first + f)] = piece[:, f, :]
 
         def scatter(s, f):
-            places = offsets[:, s * P // LIST : (s + 1) * P // LIST]
-            nc.vector.tensor_copy(out_tile[f][:].indirect(places), z_copy[(s, f)])
+            nc.vector.tensor_copy(out_tile[f][:].indirect(places(s)), z_copy[(s, f)])
 
         round_tokens(0)
         for a in range(LAST):
@@ -334,70 +321,70 @@ def tile_moe_nxt_lin_bias_kernel(tc, xT, w_words, w_scales, b, wp, gate, offs, o
                     if s not in VECTOR_TILES:
                         open_tile(s)
             if a > SHARED:
-                gather_scales(a, "all")
+                gather_scales(a)
             if a == SHARED:
-                gather_scales(0, "all")
+                gather_scales(0)
                 for u in range(1, SHARED + 1):
                     nc.sync.dma_start(
-                        out=slot_scales[(u, "all")][0:MOVED_ROWS, :].bitcast(I32),
-                        in_=slot_scales[(0, "all")][SHARED_ROW[u] : SHARED_ROW[u] + MOVED_ROWS, :].bitcast(I32),
+                        out=slot_scales[u][0:MOVED_ROWS, :].bitcast(I32),
+                        in_=slot_scales[0][SHARED_ROW[u] : SHARED_ROW[u] + MOVED_ROWS, :].bitcast(I32),
                     )
-            gather_words(a, "all")
+            gather_words(a)
         idle = psum.tile([P, N], F32, name="idle", tag="turned_0")
-        for u in range(4):
+        for u in range(WARM_UP):
             nc.tensor.matmul_mx(
                 out=idle[:],
-                lhsT=slot_words[(2, "all")][:, 0:P].bitcast(FP8X4),
-                lhsT_scale=slot_scales[(0, "all")][:, 0:P],
-                rhs=slot_words[(2, "all")].bitcast(FP8X4),
-                rhs_scale=slot_scales[(0, "all")],
+                lhsT=slot_words[SHARED][:, 0:P].bitcast(FP8X4),
+                lhsT_scale=slot_scales[0][:, 0:P],
+                rhs=slot_words[SHARED][:].bitcast(FP8X4),
+                rhs_scale=slot_scales[0][:],
                 start=True,
                 stop=True,
             )
-        w_bytes[1] = late.tile([P, PASSES, N], U8, name="w_bytes_1", offset=2048, align_bytes=64)
+        w_bytes[1] = reused.tile([P, PASSES, N], U8, name="w_bytes_1", offset=AT_W_BYTES_1, align_bytes=64)
         load_scales(1)
-        load_codes(1, 0, 1, None, 1024)
-        load_codes(0, 3, 2, None, 8192)
-        wp_raw = late.tile([P, PACK, M], F32, name="wp_raw", offset=8192 + 2048, align_bytes=64)
+        load_codes(SHARED + 1, 3, AT_MIDDLE_CODES)
+        wp_raw = reused.tile([P, PACK, M], F32, name="wp_raw", offset=AT_WP_RAW, align_bytes=64)
         nc.sync.dma_start(out=wp_raw[:], in_=wp.rearrange("(p j) f -> p j f", j=PACK))
-        load_codes(1, 1, 2, None, 16384)
-        load_codes(1, 3, 2, None, 16384 + 2048)
+        for u in range(2):
+            load_codes(PASSES + 1 + 2 * u, 2, AT_HELD_RAW + 2 * 2 * N * u)
+
         quantise_tokens(LAST)
-        for a in ORDER[:3]:
-            for s in (0, 1):
+        for a in range(LAST):
+            for s in VECTOR_TILES:
                 multiply(s, (a,))
-        for s in (2, 3):
-            multiply(s, ORDER[:1])
-        for s in (0, 1):
-            multiply(s, ORDER[3:4])
-        for s in (0, 1):
-            gather_last(s, 1, f"last_words_{s}", f"last_scales_{s}")
+        for s in VECTOR_TILES:
+            gather_last(s, keep.tile([P, P], U32, name=f"last_words_{s}", align_bytes=64), f"last_scales_{s}")
             multiply(s, (LAST,))
+        for s in (2, 3):
+            multiply(s, (0,))
         round_and_interleave("scalar", wp_rounded[:], wp_raw[:])
-        for s in (0, 1):
+        for s in VECTOR_TILES:
             finish_tile(s)
             turn_tile(s)
-        quantise_wp(wp_raw)
-        gather_last(2, 1, "gated_bias_0", "slot_last_2")
+        nc.vector.quantize_mx(
+            out=wp_words[:].bitcast(FP8X4), scales=wp_scales[:], in_=wp_rounded[:].rearrange("p f j -> p (f j)")
+        )
+        gather_last(2, keep.tile([P, P], U32, name="last_words_2", tag="gated_bias_0", align_bytes=64), "last_scales_2")
         project_tile(0)
-        multiply(2, ORDER[1:])
-        copy_result(0, 0, 2, "z_copy_0")
-        gather_last(3, 1, None, "last_scales_0", 12288)
+        multiply(2, range(1, PASSES))
+        copy_result(0, 0, FT, "z_copy_0")
+        gather_last(3, reused.tile([P, P], U32, name="last_words_3", offset=AT_TURNED, align_bytes=64), "last_scales_0")
         project_tile(1)
         copy_result(1, 0, 1, "z_copy_1")
-        multiply(3, ORDER[1:])
+        multiply(3, range(1, PASSES))
         scatter(0, 0)
         scatter(0, 1)
-        finish_and_turn_tile(2)
+        finish_and_turn_tile(2, "c_words_0")
         project_tile(2)
-        copy_result(1, 1, 1, GATED_TAG[2])
+        copy_result(1, 1, 1, "c_words_0")
         copy_result(2, 0, 1, "z_copy_2")
         scatter(1, 0)
         scatter(1, 1)
-        finish_and_turn_tile(3)
+        finish_and_turn_tile(3, "gated_y_3")
         project_tile(3)
-        copy_result(2, 1, 1, GATED_TAG[3])
-        copy_result(3, 0, 2, "z_copy_3")
+        copy_result(2, 1, 1, "gated_y_3")
+        copy_result(3, 0, FT, "z_copy_3")
         for s in (2, 3):
             scatter(s, 0)
             scatter(s, 1)

@@ -11,6 +11,7 @@ S = E * C
 TILES = S // P
 FT = M // P
 LIST = 16
+LAST = PASSES - 1
 
 WORD_COLUMNS = 688
 BYTE_COLUMNS = 704
@@ -29,21 +30,21 @@ QUANTISED = (
     ((0, 512), (512, 128)),
     ((0, 512), (512, 128)),
 )
-LAST = PASSES - 1
 SHARED = 2
 SHARED_ROW = (0, 4, 8, 0, 0)
 MOVED_ROWS = 112
-WARM_UP = 4
-VECTOR_TILES = (0, 1)
-
-AT_SHARED_SCALES = 1792
-AT_W_BYTES_1 = 2048
-AT_SHARED_WORDS = 9216
-AT_MIDDLE_CODES = 7168
-AT_WP_RAW = 10240
-AT_TURNED = 12288
+SCALAR_TILES = (1,)
+SCATTER_ENGINE = ("scalar", "vector")
 HELD = 3
-AT_HELD_RAW = 16384
+
+AT_SHARED_SCALES = 0
+AT_W_BYTES_1 = 640
+AT_MIDDLE_CODES = 3200
+AT_SHARED_WORDS = 6208
+AT_WP_RAW = 8896
+AT_HELD_RAW = 12992
+AT_GATED_BIAS_0 = 23232
+AT_TURNED_0 = AT_GATED_BIAS_0 + 4 * N
 
 FLOPS = 2 * K * N * S + 2 * N * M * T
 BYTES = 4 * (K * T + N * E + N * M + S + M * T) + E * PASSES * (2 * P * N + 16 * N) + 2 * P * S // LIST
@@ -75,6 +76,8 @@ def tile_moe_nxt_lin_bias_kernel(tc, xT, w_words, w_scales, b, wp, gate, offs, o
     with ExitStack() as ctx:
         keep = ctx.enter_context(tc.tile_pool(name="keep", bufs=1))
         psum = ctx.enter_context(tc.psum_pool(name="psum", bufs=1))
+        offsets = keep.tile([P, S // LIST], U16, name="offsets")
+        reused = ctx.enter_context(tc.tile_pool(name="reused", bufs=1))
 
         out_tile = [keep.tile([P, T], F32, name=f"out_tile_{f}") for f in range(FT)]
         gate_rows = keep.tile([P, P], F32, name="gate_rows")
@@ -82,14 +85,11 @@ def tile_moe_nxt_lin_bias_kernel(tc, xT, w_words, w_scales, b, wp, gate, offs, o
         nc.gpsimd.memset(out_tile[0][:], 0.0)
         nc.scalar.activation(out=out_tile[1][:], in_=out_tile[0][:], func=COPY)
 
-        offsets = keep.tile([P, S // LIST], U16, name="offsets")
         bias_rows = keep.tile([P, PACK * E], F32, name="bias_rows")
         gate_column = keep.tile([P, TILES], F32, name="gate_column")
-        reused = ctx.enter_context(tc.tile_pool(name="reused", bufs=1))
         w_bytes = {0: keep.tile([P, PASSES, N], U8, name="w_bytes_0", align_bytes=64)}
         w_codes = {}
         x_raw = {}
-
         nc.vector.memset(w_bytes[0][:].rearrange("p g n -> p (g n)").bitcast(I32), 0)
 
         def load_tokens(a):
@@ -173,16 +173,22 @@ def tile_moe_nxt_lin_bias_kernel(tc, xT, w_words, w_scales, b, wp, gate, offs, o
         def gather_scales(a):
             nc.vector.tensor_copy(slot_scales[a][:], scales[a][:].indirect(offsets[:]))
 
-        def places(s):
-            return offsets[:, s * P // LIST : (s + 1) * P // LIST]
+        def places(s, count=1):
+            return offsets[:, s * P // LIST : (s + count) * P // LIST]
 
         last = {}
 
-        def gather_last(s, words_tile, bytes_tag):
-            bytes_tile = keep.tile([P, P], U8, name=f"last_scales_{s}", tag=bytes_tag, align_bytes=64)
-            nc.vector.tensor_copy(words_tile[:], words[LAST][:].bitcast(U32).indirect(places(s)))
-            nc.vector.tensor_copy(bytes_tile[:], scales[LAST][:].indirect(places(s)))
-            last[s] = (words_tile[:], bytes_tile[:])
+        def gather_last(s, count, offset=None):
+            if offset is None:
+                words_tile = keep.tile([P, count * P], U32, name=f"last_words_{s}", align_bytes=64)
+                bytes_tile = keep.tile([P, count * P], U8, name=f"last_scales_{s}", align_bytes=64)
+            else:
+                words_tile = reused.tile([P, count * P], U32, name=f"last_words_{s}", offset=offset, align_bytes=64)
+                bytes_tile = reused.tile([P, count * P], U8, name=f"last_scales_{s}", offset=offset + 4 * count * P, align_bytes=64)
+            nc.vector.tensor_copy(words_tile[:], words[LAST][:].bitcast(U32).indirect(places(s, count)))
+            nc.vector.tensor_copy(bytes_tile[:], scales[LAST][:].indirect(places(s, count)))
+            for u in range(count):
+                last[s + u] = (words_tile[:, u * P : (u + 1) * P], bytes_tile[:, u * P : (u + 1) * P])
 
         y = {}
 
@@ -203,26 +209,27 @@ def tile_moe_nxt_lin_bias_kernel(tc, xT, w_words, w_scales, b, wp, gate, offs, o
                     stop=(a == LAST),
                 )
 
-        gated_bias = [keep.tile([P, N], F32, name=f"gated_bias_{s}", tag=f"gated_bias_{s}", align_bytes=64) for s in range(TILES)]
-
+        gated_bias = [reused.tile([P, N], F32, name="gated_bias_0", offset=AT_GATED_BIAS_0, align_bytes=64)]
+        for s in range(1, TILES):
+            gated_bias.append(keep.tile([P, N], F32, name=f"gated_bias_{s}", tag=f"gated_bias_{s}", align_bytes=64))
         turn_bank = {}
 
         def spread_bias():
-            gate_turned = psum.tile([P, P], F32, name="gate_turned", tag="y_2")
+            gate_turned = psum.tile([P, P], F32, name="gate_turned", tag="y_3")
             nc.tensor.transpose(gate_turned[:], gate_rows[:], identity[:])
             nc.scalar.activation(out=gate_column[:], in_=gate_turned[:, 0:TILES], func=COPY)
             for e in range(E):
-                spread = psum.tile([P, PACK, P], F32, name=f"spread_{e}", tag=f"turned_{e}")
+                spread = psum.tile([P, PACK, P], F32, name=f"spread_{e}", tag=f"y_{e}")
                 for j in range(PACK):
                     column = bias_rows[:, E * j + e : E * j + e + 1]
                     nc.tensor.transpose(spread[:, j, :], column.to_broadcast([P, P]), identity[:])
                 for s in (2 * e, 2 * e + 1):
-                    if s in VECTOR_TILES:
-                        dst = gated_bias[s][:].rearrange("s (q j) -> s q j", j=PACK)
-                        src = spread[:].rearrange("s j q -> s q j")
-                    else:
+                    if s in SCALAR_TILES:
                         dst = gated_bias[s][:].rearrange("s (j q) -> s j q", j=PACK)
                         src = spread[:]
+                    else:
+                        dst = gated_bias[s][:].rearrange("s (q j) -> s q j", j=PACK)
+                        src = spread[:].rearrange("s j q -> s q j")
                     nc.scalar.activation(out=dst, in_=src, func=COPY, scale=gate_column[:, s : s + 1])
 
         def turn_and_add(s, src, first):
@@ -237,62 +244,66 @@ def tile_moe_nxt_lin_bias_kernel(tc, xT, w_words, w_scales, b, wp, gate, offs, o
                 )
 
         def open_tile(s):
-            turn_bank[s] = psum.tile([P, PACK, P], F32, name=f"sum_{s}", tag=f"sum_{s}")
+            turn_bank[s] = psum.tile([P, PACK, P], F32, name=f"sum_{s}", tag=f"turn_{s}")
             turn_and_add(s, gated_bias[s], True)
 
         wp_rounded = keep.tile([P, M, PACK], BF16, name="wp_rounded", align_bytes=64)
         wp_words = keep.tile([P, M], U32, name="wp_words", align_bytes=64)
         wp_scales = keep.tile([P, M], U8, name="wp_scales", align_bytes=64)
 
-        c = {s: keep.tile([P, N], BF16, name=f"c_{s}", align_bytes=64) for s in VECTOR_TILES}
-        gated_y = {}
-        c_turned = {}
-        c_words = {}
+        c, gated_y, c_turned, c_words, z_bank, z_copy = {}, {}, {}, {}, {}, {}
         c_scales = keep.tile([P, S], U8, name="c_scales", align_bytes=64)
-        z_bank, z_copy = {}, {}
 
-        def finish_tile(s):
-            nc.vector.scalar_tensor_tensor(
-                out=c[s][:], in0=y[s][:], scalar=gate_column[:, s : s + 1], in1=gated_bias[s][:], op0=MULT, op1=ADD
-            )
+        def finish(s):
+            if s in SCALAR_TILES:
+                gated_y[s] = keep.tile([P, N], F32, name=f"gated_y_{s}", align_bytes=64)
+                nc.scalar.activation(
+                    out=gated_y[s][:].rearrange("s (j q) -> s j q", j=PACK),
+                    in_=y[s][:].rearrange("s (q j) -> s j q", j=PACK),
+                    func=COPY,
+                    scale=gate_column[:, s : s + 1],
+                )
+            else:
+                c[s] = keep.tile([P, N], BF16, name=f"c_{s}", tag=f"c_{s}", align_bytes=64)
+                nc.vector.scalar_tensor_tensor(
+                    out=c[s][:], in0=y[s][:], scalar=gate_column[:, s : s + 1], in1=gated_bias[s][:], op0=MULT, op1=ADD
+                )
 
-        def turn_tile(s):
-            offset = AT_TURNED + 2 * P * PACK * s
-            c_turned[s] = reused.tile([P, P, PACK], BF16, name=f"c_turned_{s}", offset=offset, align_bytes=64)
-            bank = psum.tile([P, 2, P], F32, name=f"turned_{s}", tag=f"turned_{s}")
-            pairs = c[s][:].bitcast(F32)
-            for u in range(2):
-                nc.tensor.transpose(bank[:, u, :], pairs[:, u : N // 2 : 2], identity[:])
-            nc.scalar.copy(
-                out=c_turned[s][:].rearrange("p r j -> p (r j)").bitcast(F32).rearrange("p (r u) -> p r u", u=2),
-                in_=bank[:].rearrange("p u r -> p r u"),
-            )
+        def turn(s):
+            if s in SCALAR_TILES:
+                turn_and_add(s, gated_y[s], False)
+            else:
+                turn_bank[s] = psum.tile([P, 2, P], F32, name=f"turned_{s}", tag=f"turn_{s}")
+                pairs = c[s][:].bitcast(F32)
+                for u in range(2):
+                    nc.tensor.transpose(turn_bank[s][:, u, :], pairs[:, u : N // 2 : 2], identity[:])
 
-        def finish_and_turn_tile(s, tag):
-            gated_y[s] = keep.tile([P, N], F32, name=f"gated_y_{s}", tag=tag, align_bytes=64)
-            nc.scalar.activation(
-                out=gated_y[s][:].rearrange("s (j q) -> s j q", j=PACK),
-                in_=y[s][:].rearrange("s (q j) -> s j q", j=PACK),
-                func=COPY,
-                scale=gate_column[:, s : s + 1],
-            )
-            turn_and_add(s, gated_y[s], False)
-            c_turned[s] = keep.tile([P, P, PACK], BF16, name=f"c_turned_{s}", align_bytes=64)
-            nc.scalar.activation(out=c_turned[s][:], in_=turn_bank[s][:].rearrange("p j r -> p r j"), func=COPY)
+        def lay_out(s):
+            if s == 0:
+                c_turned[s] = reused.tile([P, P, PACK], BF16, name=f"c_turned_{s}", offset=AT_TURNED_0, align_bytes=64)
+            else:
+                c_turned[s] = keep.tile([P, P, PACK], BF16, name=f"c_turned_{s}", align_bytes=64)
+            if s in SCALAR_TILES:
+                nc.scalar.activation(out=c_turned[s][:], in_=turn_bank[s][:].rearrange("p j r -> p r j"), func=COPY)
+            else:
+                nc.scalar.copy(
+                    out=c_turned[s][:].rearrange("p r j -> p (r j)").bitcast(F32).rearrange("p (r u) -> p r u", u=2),
+                    in_=turn_bank[s][:].rearrange("p u r -> p r u"),
+                )
 
-        def project_tile(s):
+        def project(s):
             slots = slice(s * P, (s + 1) * P)
-            c_words[s] = keep.tile([P, P], U32, name=f"c_words_{s}", tag=f"c_words_{s}", align_bytes=64)
+            c_words[s] = keep.tile([P, P], U32, name=f"c_words_{s}", align_bytes=64)
             nc.vector.quantize_mx(
                 out=c_words[s][:].bitcast(FP8X4),
                 scales=c_scales[:, slots],
                 in_=c_turned[s][:].rearrange("p r j -> p (r j)"),
             )
-            z = psum.tile([P, FT, P], F32, name=f"z_{s}", tag=f"y_{s}")
+            z_bank[s] = psum.tile([P, FT, P], F32, name=f"z_{s}", tag=f"y_{s}")
             for f in range(FT):
                 outputs = slice(f * P, (f + 1) * P)
                 nc.tensor.matmul_mx(
-                    out=z[:, f, :],
+                    out=z_bank[s][:, f, :],
                     lhsT=wp_words[:, outputs].bitcast(FP8X4),
                     lhsT_scale=wp_scales[:, outputs],
                     rhs=c_words[s][:].bitcast(FP8X4),
@@ -300,7 +311,6 @@ def tile_moe_nxt_lin_bias_kernel(tc, xT, w_words, w_scales, b, wp, gate, offs, o
                     start=True,
                     stop=True,
                 )
-            z_bank[s] = z
 
         def copy_result(s, first, count, tag):
             piece = keep.tile([P, count, P], F32, name=f"z_copy_{s}_{first}", tag=tag, align_bytes=64)
@@ -309,7 +319,11 @@ def tile_moe_nxt_lin_bias_kernel(tc, xT, w_words, w_scales, b, wp, gate, offs, o
                 z_copy[(s, first + f)] = piece[:, f, :]
 
         def scatter(s, f):
-            nc.vector.tensor_copy(out_tile[f][:].indirect(places(s)), z_copy[(s, f)])
+            window = out_tile[f][:].indirect(places(s))
+            if SCATTER_ENGINE[f] == "scalar":
+                nc.scalar.activation(out=window, in_=z_copy[(s, f)], func=COPY)
+            else:
+                nc.vector.tensor_copy(window, z_copy[(s, f)])
 
         round_tokens(0)
         for a in range(LAST):
@@ -317,9 +331,8 @@ def tile_moe_nxt_lin_bias_kernel(tc, xT, w_words, w_scales, b, wp, gate, offs, o
             round_tokens(a + 1)
             if a == 0:
                 spread_bias()
-                for s in range(TILES):
-                    if s not in VECTOR_TILES:
-                        open_tile(s)
+                for s in SCALAR_TILES:
+                    open_tile(s)
             if a > SHARED:
                 gather_scales(a)
             if a == SHARED:
@@ -330,17 +343,6 @@ def tile_moe_nxt_lin_bias_kernel(tc, xT, w_words, w_scales, b, wp, gate, offs, o
                         in_=slot_scales[0][SHARED_ROW[u] : SHARED_ROW[u] + MOVED_ROWS, :].bitcast(I32),
                     )
             gather_words(a)
-        idle = psum.tile([P, N], F32, name="idle", tag="turned_0")
-        for u in range(WARM_UP):
-            nc.tensor.matmul_mx(
-                out=idle[:],
-                lhsT=slot_words[SHARED][:, 0:P].bitcast(FP8X4),
-                lhsT_scale=slot_scales[0][:, 0:P],
-                rhs=slot_words[SHARED][:].bitcast(FP8X4),
-                rhs_scale=slot_scales[0][:],
-                start=True,
-                stop=True,
-            )
         w_bytes[1] = reused.tile([P, PASSES, N], U8, name="w_bytes_1", offset=AT_W_BYTES_1, align_bytes=64)
         load_scales(1)
         load_codes(SHARED + 1, 3, AT_MIDDLE_CODES)
@@ -351,39 +353,49 @@ def tile_moe_nxt_lin_bias_kernel(tc, xT, w_words, w_scales, b, wp, gate, offs, o
 
         quantise_tokens(LAST)
         for a in range(LAST):
-            for s in VECTOR_TILES:
+            for s in (0, 1):
                 multiply(s, (a,))
-        for s in VECTOR_TILES:
-            gather_last(s, keep.tile([P, P], U32, name=f"last_words_{s}", align_bytes=64), f"last_scales_{s}")
-            multiply(s, (LAST,))
         for s in (2, 3):
             multiply(s, (0,))
         round_and_interleave("scalar", wp_rounded[:], wp_raw[:])
-        for s in VECTOR_TILES:
-            finish_tile(s)
-            turn_tile(s)
+        for s in (0, 1):
+            gather_last(s, 1)
+            multiply(s, (LAST,))
+            finish(s)
         nc.vector.quantize_mx(
             out=wp_words[:].bitcast(FP8X4), scales=wp_scales[:], in_=wp_rounded[:].rearrange("p f j -> p (f j)")
         )
-        gather_last(2, keep.tile([P, P], U32, name="last_words_2", tag="gated_bias_0", align_bytes=64), "last_scales_2")
-        project_tile(0)
-        multiply(2, range(1, PASSES))
-        copy_result(0, 0, FT, "z_copy_0")
-        gather_last(3, reused.tile([P, P], U32, name="last_words_3", offset=AT_TURNED, align_bytes=64), "last_scales_0")
-        project_tile(1)
-        copy_result(1, 0, 1, "z_copy_1")
-        multiply(3, range(1, PASSES))
+        multiply(2, (1,))
+        turn(0)
+        lay_out(0)
+        gather_last(2, 1, AT_GATED_BIAS_0)
+        multiply(3, (1,))
+        multiply(2, (2,))
+        turn(1)
+        lay_out(1)
+        multiply(3, (2,))
+        project(0)
+        gather_last(3, 1, AT_TURNED_0)
+        for s in (2, 3):
+            multiply(s, (3,))
+        project(1)
+        for s in (2, 3):
+            multiply(s, (4,))
+            finish(s)
+        copy_result(0, 0, 1, "z_copy_0")
         scatter(0, 0)
+        copy_result(0, 1, 1, "gated_bias_2")
         scatter(0, 1)
-        finish_and_turn_tile(2, "c_words_0")
-        project_tile(2)
-        copy_result(1, 1, 1, "c_words_0")
-        copy_result(2, 0, 1, "z_copy_2")
+        turn(2)
+        lay_out(2)
+        turn(3)
+        project(2)
+        copy_result(1, 0, FT, "c_2")
+        lay_out(3)
+        project(3)
         scatter(1, 0)
         scatter(1, 1)
-        finish_and_turn_tile(3, "gated_y_3")
-        project_tile(3)
-        copy_result(2, 1, 1, "gated_y_3")
+        copy_result(2, 0, FT, "c_3")
         copy_result(3, 0, FT, "z_copy_3")
         for s in (2, 3):
             scatter(s, 0)

@@ -36,6 +36,7 @@ MOVED_ROWS = 112
 SCALAR_TILES = (1,)
 SCATTER_ENGINE = ("scalar", "vector")
 HELD = 3
+WARM_UP = 2
 
 AT_SHARED_SCALES = 0
 AT_W_BYTES_1 = 640
@@ -343,6 +344,17 @@ def tile_moe_nxt_lin_bias_kernel(tc, xT, w_words, w_scales, b, wp, gate, offs, o
                         in_=slot_scales[0][SHARED_ROW[u] : SHARED_ROW[u] + MOVED_ROWS, :].bitcast(I32),
                     )
             gather_words(a)
+        idle = psum.tile([P, N], F32, name="idle", tag="turn_2")
+        for u in range(WARM_UP):
+            nc.tensor.matmul_mx(
+                out=idle[:],
+                lhsT=slot_words[SHARED][:, 0:P].bitcast(FP8X4),
+                lhsT_scale=slot_scales[0][:, 0:P],
+                rhs=slot_words[SHARED][:].bitcast(FP8X4),
+                rhs_scale=slot_scales[0][:],
+                start=True,
+                stop=True,
+            )
         w_bytes[1] = reused.tile([P, PASSES, N], U8, name="w_bytes_1", offset=AT_W_BYTES_1, align_bytes=64)
         load_scales(1)
         load_codes(SHARED + 1, 3, AT_MIDDLE_CODES)

@@ -34,7 +34,6 @@ SHARED = 2
 SHARED_ROW = (0, 4, 8, 0, 0)
 MOVED_ROWS = 112
 SCALAR_TILES = (1,)
-SCATTER_ENGINE = ("scalar", "vector")
 HELD = 3
 WARM_UP = 2
 
@@ -287,10 +286,12 @@ def tile_moe_nxt_lin_bias_kernel(tc, xT, w_words, w_scales, b, wp, gate, offs, o
             if s in SCALAR_TILES:
                 nc.scalar.activation(out=c_turned[s][:], in_=turn_bank[s][:].rearrange("p j r -> p r j"), func=COPY)
             else:
-                nc.scalar.copy(
-                    out=c_turned[s][:].rearrange("p r j -> p (r j)").bitcast(F32).rearrange("p (r u) -> p r u", u=2),
-                    in_=turn_bank[s][:].rearrange("p u r -> p r u"),
-                )
+                dst = c_turned[s][:].rearrange("p r j -> p (r j)").bitcast(F32).rearrange("p (r u) -> p r u", u=2)
+                src = turn_bank[s][:].rearrange("p u r -> p r u")
+                if s < 2:
+                    nc.scalar.copy(out=dst, in_=src)
+                else:
+                    nc.vector.tensor_copy(dst, src)
 
         def project(s):
             slots = slice(s * P, (s + 1) * P)
@@ -315,13 +316,16 @@ def tile_moe_nxt_lin_bias_kernel(tc, xT, w_words, w_scales, b, wp, gate, offs, o
 
         def copy_result(s, first, count, tag):
             piece = keep.tile([P, count, P], F32, name=f"z_copy_{s}_{first}", tag=tag, align_bytes=64)
-            nc.scalar.activation(out=piece[:], in_=z_bank[s][:, first : first + count, :], func=COPY)
+            if s < 2:
+                nc.scalar.activation(out=piece[:], in_=z_bank[s][:, first : first + count, :], func=COPY)
+            else:
+                nc.vector.tensor_copy(piece[:], z_bank[s][:, first : first + count, :])
             for f in range(count):
                 z_copy[(s, first + f)] = piece[:, f, :]
 
         def scatter(s, f):
             window = out_tile[f][:].indirect(places(s))
-            if SCATTER_ENGINE[f] == "scalar":
+            if f == 1 or s < 2:
                 nc.scalar.activation(out=window, in_=z_copy[(s, f)], func=COPY)
             else:
                 nc.vector.tensor_copy(window, z_copy[(s, f)])
@@ -351,7 +355,7 @@ def tile_moe_nxt_lin_bias_kernel(tc, xT, w_words, w_scales, b, wp, gate, offs, o
                 lhsT=slot_words[SHARED][:, 0:P].bitcast(FP8X4),
                 lhsT_scale=slot_scales[0][:, 0:P],
                 rhs=slot_words[SHARED][:].bitcast(FP8X4),
-                rhs_scale=slot_scales[0][:],
+                rhs_scale=w_bytes[0][:, 0, :],
                 start=True,
                 stop=True,
             )
@@ -394,22 +398,12 @@ def tile_moe_nxt_lin_bias_kernel(tc, xT, w_words, w_scales, b, wp, gate, offs, o
         for s in (2, 3):
             multiply(s, (4,))
             finish(s)
-        copy_result(0, 0, 1, "z_copy_0")
-        scatter(0, 0)
-        copy_result(0, 1, 1, "gated_bias_2")
-        scatter(0, 1)
-        turn(2)
-        lay_out(2)
-        turn(3)
-        project(2)
-        copy_result(1, 0, FT, "c_2")
-        lay_out(3)
-        project(3)
-        scatter(1, 0)
-        scatter(1, 1)
-        copy_result(2, 0, FT, "c_3")
-        copy_result(3, 0, FT, "z_copy_3")
         for s in (2, 3):
+            turn(s)
+            lay_out(s)
+            project(s)
+        for s in range(TILES):
+            copy_result(s, 0, FT, f"z_copy_{s}")
             scatter(s, 0)
             scatter(s, 1)
         for f in range(FT):

@@ -20,8 +20,8 @@ CASTS = (
     (("vector", 0, 256), ("scalar", 256, 256), ("vector", 512, 128)),
     (("scalar", 256, 256), ("vector", 0, 256), ("vector", 512, 128)),
     (("scalar", 256, 256), ("vector", 0, 256), ("scalar", 512, 128)),
-    (("scalar", 0, 256), ("scalar", 256, 256), ("scalar", 512, 128)),
-    (("scalar", 0, 256), ("scalar", 256, 256), ("scalar", 512, 128)),
+    (("scalar", 0, 256), ("scalar", 256, 256), ("gpsimd", 512, 128)),
+    (("scalar", 0, 256), ("scalar", 256, 256), ("gpsimd", 512, 128)),
 )
 QUANTISED = (
     ((0, 256), (512, 128), (256, 256)),
@@ -35,6 +35,7 @@ SHARED_ROW = (0, 4, 8, 0, 0)
 MOVED_ROWS = 112
 SCALAR_TILES = (1,)
 HELD = 3
+SPLIT = 512
 WARM_UP = 2
 
 AT_SHARED_SCALES = 0
@@ -70,6 +71,8 @@ def tile_moe_nxt_lin_bias_kernel(tc, xT, w_words, w_scales, b, wp, gate, offs, o
         src = src.rearrange("p j (c i) -> p c j i", i=4)
         if engine == "scalar":
             nc.scalar.activation(out=dst, in_=src, func=COPY)
+        elif engine == "gpsimd":
+            nc.gpsimd.tensor_copy(dst, src)
         else:
             nc.vector.tensor_copy(dst, src)
 
@@ -152,11 +155,18 @@ def tile_moe_nxt_lin_bias_kernel(tc, xT, w_words, w_scales, b, wp, gate, offs, o
         for a in range(1, SHARED + 1):
             nc.gpsimd.memset(slot_scales[a][:].bitcast(I32), 0)
 
-        x_rounded = [keep.tile([P, T, PACK], BF16, name=f"x_rounded_{a}", align_bytes=64) for a in range(PASSES)]
+        x_rounded = {}
+
+        def rounded(a, t0, n):
+            if t0 < SPLIT:
+                return x_rounded[(a, 0)][:, t0 : t0 + n, :]
+            return x_rounded[(a, 1)][:, t0 - SPLIT : t0 - SPLIT + n, :]
 
         def round_tokens(a):
+            x_rounded[(a, 0)] = keep.tile([P, SPLIT, PACK], BF16, name=f"x_rounded_{a}", align_bytes=64)
+            x_rounded[(a, 1)] = keep.tile([P, T - SPLIT, PACK], BF16, name=f"x_rest_{a}", tag=f"x_rest_{min(a, SHARED)}", align_bytes=64)
             for engine, t0, n in CASTS[a]:
-                round_and_interleave(engine, x_rounded[a][:, t0 : t0 + n, :], x_raw[a][:, :, t0 : t0 + n])
+                round_and_interleave(engine, rounded(a, t0, n), x_raw[a][:, :, t0 : t0 + n])
 
         def quantise_tokens(a):
             row = SHARED_ROW[a]
@@ -164,7 +174,7 @@ def tile_moe_nxt_lin_bias_kernel(tc, xT, w_words, w_scales, b, wp, gate, offs, o
                 nc.vector.quantize_mx(
                     out=words[a][:, t0 : t0 + n].bitcast(FP8X4),
                     scales=scales[a][row:P, t0 : t0 + n],
-                    in_=x_rounded[a][:, t0 : t0 + n, :].rearrange("p t j -> p (t j)"),
+                    in_=rounded(a, t0, n).rearrange("p t j -> p (t j)"),
                 )
 
         def gather_words(a):

@@ -39,12 +39,12 @@ SPLIT = 512
 WARM_UP = 2
 
 AT_SHARED_SCALES = 0
-AT_W_BYTES_1 = 640
-AT_MIDDLE_CODES = 3200
-AT_SHARED_WORDS = 6208
-AT_WP_RAW = 8896
-AT_HELD_RAW = 12992
-AT_GATED_BIAS_0 = 23232
+AT_W_BYTES_1 = 512
+AT_MIDDLE_CODES = 3072
+AT_SHARED_WORDS = 5888
+AT_WP_RAW = 8448
+AT_HELD_RAW = 12544
+AT_GATED_BIAS_0 = 22784
 AT_TURNED_0 = AT_GATED_BIAS_0 + 4 * N
 
 FLOPS = 2 * K * N * S + 2 * N * M * T
@@ -90,7 +90,7 @@ def tile_moe_nxt_lin_bias_kernel(tc, xT, w_words, w_scales, b, wp, gate, offs, o
 
         bias_rows = keep.tile([P, PACK * E], F32, name="bias_rows")
         gate_column = keep.tile([P, TILES], F32, name="gate_column")
-        w_bytes = {0: keep.tile([P, PASSES, N], U8, name="w_bytes_0", align_bytes=64)}
+        w_bytes = {0: keep.tile([P, PASSES, N], U8, name="w_bytes_0", align_bytes=256)}
         w_codes = {}
         x_raw = {}
         nc.vector.memset(w_bytes[0][:].rearrange("p g n -> p (g n)").bitcast(I32), 0)
@@ -98,9 +98,9 @@ def tile_moe_nxt_lin_bias_kernel(tc, xT, w_words, w_scales, b, wp, gate, offs, o
         def load_tokens(a):
             rows = xT[P * PACK * a : P * PACK * (a + 1), :].rearrange("(p j) t -> p j t", j=PACK)
             if a == HELD:
-                x_raw[a] = reused.tile([P, PACK, T], F32, name=f"x_raw_{a}", offset=AT_HELD_RAW, align_bytes=64)
+                x_raw[a] = reused.tile([P, PACK, T], F32, name=f"x_raw_{a}", offset=AT_HELD_RAW, align_bytes=256)
             else:
-                x_raw[a] = keep.tile([P, PACK, T], F32, name=f"x_raw_{a}", align_bytes=64)
+                x_raw[a] = keep.tile([P, PACK, T], F32, name=f"x_raw_{a}", align_bytes=256)
             nc.sync.dma_start(out=x_raw[a][:], in_=rows)
 
         def load_scales(e):
@@ -110,9 +110,9 @@ def tile_moe_nxt_lin_bias_kernel(tc, xT, w_words, w_scales, b, wp, gate, offs, o
 
         def load_codes(first, count, offset=None):
             if offset is None:
-                piece = keep.tile([P, count, 2 * N], U8, name=f"w_codes_{first}", align_bytes=64)
+                piece = keep.tile([P, count, 2 * N], U8, name=f"w_codes_{first}", align_bytes=256)
             else:
-                piece = reused.tile([P, count, 2 * N], U8, name=f"w_codes_{first}", offset=offset, align_bytes=64)
+                piece = reused.tile([P, count, 2 * N], U8, name=f"w_codes_{first}", offset=offset, align_bytes=256)
             rows = w_words.rearrange("e a p c -> p (e a) c")[:, first : first + count, :]
             nc.sync.dma_start(out=piece[:].bitcast(I32), in_=rows.bitcast(I32))
             for u in range(count):
@@ -133,25 +133,25 @@ def tile_moe_nxt_lin_bias_kernel(tc, xT, w_words, w_scales, b, wp, gate, offs, o
         words = {}
         for a in range(PASSES):
             if a == SHARED:
-                words[a] = reused.tile([P, WORD_COLUMNS], I32, name=f"words_{a}", offset=AT_SHARED_WORDS, align_bytes=64)
+                words[a] = reused.tile([P, WORD_COLUMNS], I32, name=f"words_{a}", offset=AT_SHARED_WORDS, align_bytes=256)
             else:
-                words[a] = keep.tile([P, WORD_COLUMNS], I32, name=f"words_{a}", align_bytes=64)
+                words[a] = keep.tile([P, WORD_COLUMNS], I32, name=f"words_{a}", align_bytes=256)
         for a in range(PASSES):
             nc.vector.memset(words[a][:, T:WORD_COLUMNS], 0)
         scales = {}
         for a in range(SHARED, PASSES):
             if a == SHARED:
-                scales[a] = reused.tile([P, BYTE_COLUMNS], U8, name=f"scales_{a}", offset=AT_SHARED_SCALES, align_bytes=64)
+                scales[a] = reused.tile([P, BYTE_COLUMNS], U8, name=f"scales_{a}", offset=AT_SHARED_SCALES, align_bytes=256)
             else:
-                scales[a] = keep.tile([P, BYTE_COLUMNS], U8, name=f"scales_{a}", align_bytes=64)
+                scales[a] = keep.tile([P, BYTE_COLUMNS], U8, name=f"scales_{a}", align_bytes=256)
             nc.gpsimd.memset(scales[a][:, T:BYTE_COLUMNS], 0)
         for a in range(SHARED):
             scales[a] = scales[SHARED]
 
         slot_words, slot_scales = {}, {}
         for a in range(LAST):
-            slot_words[a] = keep.tile([P, S], U32, name=f"slot_words_{a}", align_bytes=64)
-            slot_scales[a] = keep.tile([P, S], U8, name=f"slot_scales_{a}", align_bytes=64)
+            slot_words[a] = keep.tile([P, S], U32, name=f"slot_words_{a}", align_bytes=256)
+            slot_scales[a] = keep.tile([P, S], U8, name=f"slot_scales_{a}", align_bytes=256)
         for a in range(1, SHARED + 1):
             nc.gpsimd.memset(slot_scales[a][:].bitcast(I32), 0)
 
@@ -163,8 +163,8 @@ def tile_moe_nxt_lin_bias_kernel(tc, xT, w_words, w_scales, b, wp, gate, offs, o
             return x_rounded[(a, 1)][:, t0 - SPLIT : t0 - SPLIT + n, :]
 
         def round_tokens(a):
-            x_rounded[(a, 0)] = keep.tile([P, SPLIT, PACK], BF16, name=f"x_rounded_{a}", align_bytes=64)
-            x_rounded[(a, 1)] = keep.tile([P, T - SPLIT, PACK], BF16, name=f"x_rest_{a}", tag=f"x_rest_{min(a, SHARED)}", align_bytes=64)
+            x_rounded[(a, 0)] = keep.tile([P, SPLIT, PACK], BF16, name=f"x_rounded_{a}", align_bytes=256)
+            x_rounded[(a, 1)] = keep.tile([P, T - SPLIT, PACK], BF16, name=f"x_rest_{a}", tag=f"x_rest_{min(a, SHARED)}", align_bytes=256)
             for engine, t0, n in CASTS[a]:
                 round_and_interleave(engine, rounded(a, t0, n), x_raw[a][:, :, t0 : t0 + n])
 
@@ -190,11 +190,11 @@ def tile_moe_nxt_lin_bias_kernel(tc, xT, w_words, w_scales, b, wp, gate, offs, o
 
         def gather_last(s, count, offset=None):
             if offset is None:
-                words_tile = keep.tile([P, count * P], U32, name=f"last_words_{s}", align_bytes=64)
-                bytes_tile = keep.tile([P, count * P], U8, name=f"last_scales_{s}", align_bytes=64)
+                words_tile = keep.tile([P, count * P], U32, name=f"last_words_{s}", align_bytes=256)
+                bytes_tile = keep.tile([P, count * P], U8, name=f"last_scales_{s}", align_bytes=256)
             else:
-                words_tile = reused.tile([P, count * P], U32, name=f"last_words_{s}", offset=offset, align_bytes=64)
-                bytes_tile = reused.tile([P, count * P], U8, name=f"last_scales_{s}", offset=offset + 4 * count * P, align_bytes=64)
+                words_tile = reused.tile([P, count * P], U32, name=f"last_words_{s}", offset=offset, align_bytes=256)
+                bytes_tile = reused.tile([P, count * P], U8, name=f"last_scales_{s}", offset=offset + 4 * count * P, align_bytes=256)
             nc.vector.tensor_copy(words_tile[:], words[LAST][:].bitcast(U32).indirect(places(s, count)))
             nc.vector.tensor_copy(bytes_tile[:], scales[LAST][:].indirect(places(s, count)))
             for u in range(count):
@@ -219,9 +219,9 @@ def tile_moe_nxt_lin_bias_kernel(tc, xT, w_words, w_scales, b, wp, gate, offs, o
                     stop=(a == LAST),
                 )
 
-        gated_bias = [reused.tile([P, N], F32, name="gated_bias_0", offset=AT_GATED_BIAS_0, align_bytes=64)]
+        gated_bias = [reused.tile([P, N], F32, name="gated_bias_0", offset=AT_GATED_BIAS_0, align_bytes=256)]
         for s in range(1, TILES):
-            gated_bias.append(keep.tile([P, N], F32, name=f"gated_bias_{s}", tag=f"gated_bias_{s}", align_bytes=64))
+            gated_bias.append(keep.tile([P, N], F32, name=f"gated_bias_{s}", tag=f"gated_bias_{s}", align_bytes=256))
         turn_bank = {}
 
         def spread_bias():
@@ -257,16 +257,16 @@ def tile_moe_nxt_lin_bias_kernel(tc, xT, w_words, w_scales, b, wp, gate, offs, o
             turn_bank[s] = psum.tile([P, PACK, P], F32, name=f"sum_{s}", tag=f"turn_{s}")
             turn_and_add(s, gated_bias[s], True)
 
-        wp_rounded = keep.tile([P, M, PACK], BF16, name="wp_rounded", align_bytes=64)
-        wp_words = keep.tile([P, M], U32, name="wp_words", align_bytes=64)
-        wp_scales = keep.tile([P, M], U8, name="wp_scales", align_bytes=64)
+        wp_rounded = keep.tile([P, M, PACK], BF16, name="wp_rounded", align_bytes=256)
+        wp_words = keep.tile([P, M], U32, name="wp_words", align_bytes=256)
+        wp_scales = keep.tile([P, M], U8, name="wp_scales", align_bytes=256)
 
         c, gated_y, c_turned, c_words, z_bank, z_copy = {}, {}, {}, {}, {}, {}
-        c_scales = keep.tile([P, S], U8, name="c_scales", align_bytes=64)
+        c_scales = keep.tile([P, S], U8, name="c_scales", align_bytes=256)
 
         def finish(s):
             if s in SCALAR_TILES:
-                gated_y[s] = keep.tile([P, N], F32, name=f"gated_y_{s}", align_bytes=64)
+                gated_y[s] = keep.tile([P, N], F32, name=f"gated_y_{s}", align_bytes=256)
                 nc.scalar.activation(
                     out=gated_y[s][:].rearrange("s (j q) -> s j q", j=PACK),
                     in_=y[s][:].rearrange("s (q j) -> s j q", j=PACK),
@@ -274,7 +274,7 @@ def tile_moe_nxt_lin_bias_kernel(tc, xT, w_words, w_scales, b, wp, gate, offs, o
                     scale=gate_column[:, s : s + 1],
                 )
             else:
-                c[s] = keep.tile([P, N], BF16, name=f"c_{s}", tag=f"c_{s}", align_bytes=64)
+                c[s] = keep.tile([P, N], BF16, name=f"c_{s}", tag=f"c_{s}", align_bytes=256)
                 nc.vector.scalar_tensor_tensor(
                     out=c[s][:], in0=y[s][:], scalar=gate_column[:, s : s + 1], in1=gated_bias[s][:], op0=MULT, op1=ADD
                 )
@@ -290,9 +290,9 @@ def tile_moe_nxt_lin_bias_kernel(tc, xT, w_words, w_scales, b, wp, gate, offs, o
 
         def lay_out(s):
             if s == 0:
-                c_turned[s] = reused.tile([P, P, PACK], BF16, name=f"c_turned_{s}", offset=AT_TURNED_0, align_bytes=64)
+                c_turned[s] = reused.tile([P, P, PACK], BF16, name=f"c_turned_{s}", offset=AT_TURNED_0, align_bytes=256)
             else:
-                c_turned[s] = keep.tile([P, P, PACK], BF16, name=f"c_turned_{s}", align_bytes=64)
+                c_turned[s] = keep.tile([P, P, PACK], BF16, name=f"c_turned_{s}", align_bytes=256)
             if s in SCALAR_TILES:
                 nc.scalar.activation(out=c_turned[s][:], in_=turn_bank[s][:].rearrange("p j r -> p r j"), func=COPY)
             else:
@@ -305,7 +305,7 @@ def tile_moe_nxt_lin_bias_kernel(tc, xT, w_words, w_scales, b, wp, gate, offs, o
 
         def project(s):
             slots = slice(s * P, (s + 1) * P)
-            c_words[s] = keep.tile([P, P], U32, name=f"c_words_{s}", align_bytes=64)
+            c_words[s] = keep.tile([P, P], U32, name=f"c_words_{s}", align_bytes=256)
             nc.vector.quantize_mx(
                 out=c_words[s][:].bitcast(FP8X4),
                 scales=c_scales[:, slots],
@@ -325,7 +325,7 @@ def tile_moe_nxt_lin_bias_kernel(tc, xT, w_words, w_scales, b, wp, gate, offs, o
                 )
 
         def copy_result(s, first, count, tag):
-            piece = keep.tile([P, count, P], F32, name=f"z_copy_{s}_{first}", tag=tag, align_bytes=64)
+            piece = keep.tile([P, count, P], F32, name=f"z_copy_{s}_{first}", tag=tag, align_bytes=256)
             if s < 2:
                 nc.scalar.activation(out=piece[:], in_=z_bank[s][:, first : first + count, :], func=COPY)
             else:
@@ -365,14 +365,14 @@ def tile_moe_nxt_lin_bias_kernel(tc, xT, w_words, w_scales, b, wp, gate, offs, o
                 lhsT=slot_words[SHARED][:, 0:P].bitcast(FP8X4),
                 lhsT_scale=slot_scales[0][:, 0:P],
                 rhs=slot_words[SHARED][:].bitcast(FP8X4),
-                rhs_scale=w_bytes[0][:, 0, :],
+                rhs_scale=slot_scales[0][:],
                 start=True,
                 stop=True,
             )
-        w_bytes[1] = reused.tile([P, PASSES, N], U8, name="w_bytes_1", offset=AT_W_BYTES_1, align_bytes=64)
+        w_bytes[1] = reused.tile([P, PASSES, N], U8, name="w_bytes_1", offset=AT_W_BYTES_1, align_bytes=256)
         load_scales(1)
         load_codes(SHARED + 1, 3, AT_MIDDLE_CODES)
-        wp_raw = reused.tile([P, PACK, M], F32, name="wp_raw", offset=AT_WP_RAW, align_bytes=64)
+        wp_raw = reused.tile([P, PACK, M], F32, name="wp_raw", offset=AT_WP_RAW, align_bytes=256)
         nc.sync.dma_start(out=wp_raw[:], in_=wp.rearrange("(p j) f -> p j f", j=PACK))
         for u in range(2):
             load_codes(PASSES + 1 + 2 * u, 2, AT_HELD_RAW + 2 * 2 * N * u)

@@ -13,6 +13,8 @@ FT = M // P
 LIST = 16
 LAST = PASSES - 1
 
+ALIGN = 256
+
 WORD_COLUMNS = 688
 BYTE_COLUMNS = 704
 
@@ -30,19 +32,20 @@ QUANTISED = (
     ((0, 512), (512, 128)),
     ((0, 512), (512, 128)),
 )
+SPLIT = 512
 SHARED = 2
 SHARED_ROW = (0, 4, 8, 0, 0)
-MOVED_ROWS = 112
-SCALAR_TILES = (1,)
-HELD = 3
-SPLIT = 512
+MOVED_ROWS = 100
 WARM_UP = 2
+SCALAR_TILE = 1
+EARLY_TILES = (0, 1)
 
 AT_SHARED_SCALES = 0
 AT_W_BYTES_1 = 512
-AT_MIDDLE_CODES = 3072
 AT_SHARED_WORDS = 5888
+AT_MIDDLE_CODES = 3072
 AT_WP_RAW = 8448
+HELD = 3
 AT_HELD_RAW = 12544
 AT_GATED_BIAS_0 = 22784
 AT_TURNED_0 = AT_GATED_BIAS_0 + 4 * N
@@ -90,7 +93,7 @@ def tile_moe_nxt_lin_bias_kernel(tc, xT, w_words, w_scales, b, wp, gate, offs, o
 
         bias_rows = keep.tile([P, PACK * E], F32, name="bias_rows")
         gate_column = keep.tile([P, TILES], F32, name="gate_column")
-        w_bytes = {0: keep.tile([P, PASSES, N], U8, name="w_bytes_0", align_bytes=256)}
+        w_bytes = {0: keep.tile([P, PASSES, N], U8, name="w_bytes_0", align_bytes=ALIGN)}
         w_codes = {}
         x_raw = {}
         nc.vector.memset(w_bytes[0][:].rearrange("p g n -> p (g n)").bitcast(I32), 0)
@@ -98,9 +101,9 @@ def tile_moe_nxt_lin_bias_kernel(tc, xT, w_words, w_scales, b, wp, gate, offs, o
         def load_tokens(a):
             rows = xT[P * PACK * a : P * PACK * (a + 1), :].rearrange("(p j) t -> p j t", j=PACK)
             if a == HELD:
-                x_raw[a] = reused.tile([P, PACK, T], F32, name=f"x_raw_{a}", offset=AT_HELD_RAW, align_bytes=256)
+                x_raw[a] = reused.tile([P, PACK, T], F32, name=f"x_raw_{a}", offset=AT_HELD_RAW, align_bytes=ALIGN)
             else:
-                x_raw[a] = keep.tile([P, PACK, T], F32, name=f"x_raw_{a}", align_bytes=256)
+                x_raw[a] = keep.tile([P, PACK, T], F32, name=f"x_raw_{a}", align_bytes=ALIGN)
             nc.sync.dma_start(out=x_raw[a][:], in_=rows)
 
         def load_scales(e):
@@ -110,9 +113,9 @@ def tile_moe_nxt_lin_bias_kernel(tc, xT, w_words, w_scales, b, wp, gate, offs, o
 
         def load_codes(first, count, offset=None):
             if offset is None:
-                piece = keep.tile([P, count, 2 * N], U8, name=f"w_codes_{first}", align_bytes=256)
+                piece = keep.tile([P, count, 2 * N], U8, name=f"w_codes_{first}", align_bytes=ALIGN)
             else:
-                piece = reused.tile([P, count, 2 * N], U8, name=f"w_codes_{first}", offset=offset, align_bytes=256)
+                piece = reused.tile([P, count, 2 * N], U8, name=f"w_codes_{first}", offset=offset, align_bytes=ALIGN)
             rows = w_words.rearrange("e a p c -> p (e a) c")[:, first : first + count, :]
             nc.sync.dma_start(out=piece[:].bitcast(I32), in_=rows.bitcast(I32))
             for u in range(count):
@@ -133,25 +136,25 @@ def tile_moe_nxt_lin_bias_kernel(tc, xT, w_words, w_scales, b, wp, gate, offs, o
         words = {}
         for a in range(PASSES):
             if a == SHARED:
-                words[a] = reused.tile([P, WORD_COLUMNS], I32, name=f"words_{a}", offset=AT_SHARED_WORDS, align_bytes=256)
+                words[a] = reused.tile([P, WORD_COLUMNS], I32, name=f"words_{a}", offset=AT_SHARED_WORDS, align_bytes=ALIGN)
             else:
-                words[a] = keep.tile([P, WORD_COLUMNS], I32, name=f"words_{a}", align_bytes=256)
+                words[a] = keep.tile([P, WORD_COLUMNS], I32, name=f"words_{a}", align_bytes=ALIGN)
         for a in range(PASSES):
             nc.vector.memset(words[a][:, T:WORD_COLUMNS], 0)
         scales = {}
         for a in range(SHARED, PASSES):
             if a == SHARED:
-                scales[a] = reused.tile([P, BYTE_COLUMNS], U8, name=f"scales_{a}", offset=AT_SHARED_SCALES, align_bytes=256)
+                scales[a] = reused.tile([P, BYTE_COLUMNS], U8, name=f"scales_{a}", offset=AT_SHARED_SCALES, align_bytes=ALIGN)
             else:
-                scales[a] = keep.tile([P, BYTE_COLUMNS], U8, name=f"scales_{a}", align_bytes=256)
+                scales[a] = keep.tile([P, BYTE_COLUMNS], U8, name=f"scales_{a}", align_bytes=ALIGN)
             nc.gpsimd.memset(scales[a][:, T:BYTE_COLUMNS], 0)
         for a in range(SHARED):
             scales[a] = scales[SHARED]
 
         slot_words, slot_scales = {}, {}
         for a in range(LAST):
-            slot_words[a] = keep.tile([P, S], U32, name=f"slot_words_{a}", align_bytes=256)
-            slot_scales[a] = keep.tile([P, S], U8, name=f"slot_scales_{a}", align_bytes=256)
+            slot_words[a] = keep.tile([P, S], U32, name=f"slot_words_{a}", align_bytes=ALIGN)
+            slot_scales[a] = keep.tile([P, S], U8, name=f"slot_scales_{a}", align_bytes=ALIGN)
         for a in range(1, SHARED + 1):
             nc.gpsimd.memset(slot_scales[a][:].bitcast(I32), 0)
 
@@ -163,8 +166,9 @@ def tile_moe_nxt_lin_bias_kernel(tc, xT, w_words, w_scales, b, wp, gate, offs, o
             return x_rounded[(a, 1)][:, t0 - SPLIT : t0 - SPLIT + n, :]
 
         def round_tokens(a):
-            x_rounded[(a, 0)] = keep.tile([P, SPLIT, PACK], BF16, name=f"x_rounded_{a}", align_bytes=256)
-            x_rounded[(a, 1)] = keep.tile([P, T - SPLIT, PACK], BF16, name=f"x_rest_{a}", tag=f"x_rest_{min(a, SHARED)}", align_bytes=256)
+            x_rounded[(a, 0)] = keep.tile([P, SPLIT, PACK], BF16, name=f"x_rounded_{a}", align_bytes=ALIGN)
+            tag = f"x_rest_{min(a, SHARED)}"
+            x_rounded[(a, 1)] = keep.tile([P, T - SPLIT, PACK], BF16, name=f"x_rest_{a}", tag=tag, align_bytes=ALIGN)
             for engine, t0, n in CASTS[a]:
                 round_and_interleave(engine, rounded(a, t0, n), x_raw[a][:, :, t0 : t0 + n])
 
@@ -183,22 +187,21 @@ def tile_moe_nxt_lin_bias_kernel(tc, xT, w_words, w_scales, b, wp, gate, offs, o
         def gather_scales(a):
             nc.vector.tensor_copy(slot_scales[a][:], scales[a][:].indirect(offsets[:]))
 
-        def places(s, count=1):
-            return offsets[:, s * P // LIST : (s + count) * P // LIST]
+        def places(s):
+            return offsets[:, s * P // LIST : (s + 1) * P // LIST]
 
         last = {}
 
-        def gather_last(s, count, offset=None):
+        def gather_last(s, offset=None):
             if offset is None:
-                words_tile = keep.tile([P, count * P], U32, name=f"last_words_{s}", align_bytes=256)
-                bytes_tile = keep.tile([P, count * P], U8, name=f"last_scales_{s}", align_bytes=256)
+                words_tile = keep.tile([P, P], U32, name=f"last_words_{s}", align_bytes=ALIGN)
+                bytes_tile = keep.tile([P, P], U8, name=f"last_scales_{s}", align_bytes=ALIGN)
             else:
-                words_tile = reused.tile([P, count * P], U32, name=f"last_words_{s}", offset=offset, align_bytes=256)
-                bytes_tile = reused.tile([P, count * P], U8, name=f"last_scales_{s}", offset=offset + 4 * count * P, align_bytes=256)
-            nc.vector.tensor_copy(words_tile[:], words[LAST][:].bitcast(U32).indirect(places(s, count)))
-            nc.vector.tensor_copy(bytes_tile[:], scales[LAST][:].indirect(places(s, count)))
-            for u in range(count):
-                last[s + u] = (words_tile[:, u * P : (u + 1) * P], bytes_tile[:, u * P : (u + 1) * P])
+                words_tile = reused.tile([P, P], U32, name=f"last_words_{s}", offset=offset, align_bytes=ALIGN)
+                bytes_tile = reused.tile([P, P], U8, name=f"last_scales_{s}", offset=offset + 4 * P, align_bytes=ALIGN)
+            nc.vector.tensor_copy(words_tile[:], words[LAST][:].bitcast(U32).indirect(places(s)))
+            nc.vector.tensor_copy(bytes_tile[:], scales[LAST][:].indirect(places(s)))
+            last[s] = (words_tile[:], bytes_tile[:])
 
         y = {}
 
@@ -219,9 +222,9 @@ def tile_moe_nxt_lin_bias_kernel(tc, xT, w_words, w_scales, b, wp, gate, offs, o
                     stop=(a == LAST),
                 )
 
-        gated_bias = [reused.tile([P, N], F32, name="gated_bias_0", offset=AT_GATED_BIAS_0, align_bytes=256)]
+        gated_bias = [reused.tile([P, N], F32, name="gated_bias_0", offset=AT_GATED_BIAS_0, align_bytes=ALIGN)]
         for s in range(1, TILES):
-            gated_bias.append(keep.tile([P, N], F32, name=f"gated_bias_{s}", tag=f"gated_bias_{s}", align_bytes=256))
+            gated_bias.append(keep.tile([P, N], F32, name=f"gated_bias_{s}", align_bytes=ALIGN))
         turn_bank = {}
 
         def spread_bias():
@@ -234,7 +237,7 @@ def tile_moe_nxt_lin_bias_kernel(tc, xT, w_words, w_scales, b, wp, gate, offs, o
                     column = bias_rows[:, E * j + e : E * j + e + 1]
                     nc.tensor.transpose(spread[:, j, :], column.to_broadcast([P, P]), identity[:])
                 for s in (2 * e, 2 * e + 1):
-                    if s in SCALAR_TILES:
+                    if s == SCALAR_TILE:
                         dst = gated_bias[s][:].rearrange("s (j q) -> s j q", j=PACK)
                         src = spread[:]
                     else:
@@ -257,16 +260,16 @@ def tile_moe_nxt_lin_bias_kernel(tc, xT, w_words, w_scales, b, wp, gate, offs, o
             turn_bank[s] = psum.tile([P, PACK, P], F32, name=f"sum_{s}", tag=f"turn_{s}")
             turn_and_add(s, gated_bias[s], True)
 
-        wp_rounded = keep.tile([P, M, PACK], BF16, name="wp_rounded", align_bytes=256)
-        wp_words = keep.tile([P, M], U32, name="wp_words", align_bytes=256)
-        wp_scales = keep.tile([P, M], U8, name="wp_scales", align_bytes=256)
+        wp_rounded = keep.tile([P, M, PACK], BF16, name="wp_rounded", align_bytes=ALIGN)
+        wp_words = keep.tile([P, M], U32, name="wp_words", align_bytes=ALIGN)
+        wp_scales = keep.tile([P, M], U8, name="wp_scales", align_bytes=ALIGN)
 
         c, gated_y, c_turned, c_words, z_bank, z_copy = {}, {}, {}, {}, {}, {}
-        c_scales = keep.tile([P, S], U8, name="c_scales", align_bytes=256)
+        c_scales = keep.tile([P, S], U8, name="c_scales", align_bytes=ALIGN)
 
         def finish(s):
-            if s in SCALAR_TILES:
-                gated_y[s] = keep.tile([P, N], F32, name=f"gated_y_{s}", align_bytes=256)
+            if s == SCALAR_TILE:
+                gated_y[s] = keep.tile([P, N], F32, name=f"gated_y_{s}", align_bytes=ALIGN)
                 nc.scalar.activation(
                     out=gated_y[s][:].rearrange("s (j q) -> s j q", j=PACK),
                     in_=y[s][:].rearrange("s (q j) -> s j q", j=PACK),
@@ -274,13 +277,13 @@ def tile_moe_nxt_lin_bias_kernel(tc, xT, w_words, w_scales, b, wp, gate, offs, o
                     scale=gate_column[:, s : s + 1],
                 )
             else:
-                c[s] = keep.tile([P, N], BF16, name=f"c_{s}", tag=f"c_{s}", align_bytes=256)
+                c[s] = keep.tile([P, N], BF16, name=f"c_{s}", align_bytes=ALIGN)
                 nc.vector.scalar_tensor_tensor(
                     out=c[s][:], in0=y[s][:], scalar=gate_column[:, s : s + 1], in1=gated_bias[s][:], op0=MULT, op1=ADD
                 )
 
         def turn(s):
-            if s in SCALAR_TILES:
+            if s == SCALAR_TILE:
                 turn_and_add(s, gated_y[s], False)
             else:
                 turn_bank[s] = psum.tile([P, 2, P], F32, name=f"turned_{s}", tag=f"turn_{s}")
@@ -290,22 +293,22 @@ def tile_moe_nxt_lin_bias_kernel(tc, xT, w_words, w_scales, b, wp, gate, offs, o
 
         def lay_out(s):
             if s == 0:
-                c_turned[s] = reused.tile([P, P, PACK], BF16, name=f"c_turned_{s}", offset=AT_TURNED_0, align_bytes=256)
+                c_turned[s] = reused.tile([P, P, PACK], BF16, name=f"c_turned_{s}", offset=AT_TURNED_0, align_bytes=ALIGN)
             else:
-                c_turned[s] = keep.tile([P, P, PACK], BF16, name=f"c_turned_{s}", align_bytes=256)
-            if s in SCALAR_TILES:
+                c_turned[s] = keep.tile([P, P, PACK], BF16, name=f"c_turned_{s}", align_bytes=ALIGN)
+            if s == SCALAR_TILE:
                 nc.scalar.activation(out=c_turned[s][:], in_=turn_bank[s][:].rearrange("p j r -> p r j"), func=COPY)
             else:
                 dst = c_turned[s][:].rearrange("p r j -> p (r j)").bitcast(F32).rearrange("p (r u) -> p r u", u=2)
                 src = turn_bank[s][:].rearrange("p u r -> p r u")
-                if s < 2:
+                if s in EARLY_TILES:
                     nc.scalar.copy(out=dst, in_=src)
                 else:
                     nc.vector.tensor_copy(dst, src)
 
         def project(s):
             slots = slice(s * P, (s + 1) * P)
-            c_words[s] = keep.tile([P, P], U32, name=f"c_words_{s}", align_bytes=256)
+            c_words[s] = keep.tile([P, P], U32, name=f"c_words_{s}", align_bytes=ALIGN)
             nc.vector.quantize_mx(
                 out=c_words[s][:].bitcast(FP8X4),
                 scales=c_scales[:, slots],
@@ -324,21 +327,19 @@ def tile_moe_nxt_lin_bias_kernel(tc, xT, w_words, w_scales, b, wp, gate, offs, o
                     stop=True,
                 )
 
-        def copy_result(s, first, count, tag):
-            piece = keep.tile([P, count, P], F32, name=f"z_copy_{s}_{first}", tag=tag, align_bytes=256)
-            if s < 2:
-                nc.scalar.activation(out=piece[:], in_=z_bank[s][:, first : first + count, :], func=COPY)
+        def copy_result(s):
+            z_copy[s] = keep.tile([P, FT, P], F32, name=f"z_copy_{s}", align_bytes=ALIGN)
+            if s in EARLY_TILES:
+                nc.scalar.activation(out=z_copy[s][:], in_=z_bank[s][:], func=COPY)
             else:
-                nc.vector.tensor_copy(piece[:], z_bank[s][:, first : first + count, :])
-            for f in range(count):
-                z_copy[(s, first + f)] = piece[:, f, :]
+                nc.vector.tensor_copy(z_copy[s][:], z_bank[s][:])
 
         def scatter(s, f):
             window = out_tile[f][:].indirect(places(s))
-            if f == 1 or s < 2:
-                nc.scalar.activation(out=window, in_=z_copy[(s, f)], func=COPY)
+            if s in EARLY_TILES or f == FT - 1:
+                nc.scalar.activation(out=window, in_=z_copy[s][:, f, :], func=COPY)
             else:
-                nc.vector.tensor_copy(window, z_copy[(s, f)])
+                nc.vector.tensor_copy(window, z_copy[s][:, f, :])
 
         round_tokens(0)
         for a in range(LAST):
@@ -346,8 +347,7 @@ def tile_moe_nxt_lin_bias_kernel(tc, xT, w_words, w_scales, b, wp, gate, offs, o
             round_tokens(a + 1)
             if a == 0:
                 spread_bias()
-                for s in SCALAR_TILES:
-                    open_tile(s)
+                open_tile(SCALAR_TILE)
             if a > SHARED:
                 gather_scales(a)
             if a == SHARED:
@@ -369,23 +369,23 @@ def tile_moe_nxt_lin_bias_kernel(tc, xT, w_words, w_scales, b, wp, gate, offs, o
                 start=True,
                 stop=True,
             )
-        w_bytes[1] = reused.tile([P, PASSES, N], U8, name="w_bytes_1", offset=AT_W_BYTES_1, align_bytes=256)
+        w_bytes[1] = reused.tile([P, PASSES, N], U8, name="w_bytes_1", offset=AT_W_BYTES_1, align_bytes=ALIGN)
         load_scales(1)
         load_codes(SHARED + 1, 3, AT_MIDDLE_CODES)
-        wp_raw = reused.tile([P, PACK, M], F32, name="wp_raw", offset=AT_WP_RAW, align_bytes=256)
+        wp_raw = reused.tile([P, PACK, M], F32, name="wp_raw", offset=AT_WP_RAW, align_bytes=ALIGN)
         nc.sync.dma_start(out=wp_raw[:], in_=wp.rearrange("(p j) f -> p j f", j=PACK))
         for u in range(2):
             load_codes(PASSES + 1 + 2 * u, 2, AT_HELD_RAW + 2 * 2 * N * u)
 
         quantise_tokens(LAST)
         for a in range(LAST):
-            for s in (0, 1):
+            for s in EARLY_TILES:
                 multiply(s, (a,))
         for s in (2, 3):
             multiply(s, (0,))
         round_and_interleave("scalar", wp_rounded[:], wp_raw[:])
-        for s in (0, 1):
-            gather_last(s, 1)
+        for s in EARLY_TILES:
+            gather_last(s)
             multiply(s, (LAST,))
             finish(s)
         nc.vector.quantize_mx(
@@ -394,27 +394,27 @@ def tile_moe_nxt_lin_bias_kernel(tc, xT, w_words, w_scales, b, wp, gate, offs, o
         multiply(2, (1,))
         turn(0)
         lay_out(0)
-        gather_last(2, 1, AT_GATED_BIAS_0)
+        gather_last(2, AT_GATED_BIAS_0)
         multiply(3, (1,))
         multiply(2, (2,))
         turn(1)
         lay_out(1)
         multiply(3, (2,))
         project(0)
-        gather_last(3, 1, AT_TURNED_0)
+        gather_last(3, AT_TURNED_0)
         for s in (2, 3):
             multiply(s, (3,))
         project(1)
         for s in (2, 3):
-            multiply(s, (4,))
+            multiply(s, (LAST,))
             finish(s)
         for s in (2, 3):
             turn(s)
             lay_out(s)
             project(s)
         for s in range(TILES):
-            copy_result(s, 0, FT, f"z_copy_{s}")
-            scatter(s, 0)
-            scatter(s, 1)
+            copy_result(s)
+            for f in range(FT):
+                scatter(s, f)
         for f in range(FT):
             nc.sync.dma_start(out=out[f * P : (f + 1) * P, :], in_=out_tile[f][:])

@@ -21,15 +21,15 @@ BYTE_COLUMNS = 704
 CASTS = (
     (("vector", 0, 256), ("scalar", 256, 256), ("vector", 512, 128)),
     (("scalar", 256, 256), ("vector", 0, 256), ("vector", 512, 128)),
-    (("scalar", 256, 256), ("vector", 0, 256), ("scalar", 512, 128)),
+    (("scalar", 256, 256), ("vector", 0, 256), ("vector", 512, 128)),
     (("scalar", 0, 256), ("scalar", 256, 256), ("gpsimd", 512, 128)),
     (("scalar", 0, 256), ("scalar", 256, 256), ("gpsimd", 512, 128)),
 )
 QUANTISED = (
     ((0, 256), (512, 128), (256, 256)),
     ((0, 256), (512, 128), (256, 256)),
-    ((0, 256), (256, 256), (512, 128)),
-    ((0, 512), (512, 128)),
+    ((0, 256), (512, 128), (256, 256)),
+    ((0, 256), (512, 128), (256, 256)),
     ((0, 512), (512, 128)),
 )
 SPLIT = 512
@@ -48,7 +48,8 @@ AT_WP_RAW = 8448
 HELD = 3
 AT_HELD_RAW = 12544
 AT_GATED_BIAS_0 = 22784
-AT_TURNED_0 = AT_GATED_BIAS_0 + 4 * N
+AT_LAST_RAW = AT_GATED_BIAS_0
+AT_TURNED_0 = AT_LAST_RAW + 4 * PACK * T
 
 FLOPS = 2 * K * N * S + 2 * N * M * T
 BYTES = 4 * (K * T + N * E + N * M + S + M * T) + E * PASSES * (2 * P * N + 16 * N) + 2 * P * S // LIST
@@ -102,6 +103,8 @@ def tile_moe_nxt_lin_bias_kernel(tc, xT, w_words, w_scales, b, wp, gate, offs, o
             rows = xT[P * PACK * a : P * PACK * (a + 1), :].rearrange("(p j) t -> p j t", j=PACK)
             if a == HELD:
                 x_raw[a] = reused.tile([P, PACK, T], F32, name=f"x_raw_{a}", offset=AT_HELD_RAW, align_bytes=ALIGN)
+            elif a == LAST:
+                x_raw[a] = reused.tile([P, PACK, T], F32, name=f"x_raw_{a}", offset=AT_LAST_RAW, align_bytes=ALIGN)
             else:
                 x_raw[a] = keep.tile([P, PACK, T], F32, name=f"x_raw_{a}", align_bytes=ALIGN)
             nc.sync.dma_start(out=x_raw[a][:], in_=rows)
@@ -223,27 +226,33 @@ def tile_moe_nxt_lin_bias_kernel(tc, xT, w_words, w_scales, b, wp, gate, offs, o
                 )
 
         gated_bias = [reused.tile([P, N], F32, name="gated_bias_0", offset=AT_GATED_BIAS_0, align_bytes=ALIGN)]
-        for s in range(1, TILES):
-            gated_bias.append(keep.tile([P, N], F32, name=f"gated_bias_{s}", align_bytes=ALIGN))
+        gated_bias.append(keep.tile([P, N], F32, name="gated_bias_1", align_bytes=ALIGN))
+        for s in (2, 3):
+            at = AT_LAST_RAW + 4 * N * (s - 1)
+            gated_bias.append(reused.tile([P, N], F32, name=f"gated_bias_{s}", offset=at, align_bytes=ALIGN))
         turn_bank = {}
 
-        def spread_bias():
+        def turn_gate():
             gate_turned = psum.tile([P, P], F32, name="gate_turned", tag="y_3")
             nc.tensor.transpose(gate_turned[:], gate_rows[:], identity[:])
             nc.scalar.activation(out=gate_column[:], in_=gate_turned[:, 0:TILES], func=COPY)
-            for e in range(E):
-                spread = psum.tile([P, PACK, P], F32, name=f"spread_{e}", tag=f"y_{e}")
-                for j in range(PACK):
-                    column = bias_rows[:, E * j + e : E * j + e + 1]
-                    nc.tensor.transpose(spread[:, j, :], column.to_broadcast([P, P]), identity[:])
-                for s in (2 * e, 2 * e + 1):
-                    if s == SCALAR_TILE:
-                        dst = gated_bias[s][:].rearrange("s (j q) -> s j q", j=PACK)
-                        src = spread[:]
-                    else:
-                        dst = gated_bias[s][:].rearrange("s (q j) -> s q j", j=PACK)
-                        src = spread[:].rearrange("s j q -> s q j")
-                    nc.scalar.activation(out=dst, in_=src, func=COPY, scale=gate_column[:, s : s + 1])
+
+        spread = {}
+
+        def spread_bias(e):
+            spread[e] = psum.tile([P, PACK, P], F32, name=f"spread_{e}", tag=f"turn_{3 * e}")
+            for j in range(PACK):
+                column = bias_rows[:, E * j + e : E * j + e + 1]
+                nc.tensor.transpose(spread[e][:, j, :], column.to_broadcast([P, P]), identity[:])
+
+        def gate_bias(s):
+            if s == SCALAR_TILE:
+                dst = gated_bias[s][:].rearrange("s (j q) -> s j q", j=PACK)
+                src = spread[s // 2][:]
+            else:
+                dst = gated_bias[s][:].rearrange("s (u q e) -> s u q e", u=2, e=2)
+                src = spread[s // 2][:].rearrange("s (u e) q -> s u q e", u=2)
+            nc.scalar.activation(out=dst, in_=src, func=COPY, scale=gate_column[:, s : s + 1])
 
         def turn_and_add(s, src, first):
             for j in range(PACK):
@@ -278,9 +287,17 @@ def tile_moe_nxt_lin_bias_kernel(tc, xT, w_words, w_scales, b, wp, gate, offs, o
                 )
             else:
                 c[s] = keep.tile([P, N], BF16, name=f"c_{s}", align_bytes=ALIGN)
-                nc.vector.scalar_tensor_tensor(
-                    out=c[s][:], in0=y[s][:], scalar=gate_column[:, s : s + 1], in1=gated_bias[s][:], op0=MULT, op1=ADD
-                )
+                sums = y[s][:].rearrange("s (q u e) -> s u q e", u=2, e=2)
+                for u in range(2):
+                    half = slice(u * N // 2, (u + 1) * N // 2)
+                    nc.vector.scalar_tensor_tensor(
+                        out=c[s][:, half].rearrange("s (q e) -> s q e", e=2),
+                        in0=sums[:, u, :, :],
+                        scalar=gate_column[:, s : s + 1],
+                        in1=gated_bias[s][:, half].rearrange("s (q e) -> s q e", e=2),
+                        op0=MULT,
+                        op1=ADD,
+                    )
 
         def turn(s):
             if s == SCALAR_TILE:
@@ -289,7 +306,7 @@ def tile_moe_nxt_lin_bias_kernel(tc, xT, w_words, w_scales, b, wp, gate, offs, o
                 turn_bank[s] = psum.tile([P, 2, P], F32, name=f"turned_{s}", tag=f"turn_{s}")
                 pairs = c[s][:].bitcast(F32)
                 for u in range(2):
-                    nc.tensor.transpose(turn_bank[s][:, u, :], pairs[:, u : N // 2 : 2], identity[:])
+                    nc.tensor.transpose(turn_bank[s][:, u, :], pairs[:, u * P : (u + 1) * P], identity[:])
 
         def lay_out(s):
             if s == 0:
@@ -329,7 +346,7 @@ def tile_moe_nxt_lin_bias_kernel(tc, xT, w_words, w_scales, b, wp, gate, offs, o
 
         def copy_result(s):
             z_copy[s] = keep.tile([P, FT, P], F32, name=f"z_copy_{s}", align_bytes=ALIGN)
-            if s in EARLY_TILES:
+            if s == 0:
                 nc.scalar.activation(out=z_copy[s][:], in_=z_bank[s][:], func=COPY)
             else:
                 nc.vector.tensor_copy(z_copy[s][:], z_bank[s][:])
@@ -344,10 +361,13 @@ def tile_moe_nxt_lin_bias_kernel(tc, xT, w_words, w_scales, b, wp, gate, offs, o
         round_tokens(0)
         for a in range(LAST):
             quantise_tokens(a)
-            round_tokens(a + 1)
             if a == 0:
-                spread_bias()
+                turn_gate()
+                for e in range(E):
+                    spread_bias(e)
+                gate_bias(SCALAR_TILE)
                 open_tile(SCALAR_TILE)
+            round_tokens(a + 1)
             if a > SHARED:
                 gather_scales(a)
             if a == SHARED:
@@ -377,6 +397,8 @@ def tile_moe_nxt_lin_bias_kernel(tc, xT, w_words, w_scales, b, wp, gate, offs, o
         for u in range(2):
             load_codes(PASSES + 1 + 2 * u, 2, AT_HELD_RAW + 2 * 2 * N * u)
 
+        for s in (0, 2, 3):
+            gate_bias(s)
         quantise_tokens(LAST)
         for a in range(LAST):
             for s in EARLY_TILES:
@@ -391,23 +413,19 @@ def tile_moe_nxt_lin_bias_kernel(tc, xT, w_words, w_scales, b, wp, gate, offs, o
         nc.vector.quantize_mx(
             out=wp_words[:].bitcast(FP8X4), scales=wp_scales[:], in_=wp_rounded[:].rearrange("p f j -> p (f j)")
         )
-        multiply(2, (1,))
+        multiply(2, (1, 2))
         turn(0)
         lay_out(0)
         gather_last(2, AT_GATED_BIAS_0)
-        multiply(3, (1,))
-        multiply(2, (2,))
+        multiply(2, (3, LAST))
         turn(1)
         lay_out(1)
-        multiply(3, (2,))
         project(0)
         gather_last(3, AT_TURNED_0)
-        for s in (2, 3):
-            multiply(s, (3,))
+        finish(2)
+        multiply(3, (1, 2, 3, LAST))
         project(1)
-        for s in (2, 3):
-            multiply(s, (LAST,))
-            finish(s)
+        finish(3)
         for s in (2, 3):
             turn(s)
             lay_out(s)

@@ -21,14 +21,14 @@ BYTE_COLUMNS = 704
 CASTS = (
     (("vector", 0, 256), ("scalar", 256, 256), ("vector", 512, 128)),
     (("scalar", 256, 256), ("vector", 0, 256), ("vector", 512, 128)),
-    (("scalar", 256, 256), ("vector", 0, 256), ("vector", 512, 128)),
+    (("scalar", 256, 256), ("vector", 0, 256), ("scalar", 512, 128)),
     (("scalar", 0, 256), ("scalar", 256, 256), ("gpsimd", 512, 128)),
     (("scalar", 0, 256), ("scalar", 256, 256), ("gpsimd", 512, 128)),
 )
 QUANTISED = (
     ((0, 256), (512, 128), (256, 256)),
     ((0, 256), (512, 128), (256, 256)),
-    ((0, 256), (512, 128), (256, 256)),
+    ((0, 256), (256, 256), (512, 128)),
     ((0, 256), (512, 128), (256, 256)),
     ((0, 512), (512, 128)),
 )

@@ -417,13 +417,14 @@ def tile_moe_nxt_lin_bias_kernel(tc, xT, w_words, w_scales, b, wp, gate, offs, o
         turn(0)
         lay_out(0)
         gather_last(2, AT_GATED_BIAS_0)
-        multiply(2, (3, LAST))
+        multiply(3, (1, 2))
         turn(1)
         lay_out(1)
         project(0)
         gather_last(3, AT_TURNED_0)
+        multiply(2, (3, LAST))
         finish(2)
-        multiply(3, (1, 2, 3, LAST))
+        multiply(3, (3, LAST))
         project(1)
         finish(3)
         for s in (2, 3):

@@ -71,8 +71,8 @@ def tile_moe_nxt_lin_bias_kernel(tc, xT, w_words, w_scales, b, wp, gate, offs, o
     nc = tc.nc
 
     def round_and_interleave(engine, dst, src):
-        dst = dst.rearrange("p (c i) j -> p c j i", i=4)
-        src = src.rearrange("p j (c i) -> p c j i", i=4)
+        dst = dst.rearrange("p (c i) j -> p c j i", i=2)
+        src = src.rearrange("p j (c i) -> p c j i", i=2)
         if engine == "scalar":
             nc.scalar.activation(out=dst, in_=src, func=COPY)
         elif engine == "gpsimd":

from contextlib import ExitStack

import concourse.mybir as mybir
from concourse.masks import make_identity

K, T, E, C, N, M = 2560, 640, 2, 256, 512, 256
P = 128
PACK = 4
PASSES = K // (P * PACK)
S = E * C
TILES = S // P
FT = M // P
LIST = 16
LAST = PASSES - 1

ALIGN = 256

WORD_COLUMNS = 688
BYTE_COLUMNS = 704

CASTS = (
    (("vector", 0, 256), ("scalar", 256, 256), ("vector", 512, 128)),
    (("scalar", 256, 256), ("vector", 0, 256), ("vector", 512, 128)),
    (("scalar", 256, 256), ("vector", 0, 256), ("scalar", 512, 128)),
    (("scalar", 0, 256), ("scalar", 256, 256), ("gpsimd", 512, 128)),
    (("scalar", 0, 256), ("scalar", 256, 256), ("gpsimd", 512, 128)),
)
QUANTISED = (
    ((0, 256), (512, 128), (256, 256)),
    ((0, 256), (512, 128), (256, 256)),
    ((0, 256), (256, 256), (512, 128)),
    ((0, 256), (512, 128), (256, 256)),
    ((0, 512), (512, 128)),
)
SPLIT = 512
SHARED = 2
SHARED_ROW = (0, 4, 8, 0, 0)
MOVED_ROWS = 100
WARM_UP = 2
SCALAR_TILE = 1
EARLY_TILES = (0, 1)

AT_SHARED_SCALES = 0
AT_W_BYTES_1 = 512
AT_SHARED_WORDS = 5888
AT_MIDDLE_CODES = 3072
AT_WP_RAW = 8448
HELD = 3
AT_HELD_RAW = 12544
AT_GATED_BIAS_0 = 22784
AT_LAST_RAW = AT_GATED_BIAS_0
AT_TURNED_0 = AT_LAST_RAW + 4 * PACK * T

FLOPS = 2 * K * N * S + 2 * N * M * T
BYTES = 4 * (K * T + N * E + N * M + S + M * T) + E * PASSES * (2 * P * N + 16 * N) + 2 * P * S // LIST

F32 = mybir.dt.float32
BF16 = mybir.dt.bfloat16
I32 = mybir.dt.int32
U32 = mybir.dt.uint32
U16 = mybir.dt.uint16
U8 = mybir.dt.uint8
FP8X4 = mybir.dt.float8_e4m3fn_x4
FP4X4 = mybir.dt.float4_e2m1fn_x4
COPY = mybir.ActivationFunctionType.Copy
MULT = mybir.AluOpType.mult
ADD = mybir.AluOpType.add


def tile_moe_nxt_lin_bias_kernel(tc, xT, w_words, w_scales, b, wp, gate, offs, out):
    nc = tc.nc

    def round_and_interleave(engine, dst, src):
        dst = dst.rearrange("p (c i) j -> p c j i", i=2)
        src = src.rearrange("p j (c i) -> p c j i", i=2)
        if engine == "scalar":
            nc.scalar.activation(out=dst, in_=src, func=COPY)
        elif engine == "gpsimd":
            nc.gpsimd.tensor_copy(dst, src)
        else:
            nc.vector.tensor_copy(dst, src)

    with ExitStack() as ctx:
        keep = ctx.enter_context(tc.tile_pool(name="keep", bufs=1))
        psum = ctx.enter_context(tc.psum_pool(name="psum", bufs=1))
        offsets = keep.tile([P, S // LIST], U16, name="offsets")
        reused = ctx.enter_context(tc.tile_pool(name="reused", bufs=1))

        out_tile = [keep.tile([P, T], F32, name=f"out_tile_{f}") for f in range(FT)]
        gate_rows = keep.tile([P, P], F32, name="gate_rows")
        nc.gpsimd.memset(gate_rows[:], 0.0)
        nc.gpsimd.memset(out_tile[0][:], 0.0)
        nc.scalar.activation(out=out_tile[1][:], in_=out_tile[0][:], func=COPY)

        bias_rows = keep.tile([P, PACK * E], F32, name="bias_rows")
        gate_column = keep.tile([P, TILES], F32, name="gate_column")
        w_bytes = {0: keep.tile([P, PASSES, N], U8, name="w_bytes_0", align_bytes=ALIGN)}
        w_codes = {}
        x_raw = {}
        nc.vector.memset(w_bytes[0][:].rearrange("p g n -> p (g n)").bitcast(I32), 0)

        def load_tokens(a):
            rows = xT[P * PACK * a : P * PACK * (a + 1), :].rearrange("(p j) t -> p j t", j=PACK)
            if a == HELD:
                x_raw[a] = reused.tile([P, PACK, T], F32, name=f"x_raw_{a}", offset=AT_HELD_RAW, align_bytes=ALIGN)
            elif a == LAST:
                x_raw[a] = reused.tile([P, PACK, T], F32, name=f"x_raw_{a}", offset=AT_LAST_RAW, align_bytes=ALIGN)
            else:
                x_raw[a] = keep.tile([P, PACK, T], F32, name=f"x_raw_{a}", align_bytes=ALIGN)
            nc.sync.dma_start(out=x_raw[a][:], in_=rows)

        def load_scales(e):
            byte_rows = w_scales[e].rearrange("a (q r) n -> r q a n", r=4)
            for r in range(4):
                nc.sync.dma_start(out=w_bytes[e][r:P:32, :, :].bitcast(I32), in_=byte_rows[r].bitcast(I32))

        def load_codes(first, count, offset=None):
            if offset is None:
                piece = keep.tile([P, count, 2 * N], U8, name=f"w_codes_{first}", align_bytes=ALIGN)
            else:
                piece = reused.tile([P, count, 2 * N], U8, name=f"w_codes_{first}", offset=offset, align_bytes=ALIGN)
            rows = w_words.rearrange("e a p c -> p (e a) c")[:, first : first + count, :]
            nc.sync.dma_start(out=piece[:].bitcast(I32), in_=rows.bitcast(I32))
            for u in range(count):
                w_codes[divmod(first + u, PASSES)] = piece[:, u, :]

        load_tokens(0)
        nc.sync.dma_start(offsets[:], offs)
        nc.sync.dma_start(out=bias_rows[:], in_=b.rearrange("(p j) e -> p (j e)", j=PACK))
        nc.sync.dma_start(out=gate_rows[0:TILES, :], in_=gate[0:1, :].rearrange("o (s u) -> (o s) u", u=P))
        for a in range(1, PASSES):
            load_tokens(a)
        load_scales(0)
        load_codes(0, SHARED + 1)

        identity = keep.tile([P, P], F32, name="identity")
        make_identity(nc, identity[:])

        words = {}
        for a in range(PASSES):
            if a == SHARED:
                words[a] = reused.tile([P, WORD_COLUMNS], I32, name=f"words_{a}", offset=AT_SHARED_WORDS, align_bytes=ALIGN)
            else:
                words[a] = keep.tile([P, WORD_COLUMNS], I32, name=f"words_{a}", align_bytes=ALIGN)
        for a in range(PASSES):
            nc.vector.memset(words[a][:, T:WORD_COLUMNS], 0)
        scales = {}
        for a in range(SHARED, PASSES):
            if a == SHARED:
                scales[a] = reused.tile([P, BYTE_COLUMNS], U8, name=f"scales_{a}", offset=AT_SHARED_SCALES, align_bytes=ALIGN)
            else:
                scales[a] = keep.tile([P, BYTE_COLUMNS], U8, name=f"scales_{a}", align_bytes=ALIGN)
            nc.gpsimd.memset(scales[a][:, T:BYTE_COLUMNS], 0)
        for a in range(SHARED):
            scales[a] = scales[SHARED]

        slot_words, slot_scales = {}, {}
        for a in range(LAST):
            slot_words[a] = keep.tile([P, S], U32, name=f"slot_words_{a}", align_bytes=ALIGN)
            slot_scales[a] = keep.tile([P, S], U8, name=f"slot_scales_{a}", align_bytes=ALIGN)
        for a in range(1, SHARED + 1):
            nc.gpsimd.memset(slot_scales[a][:].bitcast(I32), 0)

        x_rounded = {}

        def rounded(a, t0, n):
            if t0 < SPLIT:
                return x_rounded[(a, 0)][:, t0 : t0 + n, :]
            return x_rounded[(a, 1)][:, t0 - SPLIT : t0 - SPLIT + n, :]

        def round_tokens(a):
            x_rounded[(a, 0)] = keep.tile([P, SPLIT, PACK], BF16, name=f"x_rounded_{a}", align_bytes=ALIGN)
            tag = f"x_rest_{min(a, SHARED)}"
            x_rounded[(a, 1)] = keep.tile([P, T - SPLIT, PACK], BF16, name=f"x_rest_{a}", tag=tag, align_bytes=ALIGN)
            for engine, t0, n in CASTS[a]:
                round_and_interleave(engine, rounded(a, t0, n), x_raw[a][:, :, t0 : t0 + n])

        def quantise_tokens(a):
            row = SHARED_ROW[a]
            for t0, n in QUANTISED[a]:
                nc.vector.quantize_mx(
                    out=words[a][:, t0 : t0 + n].bitcast(FP8X4),
                    scales=scales[a][row:P, t0 : t0 + n],
                    in_=rounded(a, t0, n).rearrange("p t j -> p (t j)"),
                )

        def gather_words(a):
            nc.vector.tensor_copy(slot_words[a][:], words[a][:].bitcast(U32).indirect(offsets[:]))

        def gather_scales(a):
            nc.vector.tensor_copy(slot_scales[a][:], scales[a][:].indirect(offsets[:]))

        def places(s):
            return offsets[:, s * P // LIST : (s + 1) * P // LIST]

        last = {}

        def gather_last(s, offset=None):
            if offset is None:
                words_tile = keep.tile([P, P], U32, name=f"last_words_{s}", align_bytes=ALIGN)
                bytes_tile = keep.tile([P, P], U8, name=f"last_scales_{s}", align_bytes=ALIGN)
            else:
                words_tile = reused.tile([P, P], U32, name=f"last_words_{s}", offset=offset, align_bytes=ALIGN)
                bytes_tile = reused.tile([P, P], U8, name=f"last_scales_{s}", offset=offset + 4 * P, align_bytes=ALIGN)
            nc.vector.tensor_copy(words_tile[:], words[LAST][:].bitcast(U32).indirect(places(s)))
            nc.vector.tensor_copy(bytes_tile[:], scales[LAST][:].indirect(places(s)))
            last[s] = (words_tile[:], bytes_tile[:])

        y = {}

        def multiply(s, passes):
            e = s // 2
            slots = slice(s * P, (s + 1) * P)
            for a in passes:
                if a == 0:
                    y[s] = psum.tile([P, N], F32, name=f"y_{s}", tag=f"y_{s}")
                codes, code_scales = last[s] if a == LAST else (slot_words[a][:, slots], slot_scales[a][:, slots])
                nc.tensor.matmul_mx(
                    out=y[s][:],
                    lhsT=codes.bitcast(FP8X4),
                    lhsT_scale=code_scales,
                    rhs=w_codes[(e, a)].bitcast(FP4X4),
                    rhs_scale=w_bytes[e][:, a, :],
                    start=(a == 0),
                    stop=(a == LAST),
                )

        gated_bias = [reused.tile([P, N], F32, name="gated_bias_0", offset=AT_GATED_BIAS_0, align_bytes=ALIGN)]
        gated_bias.append(keep.tile([P, N], F32, name="gated_bias_1", align_bytes=ALIGN))
        for s in (2, 3):
            at = AT_LAST_RAW + 4 * N * (s - 1)
            gated_bias.append(reused.tile([P, N], F32, name=f"gated_bias_{s}", offset=at, align_bytes=ALIGN))
        turn_bank = {}

        def turn_gate():
            gate_turned = psum.tile([P, P], F32, name="gate_turned", tag="y_3")
            nc.tensor.transpose(gate_turned[:], gate_rows[:], identity[:])
            nc.scalar.activation(out=gate_column[:], in_=gate_turned[:, 0:TILES], func=COPY)

        spread = {}

        def spread_bias(e):
            spread[e] = psum.tile([P, PACK, P], F32, name=f"spread_{e}", tag=f"turn_{3 * e}")
            for j in range(PACK):
                column = bias_rows[:, E * j + e : E * j + e + 1]
                nc.tensor.transpose(spread[e][:, j, :], column.to_broadcast([P, P]), identity[:])

        def gate_bias(s):
            if s == SCALAR_TILE:
                dst = gated_bias[s][:].rearrange("s (j q) -> s j q", j=PACK)
                src = spread[s // 2][:]
            else:
                dst = gated_bias[s][:].rearrange("s (u q e) -> s u q e", u=2, e=2)
                src = spread[s // 2][:].rearrange("s (u e) q -> s u q e", u=2)
            nc.scalar.activation(out=dst, in_=src, func=COPY, scale=gate_column[:, s : s + 1])

        def turn_and_add(s, src, first):
            for j in range(PACK):
                nc.tensor.matmul(
                    turn_bank[s][:, j, :],
                    lhsT=src[:, j * P : (j + 1) * P],
                    rhs=identity[:],
                    is_transpose=True,
                    start=(first and j == 0),
                    stop=(not first and j == PACK - 1),
                )

        def open_tile(s):
            turn_bank[s] = psum.tile([P, PACK, P], F32, name=f"sum_{s}", tag=f"turn_{s}")
            turn_and_add(s, gated_bias[s], True)

        wp_rounded = keep.tile([P, M, PACK], BF16, name="wp_rounded", align_bytes=ALIGN)
        wp_words = keep.tile([P, M], U32, name="wp_words", align_bytes=ALIGN)
        wp_scales = keep.tile([P, M], U8, name="wp_scales", align_bytes=ALIGN)

        c, gated_y, c_turned, c_words, z_bank, z_copy = {}, {}, {}, {}, {}, {}
        c_scales = keep.tile([P, S], U8, name="c_scales", align_bytes=ALIGN)

        def finish(s):
            if s == SCALAR_TILE:
                gated_y[s] = keep.tile([P, N], F32, name=f"gated_y_{s}", align_bytes=ALIGN)
                nc.scalar.activation(
                    out=gated_y[s][:].rearrange("s (j q) -> s j q", j=PACK),
                    in_=y[s][:].rearrange("s (q j) -> s j q", j=PACK),
                    func=COPY,
                    scale=gate_column[:, s : s + 1],
                )
            else:
                c[s] = keep.tile([P, N], BF16, name=f"c_{s}", align_bytes=ALIGN)
                sums = y[s][:].rearrange("s (q u e) -> s u q e", u=2, e=2)
                for u in range(2):
                    half = slice(u * N // 2, (u + 1) * N // 2)
                    nc.vector.scalar_tensor_tensor(
                        out=c[s][:, half].rearrange("s (q e) -> s q e", e=2),
                        in0=sums[:, u, :, :],
                        scalar=gate_column[:, s : s + 1],
                        in1=gated_bias[s][:, half].rearrange("s (q e) -> s q e", e=2),
                        op0=MULT,
                        op1=ADD,
                    )

        def turn(s):
            if s == SCALAR_TILE:
                turn_and_add(s, gated_y[s], False)
            else:
                turn_bank[s] = psum.tile([P, 2, P], F32, name=f"turned_{s}", tag=f"turn_{s}")
                pairs = c[s][:].bitcast(F32)
                for u in range(2):
                    nc.tensor.transpose(turn_bank[s][:, u, :], pairs[:, u * P : (u + 1) * P], identity[:])

        def lay_out(s):
            if s == 0:
                c_turned[s] = reused.tile([P, P, PACK], BF16, name=f"c_turned_{s}", offset=AT_TURNED_0, align_bytes=ALIGN)
            else:
                c_turned[s] = keep.tile([P, P, PACK], BF16, name=f"c_turned_{s}", align_bytes=ALIGN)
            if s == SCALAR_TILE:
                nc.scalar.activation(out=c_turned[s][:], in_=turn_bank[s][:].rearrange("p j r -> p r j"), func=COPY)
            else:
                dst = c_turned[s][:].rearrange("p r j -> p (r j)").bitcast(F32).rearrange("p (r u) -> p r u", u=2)
                src = turn_bank[s][:].rearrange("p u r -> p r u")
                if s in EARLY_TILES:
                    nc.scalar.copy(out=dst, in_=src)
                else:
                    nc.vector.tensor_copy(dst, src)

        def project(s):
            slots = slice(s * P, (s + 1) * P)
            c_words[s] = keep.tile([P, P], U32, name=f"c_words_{s}", align_bytes=ALIGN)
            nc.vector.quantize_mx(
                out=c_words[s][:].bitcast(FP8X4),
                scales=c_scales[:, slots],
                in_=c_turned[s][:].rearrange("p r j -> p (r j)"),
            )
            z_bank[s] = psum.tile([P, FT, P], F32, name=f"z_{s}", tag=f"y_{s}")
            for f in range(FT):
                outputs = slice(f * P, (f + 1) * P)
                nc.tensor.matmul_mx(
                    out=z_bank[s][:, f, :],
                    lhsT=wp_words[:, outputs].bitcast(FP8X4),
                    lhsT_scale=wp_scales[:, outputs],
                    rhs=c_words[s][:].bitcast(FP8X4),
                    rhs_scale=c_scales[:, slots],
                    start=True,
                    stop=True,
                )

        def copy_result(s):
            z_copy[s] = keep.tile([P, FT, P], F32, name=f"z_copy_{s}", align_bytes=ALIGN)
            if s == 0:
                nc.scalar.activation(out=z_copy[s][:], in_=z_bank[s][:], func=COPY)
            else:
                nc.vector.tensor_copy(z_copy[s][:], z_bank[s][:])

        def scatter(s, f):
            window = out_tile[f][:].indirect(places(s))
            if s in EARLY_TILES or f == FT - 1:
                nc.scalar.activation(out=window, in_=z_copy[s][:, f, :], func=COPY)
            else:
                nc.vector.tensor_copy(window, z_copy[s][:, f, :])

        round_tokens(0)
        for a in range(LAST):
            quantise_tokens(a)
            if a == 0:
                turn_gate()
                for e in range(E):
                    spread_bias(e)
                gate_bias(SCALAR_TILE)
                open_tile(SCALAR_TILE)
            round_tokens(a + 1)
            if a > SHARED:
                gather_scales(a)
            if a == SHARED:
                gather_scales(0)
                for u in range(1, SHARED + 1):
                    nc.sync.dma_start(
                        out=slot_scales[u][0:MOVED_ROWS, :].bitcast(I32),
                        in_=slot_scales[0][SHARED_ROW[u] : SHARED_ROW[u] + MOVED_ROWS, :].bitcast(I32),
                    )
            gather_words(a)
        idle = psum.tile([P, N], F32, name="idle", tag="turn_2")
        for u in range(WARM_UP):
            nc.tensor.matmul_mx(
                out=idle[:],
                lhsT=slot_words[SHARED][:, 0:P].bitcast(FP8X4),
                lhsT_scale=slot_scales[0][:, 0:P],
                rhs=slot_words[SHARED][:].bitcast(FP8X4),
                rhs_scale=slot_scales[0][:],
                start=True,
                stop=True,
            )
        w_bytes[1] = reused.tile([P, PASSES, N], U8, name="w_bytes_1", offset=AT_W_BYTES_1, align_bytes=ALIGN)
        load_scales(1)
        load_codes(SHARED + 1, 3, AT_MIDDLE_CODES)
        wp_raw = reused.tile([P, PACK, M], F32, name="wp_raw", offset=AT_WP_RAW, align_bytes=ALIGN)
        nc.sync.dma_start(out=wp_raw[:], in_=wp.rearrange("(p j) f -> p j f", j=PACK))
        for u in range(2):
            load_codes(PASSES + 1 + 2 * u, 2, AT_HELD_RAW + 2 * 2 * N * u)

        for s in (0, 2, 3):
            gate_bias(s)
        quantise_tokens(LAST)
        for a in range(LAST):
            for s in EARLY_TILES:
                multiply(s, (a,))
        for s in (2, 3):
            multiply(s, (0,))
        round_and_interleave("scalar", wp_rounded[:], wp_raw[:])
        for s in EARLY_TILES:
            gather_last(s)
            multiply(s, (LAST,))
            finish(s)
        nc.vector.quantize_mx(
            out=wp_words[:].bitcast(FP8X4), scales=wp_scales[:], in_=wp_rounded[:].rearrange("p f j -> p (f j)")
        )
        multiply(2, (1, 2))
        turn(0)
        lay_out(0)
        gather_last(2, AT_GATED_BIAS_0)
        multiply(3, (1, 2))
        turn(1)
        lay_out(1)
        project(0)
        gather_last(3, AT_TURNED_0)
        multiply(2, (3, LAST))
        finish(2)
        multiply(3, (3, LAST))
        project(1)
        finish(3)
        for s in (2, 3):
            turn(s)
            lay_out(s)
            project(s)
        for s in range(TILES):
            copy_result(s)
            for f in range(FT):
                scatter(s, f)
        for f in range(FT):
            nc.sync.dma_start(out=out[f * P : (f + 1) * P, :], in_=out_tile[f][:])
